import numpy as np
import ml_dtypes


def mxq(x, axis, fmt="e4m3"):
    dtype, down = {"e4m3": (ml_dtypes.float8_e4m3fn, 7), "e5m2": (ml_dtypes.float8_e5m2, 14)}[fmt]
    v = np.moveaxis(np.asarray(x, np.float32).astype(ml_dtypes.bfloat16).astype(np.float64), axis, -1)
    blocks = v.reshape(v.shape[:-1] + (-1, 32))
    amax = np.abs(blocks).max(-1, keepdims=True)
    byte = np.maximum(np.where(amax > 0, np.frexp(amax)[1] - 1 + 127, 0) - down, 1)
    scale = np.exp2(byte - 127.0)
    codes = (blocks / scale).astype(np.float32).astype(dtype).astype(np.float64)
    return np.moveaxis((codes * scale).reshape(v.shape), -1, axis)


WIDE = False


def mx_kscale(k):
    if not WIDE:
        return np.ones(k)
    levels = np.array([10, -10, 5, -5, 0])
    if k % 512:
        return np.exp2(np.random.permutation(np.resize(levels, k // 32))).repeat(32)
    a = np.empty((k // 512, 16))
    for p in range(k // 512):
        a[p, :8] = np.random.permutation(np.resize(levels, 8))
        for g in range(8):
            far = levels[np.abs(levels - a[p, g]) >= 10]
            a[p, g + 8] = far[np.random.randint(len(far))]
    return np.exp2(a.ravel()).repeat(32)


def f64(x):
    return np.asarray(x).astype(np.float64)


def striped(idx):
    return np.tile(idx.reshape(-1, 16).T, (8, 1)).astype(np.uint16)


def unstriped(offs):
    return offs[:16].T.reshape(-1).astype(np.int64)


E2M1 = np.array([0.0, 0.5, 1.0, 1.5, 2.0, 3.0, 4.0, 6.0, -0.0, -0.5, -1.0, -1.5, -2.0, -3.0, -4.0, -6.0])


def pack_weight(w, fmt):
    k, n = w.shape
    w = f64(np.asarray(w, np.float32).astype(ml_dtypes.bfloat16)).reshape(k // 32, 32, n)
    amax = np.abs(w).max(1)
    if fmt == "e4m3":
        byte = np.frexp(amax)[1] - 1 + 127 - 7
    else:
        mant, ex = np.frexp(amax / 6.0)
        byte = np.where(mant > 0.5, ex, ex - 1) + 127
    byte = np.clip(np.where(amax > 0, byte, 1), 1, 254)
    scaled = (w * np.exp2(127.0 - byte)[:, None, :]).reshape(k, n).astype(np.float32)
    by_word = np.ascontiguousarray(scaled.reshape(k // 512, 128, 4, n).transpose(0, 1, 3, 2))
    if fmt == "e4m3":
        words = by_word.astype(ml_dtypes.float8_e4m3fn).view(np.uint8)
    else:
        c = by_word.astype(ml_dtypes.float4_e2m1fn).view(np.uint8) & 0xF
        words = (c[..., 0::2] | (c[..., 1::2] << 4)).reshape(k // 512, 128, 2 * n)
    return np.ascontiguousarray(words), np.ascontiguousarray(byte.astype(np.uint8).reshape(k // 512, 16, n))


def unpack_weight(words, scales, fmt):
    g, _, n = scales.shape
    words = np.ascontiguousarray(words).reshape(g, 128, n, -1)
    if fmt == "e4m3":
        vals = words.view(ml_dtypes.float8_e4m3fn).astype(np.float64)
    else:
        nib = np.empty((g, 128, n, 4), np.uint8)
        nib[..., 0::2] = words & 0xF
        nib[..., 1::2] = words >> 4
        vals = E2M1[nib]
    vals = vals * np.repeat(np.exp2(scales.astype(np.float64) - 127.0), 8, axis=1)[..., None]
    return vals.transpose(0, 1, 3, 2).reshape(g * 512, n)


def gelu(v):
    return 0.5 * v * (1.0 + np.tanh(np.sqrt(2.0 / np.pi) * (v + 0.044715 * v**3)))


K, H, N, T, S, T2, S2 = 1024, 512, 384, 4096, 1024, 2048, 1024

def setup_inputs():
    n = np.random.standard_normal
    s = mx_kscale(K)[:, None]
    u = mx_kscale(H)[:, None]
    w = mx_kscale(S2)[:, None]
    tab_words, tab_scales = pack_weight(n((K, T)) * s, "e4m3")
    tab2_words, tab2_scales = pack_weight(0.35 * n((H, T2)) / np.sqrt(H) / u, "e4m3")
    m4_words, m4_scales = pack_weight(n((S2, N)) / np.sqrt(S2) / w, "e2m1")
    return {
        "tab_words": tab_words, "tab_scales": tab_scales,
        "offs": striped(np.random.permutation(T)[:S]),
        "tab2_words": tab2_words, "tab2_scales": tab2_scales,
        "offs2": striped(np.random.permutation(T2)[:S2]),
        "wq": (n((K, H)) / np.sqrt(K) / s * u.T).astype(np.float32),
        "bq": (0.3 * n(H) * u[:, 0]).astype(np.float32),
        "phi": np.random.uniform(-0.8, 0.8, S2).astype(np.float32),
        "gcos": (np.random.uniform(0.5, 1.5, S2) * w[:, 0]).astype(np.float32),
        "gsin": (np.random.uniform(0.8, 2.0, S2) * w[:, 0]).astype(np.float32),
        "mcos": (n((S2, N)) / np.sqrt(S2) / w).astype(np.float32),
        "m4_words": m4_words, "m4_scales": m4_scales,
    }

def reference(tab_words, tab_scales, offs, tab2_words, tab2_scales, offs2, wq, bq, phi, gcos, gsin, mcos, m4_words, m4_scales):
    v = unpack_weight(tab_words, tab_scales, "e4m3")[:, unstriped(offs)]
    v2 = unpack_weight(tab2_words, tab2_scales, "e4m3")[:, unstriped(offs2)]
    h = (mxq(f64(wq), 0, "e4m3").T @ v) + f64(bq)[:, None]
    e = (v2.T @ mxq(h, 0, "e4m3")) + f64(phi)[:, None]
    x = np.cos(e) * f64(gcos)[:, None]
    y = np.sin(e) * f64(gsin)[:, None]
    m4 = unpack_weight(m4_words, m4_scales, "e2m1")
    return (mxq(f64(mcos), 0, "e4m3").T @ mxq(x, 0, "e4m3")
                 + m4.T @ mxq(y, 0, "e4m3"))

@@ -1,0 +1,318 @@
+import math
+from contextlib import ExitStack
+
+import concourse.mybir as mybir
+
+K, H, N, T, S, T2, S2 = 1024, 512, 384, 4096, 1024, 2048, 1024
+FLOPS = 2 * (K * H * S + H * S2 * S + 2 * S2 * N * S)
+
+F32 = mybir.dt.float32
+BF16 = mybir.dt.bfloat16
+I32 = mybir.dt.int32
+U32 = mybir.dt.uint32
+U16 = mybir.dt.uint16
+U8 = mybir.dt.uint8
+FP8X4 = mybir.dt.float8_e4m3fn_x4
+FP4X4 = mybir.dt.float4_e2m1fn_x4
+ACT = mybir.ActivationFunctionType
+ALU = mybir.AluOpType
+
+P = 128
+PACK = 4
+PASS = P * PACK
+HALF = 512
+CHUNK = 128
+LIST_COLS = HALF // 16
+TAB2_PLANE_ROW = 8
+
+
+def tile_list_fragment_phase_fields_kernel(
+    tc, tab_words, tab_scales, offs, tab2_words, tab2_scales, offs2, wq, bq, phi, gcos, gsin, mcos, m4_words, m4_scales, out
+):
+    nc = tc.nc
+    with ExitStack() as ctx:
+        keep = ctx.enter_context(tc.tile_pool(name="keep", bufs=1))
+        ring = ctx.enter_context(tc.tile_pool(name="ring", bufs=2))
+        psum = ctx.enter_context(tc.psum_pool(name="psum", bufs=1))
+
+        def held(name, shape, dtype):
+            return keep.tile(shape, dtype, name=name, align_bytes=64)
+
+        def turn(name, shape, dtype):
+            return ring.tile(shape, dtype, name=name, align_bytes=64)
+
+        def bank(index):
+            return psum.tile([P, HALF], F32, name="bank%d" % index)
+
+        idx = held("idx", [P, S // 16], U16)
+        idx2 = held("idx2", [P, S2 // 16], U16)
+        nc.sync.dma_start(idx[:], offs)
+        nc.sync.dma_start(idx2[:], offs2)
+
+        tab_plane = held("tab_plane", [P, T], U8)
+        tab2_plane = held("tab2_plane", [P, T2], U8)
+        m4_plane = held("m4_plane", [P, 2 * N], U8)
+        nc.vector.memset(tab_plane[:].bitcast(I32), 0)
+        nc.vector.memset(tab2_plane[:].bitcast(I32), 0)
+        nc.vector.memset(m4_plane[:].bitcast(I32), 0)
+        warm = held("warm", [P, 1], F32)
+        warm_out = held("warm_out", [P, 1], F32)
+        nc.vector.memset(warm[:], 0.0)
+        nc.scalar.activation(warm_out[:], warm[:], ACT.Sin)
+
+        for q in range(4):
+            nc.gpsimd.dma_start(
+                tab_plane[32 * q : 32 * q + 8, :].bitcast(I32), tab_scales[:, 4 * q : 4 * q + 4, :].bitcast(I32)
+            )
+        for q in range(4):
+            row = 32 * q + TAB2_PLANE_ROW
+            nc.gpsimd.dma_start(tab2_plane[row : row + 4, :].bitcast(I32), tab2_scales[0, 4 * q : 4 * q + 4, :].bitcast(I32))
+        bq_sb = held("bq_sb", [P, PACK], F32)
+
+        wq_raw = []
+        tab_sb = []
+        for a in range(2):
+            raw = held("wq_raw%d" % a, [P, PACK, H], F32)
+            nc.sync.dma_start(raw[:], wq[a * PASS : (a + 1) * PASS, :].rearrange("(p j) c -> p j c", j=PACK))
+            wq_raw.append(raw)
+            if a == 1:
+                nc.sync.dma_start(bq_sb[:], bq.rearrange("(p t) -> p t", t=PACK))
+            words = held("tab_sb%d" % a, [P, T], I32)
+            nc.sync.dma_start(words[:], tab_words[a].rearrange("p n t -> p (n t)").bitcast(I32))
+            tab_sb.append(words)
+        tab2_sb = held("tab2_sb", [P, T2], I32)
+        nc.sync.dma_start(tab2_sb[:], tab2_words[0].rearrange("p n t -> p (n t)").bitcast(I32))
+
+        def load_by_slot(name, vec):
+            sb = held(name, [P, 2 * PACK], F32)
+            nc.sync.dma_start(sb[:].rearrange("p (b t) -> p b t", b=2), vec.rearrange("(b p t) -> p b t", b=2, t=PACK))
+            return sb
+
+        phi_sb = load_by_slot("phi_sb", phi)
+        gsin_sb = load_by_slot("gsin_sb", gsin)
+        gcos_sb = load_by_slot("gcos_sb", gcos)
+        mcos_raw = []
+        for b in range(2):
+            raw = held("mcos_raw%d" % b, [P, PACK, N], F32)
+            nc.sync.dma_start(raw[:], mcos[b * PASS : (b + 1) * PASS, :].rearrange("(p j) c -> p j c", j=PACK))
+            mcos_raw.append(raw)
+        m4_sb = held("m4_sb", [P, 2 * 2 * N], U8)
+        nc.sync.dma_start(
+            m4_sb[:].bitcast(I32).rearrange("p (a c) -> p a c", a=2), m4_words.bitcast(I32).rearrange("a p c -> p a c")
+        )
+        for q in range(4):
+            nc.sync.dma_start(
+                m4_plane[32 * q : 32 * q + 4, :].bitcast(I32).rearrange("p (a c) -> p a c", a=2),
+                m4_scales[:, 4 * q : 4 * q + 4, :].bitcast(I32).rearrange("a r c -> r a c"),
+            )
+
+        def quantise(words, plane, src):
+            nc.vector.quantize_mx(out=words.bitcast(FP8X4), scales=plane, in_=src)
+
+        def side_by_side(dst):
+            return dst.rearrange("p (c i t) -> p c t i", i=4, t=PACK)
+
+        def by_slot(src):
+            return src.rearrange("p t (c i) -> p c t i", i=4)
+
+        def spread(vec, columns):
+            return vec.unsqueeze(1).unsqueeze(3).to_broadcast([P, columns // 4, PACK, 4])
+
+        v_plane = held("v_plane", [P, S], U8)
+        nc.vector.tensor_copy(v_plane[:], tab_plane[:].indirect(idx[:]))
+        v2_plane_listed = held("v2_plane_listed", [P, S2], U8)
+        nc.vector.tensor_copy(v2_plane_listed[:], tab2_plane[:].indirect(idx2[:]))
+        v2_plane = held("v2_plane", [P, S2], U8)
+        nc.vector.tensor_copy(
+            v2_plane[:].rearrange("p (b t c i) -> p b c t i", b=2, t=PACK, i=16),
+            v2_plane_listed[:].rearrange("p (b c i t) -> p b c t i", b=2, t=PACK, i=16),
+        )
+
+        wq_words = []
+        wq_plane = []
+        v_words = {}
+
+        def prepare_wq(a):
+            rounded = held("wq_rounded%d" % a, [P, PACK * H], BF16)
+            nc.scalar.copy(
+                rounded[:].rearrange("p (t m j) -> p m j t", t=PACK, j=PACK),
+                wq_raw[a][:].rearrange("p j (m t) -> p m j t", t=PACK),
+            )
+            words = held("wq_words%d" % a, [P, H], U32)
+            plane = held("wq_plane%d" % a, [P, H], U8)
+            quantise(words[:], plane[:], rounded[:])
+            wq_words.append(words)
+            wq_plane.append(plane)
+
+        def gather_v(a, half):
+            words = held("v_words%d_%d" % (a, half), [P, HALF], U32)
+            nc.vector.tensor_copy(words[:], tab_sb[a][:].bitcast(U32).indirect(idx[:, half * LIST_COLS : (half + 1) * LIST_COLS]))
+            v_words[a, half] = words
+
+        h_banks = {}
+
+        def h_pass(a, half):
+            for t in range(PACK):
+                if a == 0:
+                    h_banks[half, t] = bank(4 * half + t)
+                nc.tensor.matmul_mx(
+                    out=h_banks[half, t][:],
+                    lhsT=wq_words[a][:, t * P : (t + 1) * P].bitcast(FP8X4),
+                    lhsT_scale=wq_plane[a][:, t * P : (t + 1) * P],
+                    rhs=v_words[a, half][:].bitcast(FP8X4),
+                    rhs_scale=v_plane[4 * a : P, half * HALF : (half + 1) * HALF],
+                    start=(a == 0),
+                    stop=(a == 1),
+                )
+
+        h_slots = {}
+        h_words = {}
+        h_plane = {}
+
+        def h_out(half):
+            slots = held("h_slots%d" % half, [P, PACK, HALF], BF16)
+            for t in range(PACK):
+                nc.scalar.activation(slots[:, t, :], h_banks[half, t][:], ACT.Identity, bias=bq_sb[:, t : t + 1])
+            h_slots[half] = slots
+
+        def h_quantise(half):
+            woven = held("h_woven%d" % half, [P, PACK * HALF], BF16)
+            nc.vector.tensor_copy(side_by_side(woven[:]), by_slot(h_slots[half][:]))
+            h_words[half] = held("h_words%d" % half, [P, HALF], U32)
+            h_plane[half] = held("h_plane%d" % half, [P, HALF], U8)
+            quantise(h_words[half][:], h_plane[half][:], woven[:])
+
+        v2_words = {}
+
+        def gather_v2(b):
+            listed = held("v2_listed%d" % b, [P, PASS], U32)
+            nc.vector.tensor_copy(listed[:], tab2_sb[:].bitcast(U32).indirect(idx2[:, b * LIST_COLS : (b + 1) * LIST_COLS]))
+            v2_words[b] = held("v2_words%d" % b, [P, PASS], U32)
+            nc.vector.tensor_copy(
+                v2_words[b][:].rearrange("p (t c i) -> p c t i", t=PACK, i=4),
+                listed[:].rearrange("p (c i t) -> p c t i", t=PACK, i=4),
+            )
+
+        prepare_wq(0)
+        gather_v(0, 0)
+        gather_v(0, 1)
+        h_pass(0, 0)
+        h_pass(0, 1)
+        prepare_wq(1)
+        gather_v(1, 0)
+        h_pass(1, 0)
+        h_out(0)
+        gather_v(1, 1)
+        h_pass(1, 1)
+        h_out(1)
+        gather_v2(0)
+        h_quantise(0)
+        gather_v2(1)
+        h_quantise(1)
+
+        mcos_rounded = held("mcos_rounded", [P, 2 * PACK * N], BF16)
+        for b in range(2):
+            nc.vector.tensor_copy(side_by_side(mcos_rounded[:, b * PACK * N : (b + 1) * PACK * N]), by_slot(mcos_raw[b][:]))
+        mcos_words = held("mcos_words", [P, 2 * N], U32)
+        mcos_plane = held("mcos_plane", [P, 2 * N], U8)
+        quantise(mcos_words[:, 0:512], mcos_plane[:, 0:512], mcos_rounded[:, 0:2048])
+        quantise(mcos_words[:, 512:768], mcos_plane[:, 512:768], mcos_rounded[:, 2048:3072])
+
+        groups = [(half, b) for half in range(2) for b in range(2)]
+        sines = {}
+        cosines = {}
+        out_banks = {}
+
+        def phases(half, b, last):
+            sine = turn("sine", [P, PACK, HALF], F32)
+            size = turn("size", [P, PACK, HALF], F32)
+            e_banks = []
+            for t in range(PACK):
+                e_bank = bank(t)
+                cols = slice(t * P, (t + 1) * P)
+                nc.tensor.matmul_mx(
+                    out=e_bank[:],
+                    lhsT=v2_words[b][:, cols].bitcast(FP8X4),
+                    lhsT_scale=v2_plane[TAB2_PLANE_ROW:P, b * PASS + t * P : b * PASS + (t + 1) * P],
+                    rhs=h_words[half][:].bitcast(FP8X4),
+                    rhs_scale=h_plane[half][:],
+                    start=True,
+                    stop=True,
+                )
+                offset = phi_sb[:, PACK * b + t : PACK * b + t + 1]
+                nc.scalar.activation(sine[:, t, :], e_bank[:], ACT.Sin, bias=offset)
+                if last:
+                    e_banks.append(e_bank)
+                else:
+                    nc.scalar.activation(size[:, t, :], e_bank[:], ACT.Abs, bias=offset)
+            for t, e_bank in enumerate(e_banks):
+                nc.scalar.activation(size[:, t, :], e_bank[:], ACT.Abs, bias=phi_sb[:, PACK * b + t : PACK * b + t + 1])
+            sines[half, b] = sine
+            width = CHUNK if last else HALF
+            pieces = []
+            cosine = turn("cosine", [P, PACK * HALF], F32)
+            for c0 in range(0, HALF, width):
+                piece = cosine[:, PACK * c0 : PACK * (c0 + width)].rearrange("p (t j) -> p t j", t=PACK)
+                nc.scalar.activation(piece, size[:, :, c0 : c0 + width], ACT.Sin, bias=math.pi / 2, scale=-1.0)
+                pieces.append((c0, width, piece))
+            cosines[half, b] = pieces
+
+        def operand(name):
+            return turn(name + "_woven", [P, PACK * HALF], BF16), turn(name + "_words", [P, HALF], U32), turn(name + "_plane", [P, HALF], U8)
+
+        def gained(tiles, values, gain, c0, width):
+            woven, words, plane = tiles
+            part = woven[:, PACK * c0 : PACK * (c0 + width)]
+            nc.vector.tensor_tensor(side_by_side(part), by_slot(values), spread(gain, width), ALU.mult)
+            quantise(words[:, c0 : c0 + width], plane[:, c0 : c0 + width], part)
+
+        def mix(half, b, last):
+            slot_cols = slice(PACK * b, PACK * (b + 1))
+            y_tiles = operand("y")
+            y_words, y_plane = y_tiles[1:]
+            gained(y_tiles, sines[half, b][:], gsin_sb[:, slot_cols], 0, HALF)
+            for c in range(HALF // CHUNK):
+                if b == 0:
+                    out_banks[half, c] = bank(4 + c)
+                cols = slice(c * CHUNK, (c + 1) * CHUNK)
+                for n in range(N // P):
+                    nc.tensor.matmul_mx(
+                        out=out_banks[half, c][:, n * CHUNK : (n + 1) * CHUNK],
+                        lhsT=m4_sb[:, 2 * (b * N + n * P) : 2 * (b * N + (n + 1) * P)].bitcast(FP4X4),
+                        lhsT_scale=m4_plane[:, b * N + n * P : b * N + (n + 1) * P],
+                        rhs=y_words[:, cols].bitcast(FP8X4),
+                        rhs_scale=y_plane[:, cols],
+                        start=(b == 0 and n == 0),
+                        stop=False,
+                    )
+            x_tiles = operand("x")
+            x_words, x_plane = x_tiles[1:]
+            for c0, width, cosine in cosines[half, b]:
+                gained(x_tiles, cosine, gcos_sb[:, slot_cols], c0, width)
+                for c in range(c0 // CHUNK, (c0 + width) // CHUNK):
+                    cols = slice(c * CHUNK, (c + 1) * CHUNK)
+                    for n in range(N // P):
+                        nc.tensor.matmul_mx(
+                            out=out_banks[half, c][:, n * CHUNK : (n + 1) * CHUNK],
+                            lhsT=mcos_words[:, b * N + n * P : b * N + (n + 1) * P].bitcast(FP8X4),
+                            lhsT_scale=mcos_plane[:, b * N + n * P : b * N + (n + 1) * P],
+                            rhs=x_words[:, cols].bitcast(FP8X4),
+                            rhs_scale=x_plane[:, cols],
+                            start=False,
+                            stop=(b == 1 and n == N // P - 1),
+                        )
+                    if b == 1:
+                        result = held("result%d_%d" % (half, c), [P, N // P, CHUNK], F32)
+                        source = out_banks[half, c][:, 0:N].rearrange("p (n j) -> p n j", j=CHUNK)
+                        if last:
+                            nc.scalar.copy(result[:], source)
+                        else:
+                            nc.vector.tensor_copy(result[:], source)
+                        j0 = half * HALF + c * CHUNK
+                        nc.sync.dma_start(out.rearrange("(n p) j -> p n j", p=P)[:, :, j0 : j0 + CHUNK], result[:])
+
+        phases(*groups[0], False)
+        for g, (half, b) in enumerate(groups):
+            if g + 1 < len(groups):
+                phases(*groups[g + 1], g + 2 == len(groups))
+            mix(half, b, g + 1 == len(groups))

@@ -18,12 +18,15 @@ ACT = mybir.ActivationFunctionType
 ALU = mybir.AluOpType
 
 P = 128
-PACK = 4
-PASS = P * PACK
+SLOTS = 4
+PASS = P * SLOTS
+QUADS = 4
 HALF = 512
 CHUNK = 128
-LIST_COLS = HALF // 16
-TAB2_PLANE_ROW = 8
+LIST_COLS = 512 // 16
+V2_FIRST_ROW = 8
+OUT_BANK = 4
+VECTOR_RESULTS = 2
 
 
 def tile_list_fragment_phase_fields_kernel(
@@ -35,8 +38,8 @@ def tile_list_fragment_phase_fields_kernel(
         ring = ctx.enter_context(tc.tile_pool(name="ring", bufs=2))
         psum = ctx.enter_context(tc.psum_pool(name="psum", bufs=1))
 
-        def held(name, shape, dtype):
-            return keep.tile(shape, dtype, name=name, align_bytes=64)
+        def held(name, shape, dtype, reuses=None):
+            return keep.tile(shape, dtype, name=name, tag=reuses or name, align_bytes=64)
 
         def turn(name, shape, dtype):
             return ring.tile(shape, dtype, name=name, align_bytes=64)
@@ -44,99 +47,86 @@ def tile_list_fragment_phase_fields_kernel(
         def bank(index):
             return psum.tile([P, HALF], F32, name="bank%d" % index)
 
-        idx = held("idx", [P, S // 16], U16)
-        idx2 = held("idx2", [P, S2 // 16], U16)
-        nc.sync.dma_start(idx[:], offs)
-        nc.sync.dma_start(idx2[:], offs2)
+        def load_rows(name, matrix, a, reuses=None):
+            raw = held(name, [P, SLOTS, matrix.shape[1]], F32, reuses)
+            nc.sync.dma_start(raw[:], matrix[a * PASS : (a + 1) * PASS, :].rearrange("(p t) c -> p t c", t=SLOTS))
+            return raw
 
-        tab_plane = held("tab_plane", [P, T], U8)
-        tab2_plane = held("tab2_plane", [P, T2], U8)
-        m4_plane = held("m4_plane", [P, 2 * N], U8)
-        nc.vector.memset(tab_plane[:].bitcast(I32), 0)
-        nc.vector.memset(tab2_plane[:].bitcast(I32), 0)
-        nc.vector.memset(m4_plane[:].bitcast(I32), 0)
-        warm = held("warm", [P, 1], F32)
-        warm_out = held("warm_out", [P, 1], F32)
-        nc.vector.memset(warm[:], 0.0)
-        nc.scalar.activation(warm_out[:], warm[:], ACT.Sin)
-
-        for q in range(4):
-            nc.gpsimd.dma_start(
-                tab_plane[32 * q : 32 * q + 8, :].bitcast(I32), tab_scales[:, 4 * q : 4 * q + 4, :].bitcast(I32)
-            )
-        for q in range(4):
-            row = 32 * q + TAB2_PLANE_ROW
-            nc.gpsimd.dma_start(tab2_plane[row : row + 4, :].bitcast(I32), tab2_scales[0, 4 * q : 4 * q + 4, :].bitcast(I32))
-        bq_sb = held("bq_sb", [P, PACK], F32)
-
-        wq_raw = []
-        tab_sb = []
-        for a in range(2):
-            raw = held("wq_raw%d" % a, [P, PACK, H], F32)
-            nc.sync.dma_start(raw[:], wq[a * PASS : (a + 1) * PASS, :].rearrange("(p j) c -> p j c", j=PACK))
-            wq_raw.append(raw)
-            if a == 1:
-                nc.sync.dma_start(bq_sb[:], bq.rearrange("(p t) -> p t", t=PACK))
-            words = held("tab_sb%d" % a, [P, T], I32)
-            nc.sync.dma_start(words[:], tab_words[a].rearrange("p n t -> p (n t)").bitcast(I32))
-            tab_sb.append(words)
-        tab2_sb = held("tab2_sb", [P, T2], I32)
-        nc.sync.dma_start(tab2_sb[:], tab2_words[0].rearrange("p n t -> p (n t)").bitcast(I32))
-
-        def load_by_slot(name, vec):
-            sb = held(name, [P, 2 * PACK], F32)
-            nc.sync.dma_start(sb[:].rearrange("p (b t) -> p b t", b=2), vec.rearrange("(b p t) -> p b t", b=2, t=PACK))
+        def load_words(name, words, reuses=None):
+            sb = held(name, [P, words.shape[1]], I32, reuses)
+            nc.sync.dma_start(sb[:], words.rearrange("p n t -> p (n t)").bitcast(I32))
             return sb
 
-        phi_sb = load_by_slot("phi_sb", phi)
-        gsin_sb = load_by_slot("gsin_sb", gsin)
-        gcos_sb = load_by_slot("gcos_sb", gcos)
-        mcos_raw = []
-        for b in range(2):
-            raw = held("mcos_raw%d" % b, [P, PACK, N], F32)
-            nc.sync.dma_start(raw[:], mcos[b * PASS : (b + 1) * PASS, :].rearrange("(p j) c -> p j c", j=PACK))
-            mcos_raw.append(raw)
-        m4_sb = held("m4_sb", [P, 2 * 2 * N], U8)
-        nc.sync.dma_start(
-            m4_sb[:].bitcast(I32).rearrange("p (a c) -> p a c", a=2), m4_words.bitcast(I32).rearrange("a p c -> p a c")
-        )
-        for q in range(4):
-            nc.sync.dma_start(
-                m4_plane[32 * q : 32 * q + 4, :].bitcast(I32).rearrange("p (a c) -> p a c", a=2),
-                m4_scales[:, 4 * q : 4 * q + 4, :].bitcast(I32).rearrange("a r c -> r a c"),
-            )
+        def load_by_slot(name, vec, reuses):
+            sb = held(name, [P, 2, 2 * SLOTS], F32, reuses)
+            nc.sync.dma_start(sb[:, :, 0:SLOTS], vec.rearrange("(b p t) -> p b t", b=2, t=SLOTS))
+            return sb
 
         def quantise(words, plane, src):
             nc.vector.quantize_mx(out=words.bitcast(FP8X4), scales=plane, in_=src)
 
-        def side_by_side(dst):
-            return dst.rearrange("p (c i t) -> p c t i", i=4, t=PACK)
+        def side_by_side(dst, run):
+            return dst.rearrange("p (c i t) -> p c t i", i=run, t=SLOTS)
 
-        def by_slot(src):
-            return src.rearrange("p t (c i) -> p c t i", i=4)
+        def by_slot(src, run):
+            return src.rearrange("p t (c i) -> p c t i", i=run)
 
-        def spread(vec, columns):
-            return vec.unsqueeze(1).unsqueeze(3).to_broadcast([P, columns // 4, PACK, 4])
-
+        idx = held("idx", [P, S // 16], U16)
+        idx2 = held("idx2", [P, S2 // 16], U16)
+        tab_rows = held("tab_rows", [P, T], U8)
+        tab2_plane = held("tab2_plane", [P, T2], U8)
         v_plane = held("v_plane", [P, S], U8)
-        nc.vector.tensor_copy(v_plane[:], tab_plane[:].indirect(idx[:]))
+        nc.vector.memset(tab_rows[:].bitcast(I32), 0)
+        nc.vector.memset(tab2_plane[:].bitcast(I32), 0)
+        nc.vector.memset(v_plane[:].bitcast(I32), 0)
+
+        nc.sync.dma_start(idx[:], offs)
+        wq_raw = [load_rows("wq_raw0", wq, 0)]
+        nc.sync.dma_start(tab_rows[0:P:4, :].bitcast(I32), tab_scales.rearrange("a q t -> (a q) t").bitcast(I32))
+        nc.sync.dma_start(idx2[:], offs2)
+        for r in range(4):
+            nc.sync.dma_start(tab2_plane[V2_FIRST_ROW + r : P : 32, :].bitcast(I32), tab2_scales[0, r:16:4, :].bitcast(I32))
+        tab_sb = [load_words("tab_sb0", tab_words[0])]
+        bq_sb = held("bq_sb", [P, SLOTS], F32)
+        nc.sync.dma_start(bq_sb[:], bq.rearrange("(p t) -> p t", t=SLOTS))
+
+        v_rows = held("v_rows", [P, S], U8)
+        nc.vector.tensor_copy(v_rows[:], tab_rows[:].indirect(idx[:]))
+
+        def place_v_rows(a):
+            for r in range(4):
+                nc.sync.dma_start(
+                    v_plane[4 * a + r : P : 32, :].bitcast(I32), v_rows[64 * a + 4 * r : 64 * (a + 1) : 16, :].bitcast(I32)
+                )
+
+        place_v_rows(0)
+        wq_raw.append(load_rows("wq_raw1", wq, 1, reuses="tab_rows"))
+        place_v_rows(1)
         v2_plane_listed = held("v2_plane_listed", [P, S2], U8)
         nc.vector.tensor_copy(v2_plane_listed[:], tab2_plane[:].indirect(idx2[:]))
         v2_plane = held("v2_plane", [P, S2], U8)
         nc.vector.tensor_copy(
-            v2_plane[:].rearrange("p (b t c i) -> p b c t i", b=2, t=PACK, i=16),
-            v2_plane_listed[:].rearrange("p (b c i t) -> p b c t i", b=2, t=PACK, i=16),
+            v2_plane[:].rearrange("p (b t c i) -> p b c t i", b=2, t=SLOTS, i=16),
+            v2_plane_listed[:].rearrange("p (b c i t) -> p b c t i", b=2, t=SLOTS, i=16),
         )
+        tab_sb.append(load_words("tab_sb1", tab_words[1], reuses="tab2_plane"))
+        tab2_sb = load_words("tab2_sb", tab2_words[0], reuses="v2_plane_listed")
 
         wq_words = []
         wq_plane = []
-        v_words = {}
+        v_words = [held("v_words%d" % a, [P, S], U32) for a in range(2)]
+        h_banks = {}
+        h_slots = {}
+        h_woven = {}
+        h_words = {}
+        h_plane = {}
+        v2_words = {}
 
         def prepare_wq(a):
-            rounded = held("wq_rounded%d" % a, [P, PACK * H], BF16)
+            rounded = held("wq_rounded%d" % a, [P, SLOTS * H], BF16)
             nc.scalar.copy(
-                rounded[:].rearrange("p (t m j) -> p m j t", t=PACK, j=PACK),
-                wq_raw[a][:].rearrange("p j (m t) -> p m j t", t=PACK),
+                rounded[:].rearrange("p (t m j) -> p m t j", t=SLOTS, j=SLOTS),
+                wq_raw[a][:].rearrange("p j (m t) -> p m t j", t=SLOTS),
             )
             words = held("wq_words%d" % a, [P, H], U32)
             plane = held("wq_plane%d" % a, [P, H], U8)
@@ -145,52 +135,49 @@ def tile_list_fragment_phase_fields_kernel(
             wq_plane.append(plane)
 
         def gather_v(a, half):
-            words = held("v_words%d_%d" % (a, half), [P, HALF], U32)
-            nc.vector.tensor_copy(words[:], tab_sb[a][:].bitcast(U32).indirect(idx[:, half * LIST_COLS : (half + 1) * LIST_COLS]))
-            v_words[a, half] = words
-
-        h_banks = {}
+            nc.vector.tensor_copy(
+                v_words[a][:, half * HALF : (half + 1) * HALF],
+                tab_sb[a][:].bitcast(U32).indirect(idx[:, half * LIST_COLS : (half + 1) * LIST_COLS]),
+            )
 
         def h_pass(a, half):
-            for t in range(PACK):
+            for t in range(SLOTS):
                 if a == 0:
-                    h_banks[half, t] = bank(4 * half + t)
+                    h_banks[half, t] = bank(SLOTS * half + t)
                 nc.tensor.matmul_mx(
                     out=h_banks[half, t][:],
                     lhsT=wq_words[a][:, t * P : (t + 1) * P].bitcast(FP8X4),
                     lhsT_scale=wq_plane[a][:, t * P : (t + 1) * P],
-                    rhs=v_words[a, half][:].bitcast(FP8X4),
+                    rhs=v_words[a][:, half * HALF : (half + 1) * HALF].bitcast(FP8X4),
                     rhs_scale=v_plane[4 * a : P, half * HALF : (half + 1) * HALF],
                     start=(a == 0),
                     stop=(a == 1),
                 )
 
-        h_slots = {}
-        h_words = {}
-        h_plane = {}
+        def h_round(half):
+            h_slots[half] = held("h_slots%d" % half, [P, SLOTS, HALF], BF16)
+            for t in range(SLOTS):
+                nc.scalar.activation(h_slots[half][:, t, :], h_banks[half, t][:], ACT.Identity, bias=bq_sb[:, t : t + 1])
 
-        def h_out(half):
-            slots = held("h_slots%d" % half, [P, PACK, HALF], BF16)
-            for t in range(PACK):
-                nc.scalar.activation(slots[:, t, :], h_banks[half, t][:], ACT.Identity, bias=bq_sb[:, t : t + 1])
-            h_slots[half] = slots
+        def h_weave(half):
+            h_woven[half] = held("h_woven%d" % half, [P, SLOTS * HALF], BF16)
+            nc.vector.tensor_copy(side_by_side(h_woven[half][:], 4), by_slot(h_slots[half][:], 4))
 
         def h_quantise(half):
-            woven = held("h_woven%d" % half, [P, PACK * HALF], BF16)
-            nc.vector.tensor_copy(side_by_side(woven[:]), by_slot(h_slots[half][:]))
             h_words[half] = held("h_words%d" % half, [P, HALF], U32)
             h_plane[half] = held("h_plane%d" % half, [P, HALF], U8)
-            quantise(h_words[half][:], h_plane[half][:], woven[:])
+            quantise(h_words[half][:], h_plane[half][:], h_woven[half][:])
 
-        v2_words = {}
-
-        def gather_v2(b):
-            listed = held("v2_listed%d" % b, [P, PASS], U32)
+        def gather_v2(b, reuses=None):
+            listed = held("v2_listed%d" % b, [P, PASS], U32, reuses)
             nc.vector.tensor_copy(listed[:], tab2_sb[:].bitcast(U32).indirect(idx2[:, b * LIST_COLS : (b + 1) * LIST_COLS]))
+            return listed
+
+        def order_v2(b, listed):
             v2_words[b] = held("v2_words%d" % b, [P, PASS], U32)
             nc.vector.tensor_copy(
-                v2_words[b][:].rearrange("p (t c i) -> p c t i", t=PACK, i=4),
-                listed[:].rearrange("p (c i t) -> p c t i", t=PACK, i=4),
+                v2_words[b][:].rearrange("p (t c i) -> p c t i", t=SLOTS, i=4),
+                listed[:].rearrange("p (c i t) -> p c t i", t=SLOTS, i=4),
             )
 
         prepare_wq(0)
@@ -198,121 +185,154 @@ def tile_list_fragment_phase_fields_kernel(
         gather_v(0, 1)
         h_pass(0, 0)
         h_pass(0, 1)
-        prepare_wq(1)
-        gather_v(1, 0)
-        h_pass(1, 0)
-        h_out(0)
-        gather_v(1, 1)
-        h_pass(1, 1)
-        h_out(1)
-        gather_v2(0)
-        h_quantise(0)
-        gather_v2(1)
-        h_quantise(1)
 
-        mcos_rounded = held("mcos_rounded", [P, 2 * PACK * N], BF16)
-        for b in range(2):
-            nc.vector.tensor_copy(side_by_side(mcos_rounded[:, b * PACK * N : (b + 1) * PACK * N]), by_slot(mcos_raw[b][:]))
+        phi_sb = load_by_slot("phi_sb", phi, reuses="v_rows")
+        mcos_raw = [load_rows("mcos_raw0", mcos, 0, reuses="tab_sb0"), load_rows("mcos_raw1", mcos, 1, reuses="v_words0")]
+        gsin_sb = load_by_slot("gsin_sb", gsin, reuses="wq_plane0")
+        gcos_sb = load_by_slot("gcos_sb", gcos, reuses="wq_words0")
+        prepare_wq(1)
+        m4_sb = held("m4_sb", [P, 2 * 2 * N], U8, reuses="tab_rows")
+        nc.sync.dma_start(
+            m4_sb[:].bitcast(I32).rearrange("p (b c) -> p b c", b=2), m4_words.bitcast(I32).rearrange("b p c -> p b c")
+        )
+        m4_plane = held("m4_plane", [P, 2 * N], U8, reuses="wq_rounded1")
+        nc.gpsimd.memset(m4_plane[:].bitcast(I32), 0)
+        for q in range(QUADS):
+            nc.sync.dma_start(
+                m4_plane[32 * q : 32 * q + 4, :].bitcast(I32).rearrange("p (b c) -> p b c", b=2),
+                m4_scales[:, 4 * q : 4 * q + 4, :].bitcast(I32).rearrange("b r c -> r b c"),
+            )
+
+        for half in range(2):
+            gather_v(1, half)
+            h_pass(1, half)
+            h_round(half)
+        order_v2(0, gather_v2(0))
+        h_weave(0)
+        h_quantise(0)
+        v2_listed = gather_v2(1, reuses="h_slots0")
+        h_weave(1)
+        order_v2(1, v2_listed)
+
+        mcos_rounded = held("mcos_rounded", [P, 2 * SLOTS * N], BF16)
         mcos_words = held("mcos_words", [P, 2 * N], U32)
         mcos_plane = held("mcos_plane", [P, 2 * N], U8)
-        quantise(mcos_words[:, 0:512], mcos_plane[:, 0:512], mcos_rounded[:, 0:2048])
-        quantise(mcos_words[:, 512:768], mcos_plane[:, 512:768], mcos_rounded[:, 2048:3072])
+        for b in range(2):
+            nc.vector.tensor_copy(
+                side_by_side(mcos_rounded[:, b * SLOTS * N : (b + 1) * SLOTS * N], 2), by_slot(mcos_raw[b][:], 2)
+            )
+        h_quantise(1)
+        for c0, c1 in ((0, 512), (512, 2 * N)):
+            quantise(mcos_words[:, c0:c1], mcos_plane[:, c0:c1], mcos_rounded[:, SLOTS * c0 : SLOTS * c1])
 
         groups = [(half, b) for half in range(2) for b in range(2)]
         sines = {}
         cosines = {}
         out_banks = {}
 
-        def phases(half, b, last):
-            sine = turn("sine", [P, PACK, HALF], F32)
-            size = turn("size", [P, PACK, HALF], F32)
+        def phases(half, b):
+            last = (half, b) == groups[-1]
+            sine = turn("sine", [P, SLOTS, HALF], F32)
+            size = turn("size", [P, SLOTS, HALF], F32)
             e_banks = []
-            for t in range(PACK):
-                e_bank = bank(t)
-                cols = slice(t * P, (t + 1) * P)
+            for t in range(SLOTS):
+                e_banks.append(bank(t))
                 nc.tensor.matmul_mx(
-                    out=e_bank[:],
-                    lhsT=v2_words[b][:, cols].bitcast(FP8X4),
-                    lhsT_scale=v2_plane[TAB2_PLANE_ROW:P, b * PASS + t * P : b * PASS + (t + 1) * P],
+                    out=e_banks[t][:],
+                    lhsT=v2_words[b][:, t * P : (t + 1) * P].bitcast(FP8X4),
+                    lhsT_scale=v2_plane[V2_FIRST_ROW:P, b * PASS + t * P : b * PASS + (t + 1) * P],
                     rhs=h_words[half][:].bitcast(FP8X4),
                     rhs_scale=h_plane[half][:],
                     start=True,
                     stop=True,
                 )
-                offset = phi_sb[:, PACK * b + t : PACK * b + t + 1]
-                nc.scalar.activation(sine[:, t, :], e_bank[:], ACT.Sin, bias=offset)
-                if last:
-                    e_banks.append(e_bank)
-                else:
-                    nc.scalar.activation(size[:, t, :], e_bank[:], ACT.Abs, bias=offset)
-            for t, e_bank in enumerate(e_banks):
-                nc.scalar.activation(size[:, t, :], e_bank[:], ACT.Abs, bias=phi_sb[:, PACK * b + t : PACK * b + t + 1])
+                nc.scalar.activation(sine[:, t, :], e_banks[t][:], ACT.Sin, bias=phi_sb[:, b, t : t + 1])
+                if not last:
+                    nc.scalar.activation(size[:, t, :], e_banks[t][:], ACT.Abs, bias=phi_sb[:, b, t : t + 1])
+            if last:
+                for t in range(SLOTS):
+                    nc.scalar.activation(size[:, t, :], e_banks[t][:], ACT.Abs, bias=phi_sb[:, b, t : t + 1])
             sines[half, b] = sine
             width = CHUNK if last else HALF
-            pieces = []
-            cosine = turn("cosine", [P, PACK * HALF], F32)
+            cosine = turn("cosine", [P, SLOTS * HALF], F32)
+            cosines[half, b] = []
             for c0 in range(0, HALF, width):
-                piece = cosine[:, PACK * c0 : PACK * (c0 + width)].rearrange("p (t j) -> p t j", t=PACK)
+                piece = cosine[:, SLOTS * c0 : SLOTS * (c0 + width)].rearrange("p (t j) -> p t j", t=SLOTS)
                 nc.scalar.activation(piece, size[:, :, c0 : c0 + width], ACT.Sin, bias=math.pi / 2, scale=-1.0)
-                pieces.append((c0, width, piece))
-            cosines[half, b] = pieces
+                cosines[half, b].append((c0, width, piece))
 
         def operand(name):
-            return turn(name + "_woven", [P, PACK * HALF], BF16), turn(name + "_words", [P, HALF], U32), turn(name + "_plane", [P, HALF], U8)
+            return (
+                turn(name + "_woven", [P, SLOTS * HALF], BF16),
+                turn(name + "_words", [P, HALF], U32),
+                turn(name + "_plane", [P, HALF], U8),
+            )
 
-        def gained(tiles, values, gain, c0, width):
+        def gain(tiles, values, gains, c0, width):
+            part = tiles[0][:, SLOTS * c0 : SLOTS * (c0 + width)]
+            spread = gains.unsqueeze(1).unsqueeze(3).to_broadcast([P, width // 2, SLOTS, 2])
+            nc.vector.tensor_tensor(side_by_side(part, 2), by_slot(values, 2), spread, ALU.mult)
+
+        def quantise_part(tiles, c0, width):
             woven, words, plane = tiles
-            part = woven[:, PACK * c0 : PACK * (c0 + width)]
-            nc.vector.tensor_tensor(side_by_side(part), by_slot(values), spread(gain, width), ALU.mult)
-            quantise(words[:, c0 : c0 + width], plane[:, c0 : c0 + width], part)
+            quantise(words[:, c0 : c0 + width], plane[:, c0 : c0 + width], woven[:, SLOTS * c0 : SLOTS * (c0 + width)])
 
-        def mix(half, b, last):
-            slot_cols = slice(PACK * b, PACK * (b + 1))
-            y_tiles = operand("y")
-            y_words, y_plane = y_tiles[1:]
-            gained(y_tiles, sines[half, b][:], gsin_sb[:, slot_cols], 0, HALF)
+        def mix_sines(half, b, tiles):
+            quantise_part(tiles, 0, HALF)
             for c in range(HALF // CHUNK):
                 if b == 0:
-                    out_banks[half, c] = bank(4 + c)
+                    out_banks[half, c] = bank(OUT_BANK + c)
                 cols = slice(c * CHUNK, (c + 1) * CHUNK)
                 for n in range(N // P):
                     nc.tensor.matmul_mx(
                         out=out_banks[half, c][:, n * CHUNK : (n + 1) * CHUNK],
                         lhsT=m4_sb[:, 2 * (b * N + n * P) : 2 * (b * N + (n + 1) * P)].bitcast(FP4X4),
                         lhsT_scale=m4_plane[:, b * N + n * P : b * N + (n + 1) * P],
-                        rhs=y_words[:, cols].bitcast(FP8X4),
-                        rhs_scale=y_plane[:, cols],
+                        rhs=tiles[1][:, cols].bitcast(FP8X4),
+                        rhs_scale=tiles[2][:, cols],
                         start=(b == 0 and n == 0),
                         stop=False,
                     )
-            x_tiles = operand("x")
-            x_words, x_plane = x_tiles[1:]
-            for c0, width, cosine in cosines[half, b]:
-                gained(x_tiles, cosine, gcos_sb[:, slot_cols], c0, width)
-                for c in range(c0 // CHUNK, (c0 + width) // CHUNK):
-                    cols = slice(c * CHUNK, (c + 1) * CHUNK)
-                    for n in range(N // P):
-                        nc.tensor.matmul_mx(
-                            out=out_banks[half, c][:, n * CHUNK : (n + 1) * CHUNK],
-                            lhsT=mcos_words[:, b * N + n * P : b * N + (n + 1) * P].bitcast(FP8X4),
-                            lhsT_scale=mcos_plane[:, b * N + n * P : b * N + (n + 1) * P],
-                            rhs=x_words[:, cols].bitcast(FP8X4),
-                            rhs_scale=x_plane[:, cols],
-                            start=False,
-                            stop=(b == 1 and n == N // P - 1),
-                        )
-                    if b == 1:
-                        result = held("result%d_%d" % (half, c), [P, N // P, CHUNK], F32)
-                        source = out_banks[half, c][:, 0:N].rearrange("p (n j) -> p n j", j=CHUNK)
-                        if last:
-                            nc.scalar.copy(result[:], source)
-                        else:
-                            nc.vector.tensor_copy(result[:], source)
-                        j0 = half * HALF + c * CHUNK
-                        nc.sync.dma_start(out.rearrange("(n p) j -> p n j", p=P)[:, :, j0 : j0 + CHUNK], result[:])
 
-        phases(*groups[0], False)
+        def mix_cosines(half, b, tiles, c0, width):
+            quantise_part(tiles, c0, width)
+            for c in range(c0 // CHUNK, (c0 + width) // CHUNK):
+                cols = slice(c * CHUNK, (c + 1) * CHUNK)
+                for n in range(N // P):
+                    nc.tensor.matmul_mx(
+                        out=out_banks[half, c][:, n * CHUNK : (n + 1) * CHUNK],
+                        lhsT=mcos_words[:, b * N + n * P : b * N + (n + 1) * P].bitcast(FP8X4),
+                        lhsT_scale=mcos_plane[:, b * N + n * P : b * N + (n + 1) * P],
+                        rhs=tiles[1][:, cols].bitcast(FP8X4),
+                        rhs_scale=tiles[2][:, cols],
+                        start=False,
+                        stop=(b == 1 and n == N // P - 1),
+                    )
+                if b == 1:
+                    result = held("result%d_%d" % (half, c), [P, N // P, CHUNK], F32)
+                    source = out_banks[half, c][:, 0:N].rearrange("p (n j) -> p n j", j=CHUNK)
+                    if half == 0 and c < VECTOR_RESULTS:
+                        nc.vector.tensor_copy(result[:], source)
+                    else:
+                        nc.scalar.copy(result[:], source)
+                    j0 = half * HALF + c * CHUNK
+                    nc.sync.dma_start(out.rearrange("(n p) j -> p n j", p=P)[:, :, j0 : j0 + CHUNK], result[:])
+
+        phases(*groups[0])
+        waiting = []
         for g, (half, b) in enumerate(groups):
             if g + 1 < len(groups):
-                phases(*groups[g + 1], g + 2 == len(groups))
-            mix(half, b, g + 1 == len(groups))
+                phases(*groups[g + 1])
+            y_tiles = operand("y")
+            gain(y_tiles, sines[half, b][:], gsin_sb[:, b, 0:SLOTS], 0, HALF)
+            for args in waiting:
+                mix_cosines(*args)
+            waiting = []
+            mix_sines(half, b, y_tiles)
+            x_tiles = operand("x")
+            for c0, width, piece in cosines[half, b]:
+                gain(x_tiles, piece, gcos_sb[:, b, 0:SLOTS], c0, width)
+                if width == HALF:
+                    waiting.append((half, b, x_tiles, c0, width))
+                else:
+                    mix_cosines(half, b, x_tiles, c0, width)

@@ -2,6 +2,7 @@ import math
 from contextlib import ExitStack
 
 import concourse.mybir as mybir
+from concourse.masks import make_identity
 
 K, H, N, T, S, T2, S2 = 1024, 512, 384, 4096, 1024, 2048, 1024
 FLOPS = 2 * (K * H * S + H * S2 * S + 2 * S2 * N * S)
@@ -25,8 +26,12 @@ HALF = 512
 CHUNK = 128
 LIST_COLS = 512 // 16
 V2_FIRST_ROW = 8
-OUT_BANK = 4
-VECTOR_RESULTS = 2
+E_BANKS = (0, 1, 2)
+VECTOR_BANK = 3
+OUT_BANKS = (4, 5, 6, 7)
+GSIN_ROW, GCOS_ROW, VECTOR_ROWS = 0, 2, 4
+VECTOR_RESULTS = 4
+GPSIMD_COLS = {512: 128, 256: 56, 128: 0}
 
 
 def tile_list_fragment_phase_fields_kernel(
@@ -36,6 +41,7 @@ def tile_list_fragment_phase_fields_kernel(
     with ExitStack() as ctx:
         keep = ctx.enter_context(tc.tile_pool(name="keep", bufs=1))
         ring = ctx.enter_context(tc.tile_pool(name="ring", bufs=2))
+        codes = ctx.enter_context(tc.tile_pool(name="codes", bufs=3))
         psum = ctx.enter_context(tc.psum_pool(name="psum", bufs=1))
 
         def held(name, shape, dtype, reuses=None):
@@ -79,6 +85,8 @@ def tile_list_fragment_phase_fields_kernel(
         nc.vector.memset(tab_rows[:].bitcast(I32), 0)
         nc.vector.memset(tab2_plane[:].bitcast(I32), 0)
         nc.vector.memset(v_plane[:].bitcast(I32), 0)
+        identity = held("identity", [P, P], F32)
+        make_identity(nc, identity[:])
 
         nc.sync.dma_start(idx[:], offs)
         wq_raw = [load_rows("wq_raw0", wq, 0)]
@@ -109,17 +117,15 @@ def tile_list_fragment_phase_fields_kernel(
             v2_plane[:].rearrange("p (b t c i) -> p b c t i", b=2, t=SLOTS, i=16),
             v2_plane_listed[:].rearrange("p (b c i t) -> p b c t i", b=2, t=SLOTS, i=16),
         )
-        tab_sb.append(load_words("tab_sb1", tab_words[1], reuses="tab2_plane"))
-        tab2_sb = load_words("tab2_sb", tab2_words[0], reuses="v2_plane_listed")
+        tab2_sb = load_words("tab2_sb", tab2_words[0], reuses="tab2_plane")
+        tab_sb.append(load_words("tab_sb1", tab_words[1], reuses="v2_plane_listed"))
 
         wq_words = []
         wq_plane = []
         v_words = [held("v_words%d" % a, [P, S], U32) for a in range(2)]
         h_banks = {}
-        h_slots = {}
-        h_woven = {}
-        h_words = {}
-        h_plane = {}
+        h_words = held("h_words", [P, S], U32)
+        h_plane = held("h_plane", [P, S], U8)
         v2_words = {}
 
         def prepare_wq(a):
@@ -141,35 +147,34 @@ def tile_list_fragment_phase_fields_kernel(
             )
 
         def h_pass(a, half):
-            for t in range(SLOTS):
+            for c in range(HALF // CHUNK):
                 if a == 0:
-                    h_banks[half, t] = bank(SLOTS * half + t)
-                nc.tensor.matmul_mx(
-                    out=h_banks[half, t][:],
-                    lhsT=wq_words[a][:, t * P : (t + 1) * P].bitcast(FP8X4),
-                    lhsT_scale=wq_plane[a][:, t * P : (t + 1) * P],
-                    rhs=v_words[a][:, half * HALF : (half + 1) * HALF].bitcast(FP8X4),
-                    rhs_scale=v_plane[4 * a : P, half * HALF : (half + 1) * HALF],
-                    start=(a == 0),
-                    stop=(a == 1),
-                )
+                    h_banks[half, c] = bank(SLOTS * half + c)
+                cols = slice(half * HALF + c * CHUNK, half * HALF + (c + 1) * CHUNK)
+                for t in range(SLOTS):
+                    nc.tensor.matmul_mx(
+                        out=h_banks[half, c][:, t * CHUNK : (t + 1) * CHUNK],
+                        lhsT=wq_words[a][:, t * P : (t + 1) * P].bitcast(FP8X4),
+                        lhsT_scale=wq_plane[a][:, t * P : (t + 1) * P],
+                        rhs=v_words[a][:, cols].bitcast(FP8X4),
+                        rhs_scale=v_plane[4 * a : P, cols],
+                        start=(a == 0 and t == 0),
+                        stop=(a == 1 and t == SLOTS - 1),
+                    )
 
-        def h_round(half):
-            h_slots[half] = held("h_slots%d" % half, [P, SLOTS, HALF], BF16)
-            for t in range(SLOTS):
-                nc.scalar.activation(h_slots[half][:, t, :], h_banks[half, t][:], ACT.Identity, bias=bq_sb[:, t : t + 1])
+        def spread(by_slot_values, width):
+            return by_slot_values.unsqueeze(1).unsqueeze(3).to_broadcast([P, width // 2, SLOTS, 2])
 
-        def h_weave(half):
-            h_woven[half] = held("h_woven%d" % half, [P, SLOTS * HALF], BF16)
-            nc.vector.tensor_copy(side_by_side(h_woven[half][:], 4), by_slot(h_slots[half][:], 4))
+        def h_finish(j0, width):
+            woven = held("h_woven%d" % j0, [P, SLOTS * width], BF16)
+            for c in range(width // CHUNK):
+                source = h_banks[divmod(j0 // CHUNK + c, HALF // CHUNK)][:].rearrange("p (t j) -> p t j", t=SLOTS)
+                part = woven[:, SLOTS * c * CHUNK : SLOTS * (c + 1) * CHUNK]
+                nc.vector.tensor_tensor(side_by_side(part, 2), by_slot(source, 2), spread(bq_sb[:], CHUNK), ALU.add)
+            quantise(h_words[:, j0 : j0 + width], h_plane[:, j0 : j0 + width], woven[:])
 
-        def h_quantise(half):
-            h_words[half] = held("h_words%d" % half, [P, HALF], U32)
-            h_plane[half] = held("h_plane%d" % half, [P, HALF], U8)
-            quantise(h_words[half][:], h_plane[half][:], h_woven[half][:])
-
-        def gather_v2(b, reuses=None):
-            listed = held("v2_listed%d" % b, [P, PASS], U32, reuses)
+        def gather_v2(b):
+            listed = held("v2_listed%d" % b, [P, PASS], U32)
             nc.vector.tensor_copy(listed[:], tab2_sb[:].bitcast(U32).indirect(idx2[:, b * LIST_COLS : (b + 1) * LIST_COLS]))
             return listed
 
@@ -188,8 +193,10 @@ def tile_list_fragment_phase_fields_kernel(
 
         phi_sb = load_by_slot("phi_sb", phi, reuses="v_rows")
         mcos_raw = [load_rows("mcos_raw0", mcos, 0, reuses="tab_sb0"), load_rows("mcos_raw1", mcos, 1, reuses="v_words0")]
-        gsin_sb = load_by_slot("gsin_sb", gsin, reuses="wq_plane0")
-        gcos_sb = load_by_slot("gcos_sb", gcos, reuses="wq_words0")
+        vector_rows = held("vector_rows", [P, PASS], F32, reuses="wq_words0")
+        nc.vector.memset(vector_rows[:], 0.0)
+        for vec, row in ((gsin, GSIN_ROW), (gcos, GCOS_ROW)):
+            nc.sync.dma_start(vector_rows[row : row + 2, :], vec.rearrange("(b m) -> b m", b=2))
         prepare_wq(1)
         m4_sb = held("m4_sb", [P, 2 * 2 * N], U8, reuses="tab_rows")
         nc.sync.dma_start(
@@ -203,16 +210,21 @@ def tile_list_fragment_phase_fields_kernel(
                 m4_scales[:, 4 * q : 4 * q + 4, :].bitcast(I32).rearrange("b r c -> r b c"),
             )
 
-        for half in range(2):
-            gather_v(1, half)
-            h_pass(1, half)
-            h_round(half)
-        order_v2(0, gather_v2(0))
-        h_weave(0)
-        h_quantise(0)
-        v2_listed = gather_v2(1, reuses="h_slots0")
-        h_weave(1)
-        order_v2(1, v2_listed)
+        for b in range(2):
+            order_v2(b, gather_v2(b))
+        gather_v(1, 0)
+        h_pass(1, 0)
+        h_finish(0, HALF // 2)
+        h_finish(HALF // 2, HALF // 2)
+        vector_bank = bank(VECTOR_BANK)
+        for t in range(SLOTS):
+            nc.tensor.transpose(vector_bank[:, t * P : (t + 1) * P], vector_rows[:, t:PASS:SLOTS], identity[:])
+        vectors_psum = vector_bank[:].rearrange("p (t r) -> p t r", t=SLOTS)
+        vectors = held("vectors", [P, SLOTS, VECTOR_ROWS], F32)
+        nc.vector.tensor_copy(vectors[:], vectors_psum[:, :, 0:VECTOR_ROWS])
+        gather_v(1, 1)
+        h_pass(1, 1)
+        h_finish(HALF, HALF)
 
         mcos_rounded = held("mcos_rounded", [P, 2 * SLOTS * N], BF16)
         mcos_words = held("mcos_words", [P, 2 * N], U32)
@@ -221,71 +233,83 @@ def tile_list_fragment_phase_fields_kernel(
             nc.vector.tensor_copy(
                 side_by_side(mcos_rounded[:, b * SLOTS * N : (b + 1) * SLOTS * N], 2), by_slot(mcos_raw[b][:], 2)
             )
-        h_quantise(1)
         for c0, c1 in ((0, 512), (512, 2 * N)):
             quantise(mcos_words[:, c0:c1], mcos_plane[:, c0:c1], mcos_rounded[:, SLOTS * c0 : SLOTS * c1])
 
-        groups = [(half, b) for half in range(2) for b in range(2)]
+        quarter = HALF // 2
+        units = [(0, quarter, 0), (quarter, quarter, 0), (0, HALF, 1), (HALF, HALF, 0), (HALF, quarter, 1), (HALF + quarter, quarter, 1)]
         sines = {}
         cosines = {}
         out_banks = {}
+        e_banks = []
 
-        def phases(half, b):
-            last = (half, b) == groups[-1]
-            sine = turn("sine", [P, SLOTS, HALF], F32)
-            size = turn("size", [P, SLOTS, HALF], F32)
-            e_banks = []
-            for t in range(SLOTS):
-                e_banks.append(bank(t))
-                nc.tensor.matmul_mx(
-                    out=e_banks[t][:],
-                    lhsT=v2_words[b][:, t * P : (t + 1) * P].bitcast(FP8X4),
-                    lhsT_scale=v2_plane[V2_FIRST_ROW:P, b * PASS + t * P : b * PASS + (t + 1) * P],
-                    rhs=h_words[half][:].bitcast(FP8X4),
-                    rhs_scale=h_plane[half][:],
-                    start=True,
-                    stop=True,
-                )
-                nc.scalar.activation(sine[:, t, :], e_banks[t][:], ACT.Sin, bias=phi_sb[:, b, t : t + 1])
-                if not last:
-                    nc.scalar.activation(size[:, t, :], e_banks[t][:], ACT.Abs, bias=phi_sb[:, b, t : t + 1])
+        def phases(unit):
+            j0, width, b = unit
+            last = unit == units[-1]
+            sine = turn("sine", [P, SLOTS, width], F32)
+            size = turn("size", [P, SLOTS, width], F32)
+            per_bank = HALF // width
+            sums = []
+            for t0 in range(0, SLOTS, per_bank):
+                e_banks.append(bank(E_BANKS[len(e_banks) % len(E_BANKS)]))
+                for t in range(t0, t0 + per_bank):
+                    sums.append(e_banks[-1][:, (t - t0) * width : (t - t0 + 1) * width])
+                    nc.tensor.matmul_mx(
+                        out=sums[t],
+                        lhsT=v2_words[b][:, t * P : (t + 1) * P].bitcast(FP8X4),
+                        lhsT_scale=v2_plane[V2_FIRST_ROW:P, b * PASS + t * P : b * PASS + (t + 1) * P],
+                        rhs=h_words[:, j0 : j0 + width].bitcast(FP8X4),
+                        rhs_scale=h_plane[:, j0 : j0 + width],
+                        start=True,
+                        stop=True,
+                    )
+                for t in range(t0, t0 + per_bank):
+                    nc.scalar.activation(sine[:, t, :], sums[t], ACT.Sin, bias=phi_sb[:, b, t : t + 1])
+                    if not last:
+                        nc.scalar.activation(size[:, t, :], sums[t], ACT.Abs, bias=phi_sb[:, b, t : t + 1])
             if last:
                 for t in range(SLOTS):
-                    nc.scalar.activation(size[:, t, :], e_banks[t][:], ACT.Abs, bias=phi_sb[:, b, t : t + 1])
-            sines[half, b] = sine
-            width = CHUNK if last else HALF
-            cosine = turn("cosine", [P, SLOTS * HALF], F32)
-            cosines[half, b] = []
-            for c0 in range(0, HALF, width):
-                piece = cosine[:, SLOTS * c0 : SLOTS * (c0 + width)].rearrange("p (t j) -> p t j", t=SLOTS)
-                nc.scalar.activation(piece, size[:, :, c0 : c0 + width], ACT.Sin, bias=math.pi / 2, scale=-1.0)
-                cosines[half, b].append((c0, width, piece))
+                    nc.scalar.activation(size[:, t, :], sums[t], ACT.Abs, bias=phi_sb[:, b, t : t + 1])
+            sines[unit] = sine
+            step = CHUNK if last else width
+            cosine = turn("cosine", [P, SLOTS * width], F32)
+            cosines[unit] = []
+            for c0 in range(0, width, step):
+                piece = cosine[:, SLOTS * c0 : SLOTS * (c0 + step)].rearrange("p (t j) -> p t j", t=SLOTS)
+                nc.scalar.activation(piece, size[:, :, c0 : c0 + step], ACT.Sin, bias=math.pi / 2, scale=-1.0)
+                cosines[unit].append((c0, step, piece))
 
-        def operand(name):
+        def operand(name, buffer, width):
             return (
-                turn(name + "_woven", [P, SLOTS * HALF], BF16),
-                turn(name + "_words", [P, HALF], U32),
-                turn(name + "_plane", [P, HALF], U8),
+                held(name + "_woven", [P, SLOTS * width], BF16, reuses="woven%d" % buffer),
+                codes.tile([P, width], U32, name=name + "_words", align_bytes=64),
+                codes.tile([P, width], U8, name=name + "_plane", align_bytes=64),
             )
 
-        def gain(tiles, values, gains, c0, width):
-            part = tiles[0][:, SLOTS * c0 : SLOTS * (c0 + width)]
-            spread = gains.unsqueeze(1).unsqueeze(3).to_broadcast([P, width // 2, SLOTS, 2])
-            nc.vector.tensor_tensor(side_by_side(part, 2), by_slot(values, 2), spread, ALU.mult)
+        def gain(tiles, values, row, c0, width):
+            split = width - GPSIMD_COLS[width]
+            for engine, gains, k0, k1 in ((nc.vector, vectors_psum, 0, split), (nc.gpsimd, vectors, split, width)):
+                if k1 > k0:
+                    part = tiles[0][:, SLOTS * (c0 + k0) : SLOTS * (c0 + k1)]
+                    engine.tensor_tensor(
+                        side_by_side(part, 2), by_slot(values[:, :, k0:k1], 2), spread(gains[:, :, row], k1 - k0), ALU.mult
+                    )
 
         def quantise_part(tiles, c0, width):
             woven, words, plane = tiles
             quantise(words[:, c0 : c0 + width], plane[:, c0 : c0 + width], woven[:, SLOTS * c0 : SLOTS * (c0 + width)])
 
-        def mix_sines(half, b, tiles):
-            quantise_part(tiles, 0, HALF)
-            for c in range(HALF // CHUNK):
+        def mix_sines(unit, tiles):
+            j0, width, b = unit
+            quantise_part(tiles, 0, width)
+            for c0 in range(0, width, CHUNK):
+                chunk = (j0 + c0) // CHUNK
                 if b == 0:
-                    out_banks[half, c] = bank(OUT_BANK + c)
-                cols = slice(c * CHUNK, (c + 1) * CHUNK)
+                    out_banks[chunk] = bank(OUT_BANKS[chunk % len(OUT_BANKS)])
+                cols = slice(c0, c0 + CHUNK)
                 for n in range(N // P):
                     nc.tensor.matmul_mx(
-                        out=out_banks[half, c][:, n * CHUNK : (n + 1) * CHUNK],
+                        out=out_banks[chunk][:, n * CHUNK : (n + 1) * CHUNK],
                         lhsT=m4_sb[:, 2 * (b * N + n * P) : 2 * (b * N + (n + 1) * P)].bitcast(FP4X4),
                         lhsT_scale=m4_plane[:, b * N + n * P : b * N + (n + 1) * P],
                         rhs=tiles[1][:, cols].bitcast(FP8X4),
@@ -294,13 +318,15 @@ def tile_list_fragment_phase_fields_kernel(
                         stop=False,
                     )
 
-        def mix_cosines(half, b, tiles, c0, width):
-            quantise_part(tiles, c0, width)
-            for c in range(c0 // CHUNK, (c0 + width) // CHUNK):
-                cols = slice(c * CHUNK, (c + 1) * CHUNK)
+        def mix_cosines(unit, tiles, k0, width):
+            j0, b = unit[0], unit[2]
+            quantise_part(tiles, k0, width)
+            for c0 in range(k0, k0 + width, CHUNK):
+                chunk = (j0 + c0) // CHUNK
+                cols = slice(c0, c0 + CHUNK)
                 for n in range(N // P):
                     nc.tensor.matmul_mx(
-                        out=out_banks[half, c][:, n * CHUNK : (n + 1) * CHUNK],
+                        out=out_banks[chunk][:, n * CHUNK : (n + 1) * CHUNK],
                         lhsT=mcos_words[:, b * N + n * P : b * N + (n + 1) * P].bitcast(FP8X4),
                         lhsT_scale=mcos_plane[:, b * N + n * P : b * N + (n + 1) * P],
                         rhs=tiles[1][:, cols].bitcast(FP8X4),
@@ -309,30 +335,32 @@ def tile_list_fragment_phase_fields_kernel(
                         stop=(b == 1 and n == N // P - 1),
                     )
                 if b == 1:
-                    result = held("result%d_%d" % (half, c), [P, N // P, CHUNK], F32)
-                    source = out_banks[half, c][:, 0:N].rearrange("p (n j) -> p n j", j=CHUNK)
-                    if half == 0 and c < VECTOR_RESULTS:
+                    result = held("result%d" % chunk, [P, N // P, CHUNK], F32)
+                    source = out_banks[chunk][:, 0:N].rearrange("p (n j) -> p n j", j=CHUNK)
+                    if chunk < VECTOR_RESULTS:
                         nc.vector.tensor_copy(result[:], source)
                     else:
                         nc.scalar.copy(result[:], source)
-                    j0 = half * HALF + c * CHUNK
-                    nc.sync.dma_start(out.rearrange("(n p) j -> p n j", p=P)[:, :, j0 : j0 + CHUNK], result[:])
+                    nc.sync.dma_start(
+                        out.rearrange("(n p) j -> p n j", p=P)[:, :, chunk * CHUNK : (chunk + 1) * CHUNK], result[:]
+                    )
 
-        phases(*groups[0])
+        phases(units[0])
         waiting = []
-        for g, (half, b) in enumerate(groups):
-            if g + 1 < len(groups):
-                phases(*groups[g + 1])
-            y_tiles = operand("y")
-            gain(y_tiles, sines[half, b][:], gsin_sb[:, b, 0:SLOTS], 0, HALF)
+        for g, unit in enumerate(units):
+            width, b = unit[1], unit[2]
+            if g + 1 < len(units):
+                phases(units[g + 1])
+            y_tiles = operand("y", g % 2, width)
+            gain(y_tiles, sines[unit][:], GSIN_ROW + b, 0, width)
             for args in waiting:
                 mix_cosines(*args)
             waiting = []
-            mix_sines(half, b, y_tiles)
-            x_tiles = operand("x")
-            for c0, width, piece in cosines[half, b]:
-                gain(x_tiles, piece, gcos_sb[:, b, 0:SLOTS], c0, width)
-                if width == HALF:
-                    waiting.append((half, b, x_tiles, c0, width))
+            mix_sines(unit, y_tiles)
+            x_tiles = operand("x", g % 2, width)
+            for c0, step, piece in cosines[unit]:
+                gain(x_tiles, piece, GCOS_ROW + b, c0, step)
+                if step == width:
+                    waiting.append((unit, x_tiles, c0, step))
                 else:
-                    mix_cosines(half, b, x_tiles, c0, width)
+                    mix_cosines(unit, x_tiles, c0, step)

@@ -81,10 +81,13 @@ def tile_list_fragment_phase_fields_kernel(
         idx2 = held("idx2", [P, S2 // 16], U16)
         tab_rows = held("tab_rows", [P, T], U8)
         tab2_plane = held("tab2_plane", [P, T2], U8)
-        v_plane = held("v_plane", [P, S], U8)
+        v_plane = [held("v_plane0", [P, S], U8)]
         nc.vector.memset(tab_rows[:].bitcast(I32), 0)
         nc.vector.memset(tab2_plane[:].bitcast(I32), 0)
-        nc.vector.memset(v_plane[:].bitcast(I32), 0)
+        nc.vector.memset(v_plane[0][:].bitcast(I32), 0)
+        warm = held("warm", [P, 2], F32)
+        nc.gpsimd.memset(warm[:, 0:1], 0.0)
+        nc.scalar.activation(warm[:, 1:2], warm[:, 0:1], ACT.Sin)
         identity = held("identity", [P, P], F32)
         make_identity(nc, identity[:])
 
@@ -95,8 +98,7 @@ def tile_list_fragment_phase_fields_kernel(
         for r in range(4):
             nc.sync.dma_start(tab2_plane[V2_FIRST_ROW + r : P : 32, :].bitcast(I32), tab2_scales[0, r:16:4, :].bitcast(I32))
         tab_sb = [load_words("tab_sb0", tab_words[0])]
-        bq_sb = held("bq_sb", [P, SLOTS], F32)
-        nc.sync.dma_start(bq_sb[:], bq.rearrange("(p t) -> p t", t=SLOTS))
+        wq_raw.append(load_rows("wq_raw1", wq, 1))
 
         v_rows = held("v_rows", [P, S], U8)
         nc.vector.tensor_copy(v_rows[:], tab_rows[:].indirect(idx[:]))
@@ -104,12 +106,11 @@ def tile_list_fragment_phase_fields_kernel(
         def place_v_rows(a):
             for r in range(4):
                 nc.sync.dma_start(
-                    v_plane[4 * a + r : P : 32, :].bitcast(I32), v_rows[64 * a + 4 * r : 64 * (a + 1) : 16, :].bitcast(I32)
+                    v_plane[a][r:P:32, :].bitcast(I32), v_rows[64 * a + 4 * r : 64 * (a + 1) : 16, :].bitcast(I32)
                 )
 
+        tab2_sb = load_words("tab2_sb", tab2_words[0])
         place_v_rows(0)
-        wq_raw.append(load_rows("wq_raw1", wq, 1, reuses="tab_rows"))
-        place_v_rows(1)
         v2_plane_listed = held("v2_plane_listed", [P, S2], U8)
         nc.vector.tensor_copy(v2_plane_listed[:], tab2_plane[:].indirect(idx2[:]))
         v2_plane = held("v2_plane", [P, S2], U8)
@@ -117,8 +118,12 @@ def tile_list_fragment_phase_fields_kernel(
             v2_plane[:].rearrange("p (b t c i) -> p b c t i", b=2, t=SLOTS, i=16),
             v2_plane_listed[:].rearrange("p (b c i t) -> p b c t i", b=2, t=SLOTS, i=16),
         )
-        tab2_sb = load_words("tab2_sb", tab2_words[0], reuses="tab2_plane")
-        tab_sb.append(load_words("tab_sb1", tab_words[1], reuses="v2_plane_listed"))
+        tab_sb.append(load_words("tab_sb1", tab_words[1], reuses="tab2_plane"))
+        v_plane.append(held("v_plane1", [P, S], U8, reuses="v2_plane_listed"))
+        nc.vector.memset(v_plane[1][:].bitcast(I32), 0)
+        place_v_rows(1)
+        bq_sb = held("bq_sb", [P, SLOTS], F32, reuses="wq_raw0")
+        nc.sync.dma_start(bq_sb[:], bq.rearrange("(p t) -> p t", t=SLOTS))
 
         wq_words = []
         wq_plane = []
@@ -157,7 +162,7 @@ def tile_list_fragment_phase_fields_kernel(
                         lhsT=wq_words[a][:, t * P : (t + 1) * P].bitcast(FP8X4),
                         lhsT_scale=wq_plane[a][:, t * P : (t + 1) * P],
                         rhs=v_words[a][:, cols].bitcast(FP8X4),
-                        rhs_scale=v_plane[4 * a : P, cols],
+                        rhs_scale=v_plane[a][:, cols],
                         start=(a == 0 and t == 0),
                         stop=(a == 1 and t == SLOTS - 1),
                     )
@@ -198,7 +203,7 @@ def tile_list_fragment_phase_fields_kernel(
         for vec, row in ((gsin, GSIN_ROW), (gcos, GCOS_ROW)):
             nc.sync.dma_start(vector_rows[row : row + 2, :], vec.rearrange("(b m) -> b m", b=2))
         prepare_wq(1)
-        m4_sb = held("m4_sb", [P, 2 * 2 * N], U8, reuses="tab_rows")
+        m4_sb = held("m4_sb", [P, 2 * 2 * N], U8, reuses="wq_raw1")
         nc.sync.dma_start(
             m4_sb[:].bitcast(I32).rearrange("p (b c) -> p b c", b=2), m4_words.bitcast(I32).rearrange("b p c -> p b c")
         )
@@ -229,8 +234,8 @@ def tile_list_fragment_phase_fields_kernel(
         mcos_rounded = held("mcos_rounded", [P, 2 * SLOTS * N], BF16)
         mcos_words = held("mcos_words", [P, 2 * N], U32)
         mcos_plane = held("mcos_plane", [P, 2 * N], U8)
-        for b in range(2):
-            nc.vector.tensor_copy(
+        for b, copy in enumerate((nc.scalar.copy, nc.vector.tensor_copy)):
+            copy(
                 side_by_side(mcos_rounded[:, b * SLOTS * N : (b + 1) * SLOTS * N], 2), by_slot(mcos_raw[b][:], 2)
             )
         for c0, c1 in ((0, 512), (512, 2 * N)):

@@ -31,7 +31,7 @@ VECTOR_BANK = 3
 OUT_BANKS = (4, 5, 6, 7)
 GSIN_ROW, GCOS_ROW, VECTOR_ROWS = 0, 2, 4
 VECTOR_RESULTS = 4
-GPSIMD_COLS = {512: 128, 256: 56, 128: 0}
+GPSIMD_COLS = {512: 160, 256: 72, 128: 0}
 
 
 def tile_list_fragment_phase_fields_kernel(
@@ -47,8 +47,8 @@ def tile_list_fragment_phase_fields_kernel(
         def held(name, shape, dtype, reuses=None):
             return keep.tile(shape, dtype, name=name, tag=reuses or name, align_bytes=64)
 
-        def turn(name, shape, dtype):
-            return ring.tile(shape, dtype, name=name, align_bytes=64)
+        def turn(name, shape, dtype, bufs=2):
+            return ring.tile(shape, dtype, name=name, align_bytes=64, bufs=bufs)
 
         def bank(index):
             return psum.tile([P, HALF], F32, name="bank%d" % index)
@@ -196,7 +196,7 @@ def tile_list_fragment_phase_fields_kernel(
         h_pass(0, 0)
         h_pass(0, 1)
 
-        phi_sb = load_by_slot("phi_sb", phi, reuses="v_rows")
+        phi_sb = load_by_slot("phi_sb", phi, reuses="wq_rounded0")
         mcos_raw = [load_rows("mcos_raw0", mcos, 0, reuses="tab_sb0"), load_rows("mcos_raw1", mcos, 1, reuses="v_words0")]
         vector_rows = held("vector_rows", [P, PASS], F32, reuses="wq_words0")
         nc.vector.memset(vector_rows[:], 0.0)
@@ -251,7 +251,7 @@ def tile_list_fragment_phase_fields_kernel(
         def phases(unit):
             j0, width, b = unit
             last = unit == units[-1]
-            sine = turn("sine", [P, SLOTS, width], F32)
+            sine = turn("sine", [P, SLOTS, width], F32, bufs=3)
             size = turn("size", [P, SLOTS, width], F32)
             per_bank = HALF // width
             sums = []
@@ -269,24 +269,24 @@ def tile_list_fragment_phase_fields_kernel(
                         stop=True,
                     )
                 for t in range(t0, t0 + per_bank):
-                    nc.scalar.activation(sine[:, t, :], sums[t], ACT.Sin, bias=phi_sb[:, b, t : t + 1])
                     if not last:
                         nc.scalar.activation(size[:, t, :], sums[t], ACT.Abs, bias=phi_sb[:, b, t : t + 1])
+                    nc.scalar.activation(sine[:, t, :], sums[t], ACT.Sin, bias=phi_sb[:, b, t : t + 1])
             if last:
                 for t in range(SLOTS):
                     nc.scalar.activation(size[:, t, :], sums[t], ACT.Abs, bias=phi_sb[:, b, t : t + 1])
             sines[unit] = sine
             step = CHUNK if last else width
-            cosine = turn("cosine", [P, SLOTS * width], F32)
+            cosine = turn("cosine", [P, SLOTS * width], F32, bufs=3)
             cosines[unit] = []
             for c0 in range(0, width, step):
                 piece = cosine[:, SLOTS * c0 : SLOTS * (c0 + step)].rearrange("p (t j) -> p t j", t=SLOTS)
                 nc.scalar.activation(piece, size[:, :, c0 : c0 + step], ACT.Sin, bias=math.pi / 2, scale=-1.0)
                 cosines[unit].append((c0, step, piece))
 
-        def operand(name, buffer, width):
+        def operand(name, woven, width):
             return (
-                held(name + "_woven", [P, SLOTS * width], BF16, reuses="woven%d" % buffer),
+                woven[:, 0 : SLOTS * width],
                 codes.tile([P, width], U32, name=name + "_words", align_bytes=64),
                 codes.tile([P, width], U8, name=name + "_plane", align_bytes=64),
             )
@@ -352,17 +352,19 @@ def tile_list_fragment_phase_fields_kernel(
 
         phases(units[0])
         waiting = []
+        woven = held("woven", [P, 2 * SLOTS * HALF], BF16)
         for g, unit in enumerate(units):
             width, b = unit[1], unit[2]
             if g + 1 < len(units):
                 phases(units[g + 1])
-            y_tiles = operand("y", g % 2, width)
+            y_tiles = operand("y", woven[:, SLOTS * HALF :], width)
             gain(y_tiles, sines[unit][:], GSIN_ROW + b, 0, width)
             for args in waiting:
                 mix_cosines(*args)
             waiting = []
             mix_sines(unit, y_tiles)
-            x_tiles = operand("x", g % 2, width)
+            woven = held("woven", [P, 2 * SLOTS * HALF], BF16)
+            x_tiles = operand("x", woven, width)
             for c0, step, piece in cosines[unit]:
                 gain(x_tiles, piece, GCOS_ROW + b, c0, step)
                 if step == width:

@@ -30,8 +30,8 @@ E_BANKS = (0, 1, 2)
 VECTOR_BANK = 3
 OUT_BANKS = (4, 5, 6, 7)
 GSIN_ROW, GCOS_ROW, VECTOR_ROWS = 0, 2, 4
-VECTOR_RESULTS = 4
-GPSIMD_COLS = {512: 160, 256: 72, 128: 0}
+VECTOR_RESULTS = 3
+GPSIMD_COLS = {512: 128, 256: 56, 128: 0}
 
 
 def tile_list_fragment_phase_fields_kernel(
@@ -122,8 +122,6 @@ def tile_list_fragment_phase_fields_kernel(
         v_plane.append(held("v_plane1", [P, S], U8, reuses="v2_plane_listed"))
         nc.vector.memset(v_plane[1][:].bitcast(I32), 0)
         place_v_rows(1)
-        bq_sb = held("bq_sb", [P, SLOTS], F32, reuses="wq_raw0")
-        nc.sync.dma_start(bq_sb[:], bq.rearrange("(p t) -> p t", t=SLOTS))
 
         wq_words = []
         wq_plane = []
@@ -167,15 +165,15 @@ def tile_list_fragment_phase_fields_kernel(
                         stop=(a == 1 and t == SLOTS - 1),
                     )
 
-        def spread(by_slot_values, width):
-            return by_slot_values.unsqueeze(1).unsqueeze(3).to_broadcast([P, width // 2, SLOTS, 2])
+        def spread(by_slot_values, width, run):
+            return by_slot_values.unsqueeze(1).unsqueeze(3).to_broadcast([P, width // run, SLOTS, run])
 
         def h_finish(j0, width):
             woven = held("h_woven%d" % j0, [P, SLOTS * width], BF16)
             for c in range(width // CHUNK):
                 source = h_banks[divmod(j0 // CHUNK + c, HALF // CHUNK)][:].rearrange("p (t j) -> p t j", t=SLOTS)
                 part = woven[:, SLOTS * c * CHUNK : SLOTS * (c + 1) * CHUNK]
-                nc.vector.tensor_tensor(side_by_side(part, 2), by_slot(source, 2), spread(bq_sb[:], CHUNK), ALU.add)
+                nc.vector.tensor_tensor(side_by_side(part, 2), by_slot(source, 2), spread(bq_sb[:], CHUNK, 2), ALU.add)
             quantise(h_words[:, j0 : j0 + width], h_plane[:, j0 : j0 + width], woven[:])
 
         def gather_v2(b):
@@ -196,7 +194,9 @@ def tile_list_fragment_phase_fields_kernel(
         h_pass(0, 0)
         h_pass(0, 1)
 
-        phi_sb = load_by_slot("phi_sb", phi, reuses="wq_rounded0")
+        bq_sb = held("bq_sb", [P, SLOTS], F32, reuses="wq_rounded0")
+        nc.sync.dma_start(bq_sb[:], bq.rearrange("(p t) -> p t", t=SLOTS))
+        phi_sb = load_by_slot("phi_sb", phi, reuses="v_rows")
         mcos_raw = [load_rows("mcos_raw0", mcos, 0, reuses="tab_sb0"), load_rows("mcos_raw1", mcos, 1, reuses="v_words0")]
         vector_rows = held("vector_rows", [P, PASS], F32, reuses="wq_words0")
         nc.vector.memset(vector_rows[:], 0.0)
@@ -231,7 +231,7 @@ def tile_list_fragment_phase_fields_kernel(
         h_pass(1, 1)
         h_finish(HALF, HALF)
 
-        mcos_rounded = held("mcos_rounded", [P, 2 * SLOTS * N], BF16)
+        mcos_rounded = held("mcos_rounded", [P, 2 * SLOTS * N], BF16, reuses="woven")
         mcos_words = held("mcos_words", [P, 2 * N], U32)
         mcos_plane = held("mcos_plane", [P, 2 * N], U8)
         for b, copy in enumerate((nc.scalar.copy, nc.vector.tensor_copy)):
@@ -293,11 +293,11 @@ def tile_list_fragment_phase_fields_kernel(
 
         def gain(tiles, values, row, c0, width):
             split = width - GPSIMD_COLS[width]
-            for engine, gains, k0, k1 in ((nc.vector, vectors_psum, 0, split), (nc.gpsimd, vectors, split, width)):
+            for engine, gains, k0, k1, run in ((nc.vector, vectors_psum, 0, split, 2), (nc.gpsimd, vectors, split, width, 1)):
                 if k1 > k0:
                     part = tiles[0][:, SLOTS * (c0 + k0) : SLOTS * (c0 + k1)]
                     engine.tensor_tensor(
-                        side_by_side(part, 2), by_slot(values[:, :, k0:k1], 2), spread(gains[:, :, row], k1 - k0), ALU.mult
+                        side_by_side(part, run), by_slot(values[:, :, k0:k1], run), spread(gains[:, :, row], k1 - k0, run), ALU.mult
                     )
 
         def quantise_part(tiles, c0, width):
@@ -363,7 +363,7 @@ def tile_list_fragment_phase_fields_kernel(
                 mix_cosines(*args)
             waiting = []
             mix_sines(unit, y_tiles)
-            woven = held("woven", [P, 2 * SLOTS * HALF], BF16)
+            woven = held("woven" if g + 1 < len(units) else "last_woven", [P, 2 * SLOTS * HALF], BF16)
             x_tiles = operand("x", woven, width)
             for c0, step, piece in cosines[unit]:
                 gain(x_tiles, piece, GCOS_ROW + b, c0, step)

@@ -30,8 +30,8 @@ E_BANKS = (0, 1, 2)
 VECTOR_BANK = 3
 OUT_BANKS = (4, 5, 6, 7)
 GSIN_ROW, GCOS_ROW, VECTOR_ROWS = 0, 2, 4
-VECTOR_RESULTS = 3
-GPSIMD_COLS = {512: 128, 256: 56, 128: 0}
+VECTOR_RESULTS = 2
+GPSIMD_COLS = {512: 112, 256: 48, 128: 0}
 
 
 def tile_list_fragment_phase_fields_kernel(
@@ -85,9 +85,6 @@ def tile_list_fragment_phase_fields_kernel(
         nc.vector.memset(tab_rows[:].bitcast(I32), 0)
         nc.vector.memset(tab2_plane[:].bitcast(I32), 0)
         nc.vector.memset(v_plane[0][:].bitcast(I32), 0)
-        warm = held("warm", [P, 2], F32)
-        nc.gpsimd.memset(warm[:, 0:1], 0.0)
-        nc.scalar.activation(warm[:, 1:2], warm[:, 0:1], ACT.Sin)
         identity = held("identity", [P, P], F32)
         make_identity(nc, identity[:])
 
@@ -225,8 +222,9 @@ def tile_list_fragment_phase_fields_kernel(
         for t in range(SLOTS):
             nc.tensor.transpose(vector_bank[:, t * P : (t + 1) * P], vector_rows[:, t:PASS:SLOTS], identity[:])
         vectors_psum = vector_bank[:].rearrange("p (t r) -> p t r", t=SLOTS)
-        vectors = held("vectors", [P, SLOTS, VECTOR_ROWS], F32)
-        nc.vector.tensor_copy(vectors[:], vectors_psum[:, :, 0:VECTOR_ROWS])
+        vectors_sb = held("vectors_sb", [P, VECTOR_ROWS, SLOTS], F32)
+        vectors = vectors_sb[:].rearrange("p r t -> p t r")
+        nc.vector.tensor_copy(vectors, vectors_psum[:, :, 0:VECTOR_ROWS])
         gather_v(1, 1)
         h_pass(1, 1)
         h_finish(HALF, HALF)
@@ -234,7 +232,7 @@ def tile_list_fragment_phase_fields_kernel(
         mcos_rounded = held("mcos_rounded", [P, 2 * SLOTS * N], BF16, reuses="woven")
         mcos_words = held("mcos_words", [P, 2 * N], U32)
         mcos_plane = held("mcos_plane", [P, 2 * N], U8)
-        for b, copy in enumerate((nc.scalar.copy, nc.vector.tensor_copy)):
+        for b, copy in enumerate((nc.vector.tensor_copy, nc.vector.tensor_copy)):
             copy(
                 side_by_side(mcos_rounded[:, b * SLOTS * N : (b + 1) * SLOTS * N], 2), by_slot(mcos_raw[b][:], 2)
             )
@@ -269,9 +267,9 @@ def tile_list_fragment_phase_fields_kernel(
                         stop=True,
                     )
                 for t in range(t0, t0 + per_bank):
+                    nc.scalar.activation(sine[:, t, :], sums[t], ACT.Sin, bias=phi_sb[:, b, t : t + 1])
                     if not last:
                         nc.scalar.activation(size[:, t, :], sums[t], ACT.Abs, bias=phi_sb[:, b, t : t + 1])
-                    nc.scalar.activation(sine[:, t, :], sums[t], ACT.Sin, bias=phi_sb[:, b, t : t + 1])
             if last:
                 for t in range(SLOTS):
                     nc.scalar.activation(size[:, t, :], sums[t], ACT.Abs, bias=phi_sb[:, b, t : t + 1])
@@ -293,7 +291,7 @@ def tile_list_fragment_phase_fields_kernel(
 
         def gain(tiles, values, row, c0, width):
             split = width - GPSIMD_COLS[width]
-            for engine, gains, k0, k1, run in ((nc.vector, vectors_psum, 0, split, 2), (nc.gpsimd, vectors, split, width, 1)):
+            for engine, gains, k0, k1, run in ((nc.vector, vectors_psum, 0, split, 2), (nc.gpsimd, vectors, split, width, 2)):
                 if k1 > k0:
                     part = tiles[0][:, SLOTS * (c0 + k0) : SLOTS * (c0 + k1)]
                     engine.tensor_tensor(

@@ -25,13 +25,15 @@ QUADS = 4
 HALF = 512
 CHUNK = 128
 LIST_COLS = 512 // 16
+QUARTER = HALF // 2
+RUN = 2
 V2_FIRST_ROW = 8
 E_BANKS = (0, 1, 2)
-VECTOR_BANK = 3
+GAIN_BANK = 3
 OUT_BANKS = (4, 5, 6, 7)
-GSIN_ROW, GCOS_ROW, VECTOR_ROWS = 0, 2, 4
+GSIN_ROW, GCOS_ROW, GAIN_ROWS = 0, 2, 4
 VECTOR_RESULTS = 2
-GPSIMD_COLS = {512: 112, 256: 48, 128: 0}
+GPSIMD_COLS = {HALF: 112, QUARTER: 48, CHUNK: 0}
 
 
 def tile_list_fragment_phase_fields_kernel(
@@ -47,7 +49,7 @@ def tile_list_fragment_phase_fields_kernel(
         def held(name, shape, dtype, reuses=None):
             return keep.tile(shape, dtype, name=name, tag=reuses or name, align_bytes=64)
 
-        def turn(name, shape, dtype, bufs=2):
+        def turn(name, shape, dtype, bufs):
             return ring.tile(shape, dtype, name=name, align_bytes=64, bufs=bufs)
 
         def bank(index):
@@ -71,11 +73,14 @@ def tile_list_fragment_phase_fields_kernel(
         def quantise(words, plane, src):
             nc.vector.quantize_mx(out=words.bitcast(FP8X4), scales=plane, in_=src)
 
-        def side_by_side(dst, run):
-            return dst.rearrange("p (c i t) -> p c t i", i=run, t=SLOTS)
+        def side_by_side(dst):
+            return dst.rearrange("p (c i t) -> p c t i", i=RUN, t=SLOTS)
 
-        def by_slot(src, run):
-            return src.rearrange("p t (c i) -> p c t i", i=run)
+        def by_slot(src):
+            return src.rearrange("p t (c i) -> p c t i", i=RUN)
+
+        def spread(values, width):
+            return values.unsqueeze(1).unsqueeze(3).to_broadcast([P, width // RUN, SLOTS, RUN])
 
         idx = held("idx", [P, S // 16], U16)
         idx2 = held("idx2", [P, S2 // 16], U16)
@@ -162,15 +167,12 @@ def tile_list_fragment_phase_fields_kernel(
                         stop=(a == 1 and t == SLOTS - 1),
                     )
 
-        def spread(by_slot_values, width, run):
-            return by_slot_values.unsqueeze(1).unsqueeze(3).to_broadcast([P, width // run, SLOTS, run])
-
         def h_finish(j0, width):
             woven = held("h_woven%d" % j0, [P, SLOTS * width], BF16)
             for c in range(width // CHUNK):
                 source = h_banks[divmod(j0 // CHUNK + c, HALF // CHUNK)][:].rearrange("p (t j) -> p t j", t=SLOTS)
                 part = woven[:, SLOTS * c * CHUNK : SLOTS * (c + 1) * CHUNK]
-                nc.vector.tensor_tensor(side_by_side(part, 2), by_slot(source, 2), spread(bq_sb[:], CHUNK, 2), ALU.add)
+                nc.vector.tensor_tensor(side_by_side(part), by_slot(source), spread(bq_sb[:], CHUNK), ALU.add)
             quantise(h_words[:, j0 : j0 + width], h_plane[:, j0 : j0 + width], woven[:])
 
         def gather_v2(b):
@@ -187,18 +189,20 @@ def tile_list_fragment_phase_fields_kernel(
 
         prepare_wq(0)
         gather_v(0, 0)
-        gather_v(0, 1)
         h_pass(0, 0)
+        for b in range(2):
+            order_v2(b, gather_v2(b))
+        gather_v(0, 1)
         h_pass(0, 1)
 
         bq_sb = held("bq_sb", [P, SLOTS], F32, reuses="wq_rounded0")
         nc.sync.dma_start(bq_sb[:], bq.rearrange("(p t) -> p t", t=SLOTS))
         phi_sb = load_by_slot("phi_sb", phi, reuses="v_rows")
-        mcos_raw = [load_rows("mcos_raw0", mcos, 0, reuses="tab_sb0"), load_rows("mcos_raw1", mcos, 1, reuses="v_words0")]
-        vector_rows = held("vector_rows", [P, PASS], F32, reuses="wq_words0")
-        nc.vector.memset(vector_rows[:], 0.0)
+        mcos_raw = [load_rows("mcos_raw0", mcos, 0, reuses="tab2_sb"), load_rows("mcos_raw1", mcos, 1, reuses="tab_sb0")]
+        gain_rows = held("gain_rows", [P, PASS], F32, reuses="v2_listed0")
+        nc.vector.memset(gain_rows[:], 0.0)
         for vec, row in ((gsin, GSIN_ROW), (gcos, GCOS_ROW)):
-            nc.sync.dma_start(vector_rows[row : row + 2, :], vec.rearrange("(b m) -> b m", b=2))
+            nc.sync.dma_start(gain_rows[row : row + 2, :], vec.rearrange("(b m) -> b m", b=2))
         prepare_wq(1)
         m4_sb = held("m4_sb", [P, 2 * 2 * N], U8, reuses="wq_raw1")
         nc.sync.dma_start(
@@ -212,19 +216,16 @@ def tile_list_fragment_phase_fields_kernel(
                 m4_scales[:, 4 * q : 4 * q + 4, :].bitcast(I32).rearrange("b r c -> r b c"),
             )
 
-        for b in range(2):
-            order_v2(b, gather_v2(b))
         gather_v(1, 0)
         h_pass(1, 0)
-        h_finish(0, HALF // 2)
-        h_finish(HALF // 2, HALF // 2)
-        vector_bank = bank(VECTOR_BANK)
+        h_finish(0, QUARTER)
+        h_finish(QUARTER, QUARTER)
+        gain_bank = bank(GAIN_BANK)
         for t in range(SLOTS):
-            nc.tensor.transpose(vector_bank[:, t * P : (t + 1) * P], vector_rows[:, t:PASS:SLOTS], identity[:])
-        vectors_psum = vector_bank[:].rearrange("p (t r) -> p t r", t=SLOTS)
-        vectors_sb = held("vectors_sb", [P, VECTOR_ROWS, SLOTS], F32)
-        vectors = vectors_sb[:].rearrange("p r t -> p t r")
-        nc.vector.tensor_copy(vectors, vectors_psum[:, :, 0:VECTOR_ROWS])
+            nc.tensor.transpose(gain_bank[:, t * P : (t + 1) * P], gain_rows[:, t:PASS:SLOTS], identity[:])
+        gains_psum = gain_bank[:].rearrange("p (t r) -> p t r", t=SLOTS)
+        gains_sbuf = held("gains_sbuf", [P, GAIN_ROWS, SLOTS], F32)[:].rearrange("p r t -> p t r")
+        nc.vector.tensor_copy(gains_sbuf, gains_psum[:, :, 0:GAIN_ROWS])
         gather_v(1, 1)
         h_pass(1, 1)
         h_finish(HALF, HALF)
@@ -232,15 +233,13 @@ def tile_list_fragment_phase_fields_kernel(
         mcos_rounded = held("mcos_rounded", [P, 2 * SLOTS * N], BF16, reuses="woven")
         mcos_words = held("mcos_words", [P, 2 * N], U32)
         mcos_plane = held("mcos_plane", [P, 2 * N], U8)
-        for b, copy in enumerate((nc.vector.tensor_copy, nc.vector.tensor_copy)):
-            copy(
-                side_by_side(mcos_rounded[:, b * SLOTS * N : (b + 1) * SLOTS * N], 2), by_slot(mcos_raw[b][:], 2)
-            )
+        for b in range(2):
+            nc.vector.tensor_copy(side_by_side(mcos_rounded[:, b * SLOTS * N : (b + 1) * SLOTS * N]), by_slot(mcos_raw[b][:]))
         for c0, c1 in ((0, 512), (512, 2 * N)):
             quantise(mcos_words[:, c0:c1], mcos_plane[:, c0:c1], mcos_rounded[:, SLOTS * c0 : SLOTS * c1])
 
-        quarter = HALF // 2
-        units = [(0, quarter, 0), (quarter, quarter, 0), (0, HALF, 1), (HALF, HALF, 0), (HALF, quarter, 1), (HALF + quarter, quarter, 1)]
+        units = [(0, QUARTER, 0), (QUARTER, QUARTER, 0), (0, HALF, 1)]
+        units.extend([(HALF, HALF, 0), (HALF, QUARTER, 1), (HALF + QUARTER, QUARTER, 1)])
         sines = {}
         cosines = {}
         out_banks = {}
@@ -250,7 +249,7 @@ def tile_list_fragment_phase_fields_kernel(
             j0, width, b = unit
             last = unit == units[-1]
             sine = turn("sine", [P, SLOTS, width], F32, bufs=3)
-            size = turn("size", [P, SLOTS, width], F32)
+            size = turn("size", [P, SLOTS, width], F32, bufs=2)
             per_bank = HALF // width
             sums = []
             for t0 in range(0, SLOTS, per_bank):
@@ -291,11 +290,11 @@ def tile_list_fragment_phase_fields_kernel(
 
         def gain(tiles, values, row, c0, width):
             split = width - GPSIMD_COLS[width]
-            for engine, gains, k0, k1, run in ((nc.vector, vectors_psum, 0, split, 2), (nc.gpsimd, vectors, split, width, 2)):
+            for engine, gains, k0, k1 in ((nc.vector, gains_psum, 0, split), (nc.gpsimd, gains_sbuf, split, width)):
                 if k1 > k0:
                     part = tiles[0][:, SLOTS * (c0 + k0) : SLOTS * (c0 + k1)]
                     engine.tensor_tensor(
-                        side_by_side(part, run), by_slot(values[:, :, k0:k1], run), spread(gains[:, :, row], k1 - k0, run), ALU.mult
+                        side_by_side(part), by_slot(values[:, :, k0:k1]), spread(gains[:, :, row], k1 - k0), ALU.mult
                     )
 
         def quantise_part(tiles, c0, width):

@@ -26,6 +26,7 @@ HALF = 512
 CHUNK = 128
 LIST_COLS = 512 // 16
 QUARTER = HALF // 2
+LINE = 4
 RUN = 2
 V2_FIRST_ROW = 8
 E_BANKS = (0, 1, 2)
@@ -79,8 +80,11 @@ def tile_list_fragment_phase_fields_kernel(
         def by_slot(src):
             return src.rearrange("p t (c i) -> p c t i", i=RUN)
 
-        def spread(values, width):
-            return values.unsqueeze(1).unsqueeze(3).to_broadcast([P, width // RUN, SLOTS, RUN])
+        def spread(values, width, run=RUN):
+            return values.unsqueeze(1).unsqueeze(3).to_broadcast([P, width // run, SLOTS, run])
+
+        def by_line(flat):
+            return flat.rearrange("p (c t i) -> p c t i", t=SLOTS, i=LINE)
 
         idx = held("idx", [P, S // 16], U16)
         idx2 = held("idx2", [P, S2 // 16], U16)
@@ -248,16 +252,17 @@ def tile_list_fragment_phase_fields_kernel(
         def phases(unit):
             j0, width, b = unit
             last = unit == units[-1]
-            sine = turn("sine", [P, SLOTS, width], F32, bufs=3)
-            size = turn("size", [P, SLOTS, width], F32, bufs=2)
+            sine = turn("sine", [P, SLOTS * width], F32, bufs=3)
+            size = turn("size", [P, SLOTS * width], F32, bufs=2)
             per_bank = HALF // width
             sums = []
             for t0 in range(0, SLOTS, per_bank):
                 e_banks.append(bank(E_BANKS[len(e_banks) % len(E_BANKS)]))
                 for t in range(t0, t0 + per_bank):
-                    sums.append(e_banks[-1][:, (t - t0) * width : (t - t0 + 1) * width])
+                    target = e_banks[-1][:, (t - t0) * width : (t - t0 + 1) * width]
+                    sums.append(target.rearrange("p (c i) -> p c i", i=LINE))
                     nc.tensor.matmul_mx(
-                        out=sums[t],
+                        out=target,
                         lhsT=v2_words[b][:, t * P : (t + 1) * P].bitcast(FP8X4),
                         lhsT_scale=v2_plane[V2_FIRST_ROW:P, b * PASS + t * P : b * PASS + (t + 1) * P],
                         rhs=h_words[:, j0 : j0 + width].bitcast(FP8X4),
@@ -266,19 +271,19 @@ def tile_list_fragment_phase_fields_kernel(
                         stop=True,
                     )
                 for t in range(t0, t0 + per_bank):
-                    nc.scalar.activation(sine[:, t, :], sums[t], ACT.Sin, bias=phi_sb[:, b, t : t + 1])
+                    nc.scalar.activation(by_line(sine[:])[:, :, t, :], sums[t], ACT.Sin, bias=phi_sb[:, b, t : t + 1])
                     if not last:
-                        nc.scalar.activation(size[:, t, :], sums[t], ACT.Abs, bias=phi_sb[:, b, t : t + 1])
+                        nc.scalar.activation(by_line(size[:])[:, :, t, :], sums[t], ACT.Abs, bias=phi_sb[:, b, t : t + 1])
             if last:
                 for t in range(SLOTS):
-                    nc.scalar.activation(size[:, t, :], sums[t], ACT.Abs, bias=phi_sb[:, b, t : t + 1])
+                    nc.scalar.activation(by_line(size[:])[:, :, t, :], sums[t], ACT.Abs, bias=phi_sb[:, b, t : t + 1])
             sines[unit] = sine
             step = CHUNK if last else width
             cosine = turn("cosine", [P, SLOTS * width], F32, bufs=3)
             cosines[unit] = []
             for c0 in range(0, width, step):
-                piece = cosine[:, SLOTS * c0 : SLOTS * (c0 + step)].rearrange("p (t j) -> p t j", t=SLOTS)
-                nc.scalar.activation(piece, size[:, :, c0 : c0 + step], ACT.Sin, bias=math.pi / 2, scale=-1.0)
+                piece = cosine[:, SLOTS * c0 : SLOTS * (c0 + step)]
+                nc.scalar.activation(piece, size[:, SLOTS * c0 : SLOTS * (c0 + step)], ACT.Sin, bias=math.pi / 2, scale=-1.0)
                 cosines[unit].append((c0, step, piece))
 
         def operand(name, woven, width):
@@ -294,7 +299,10 @@ def tile_list_fragment_phase_fields_kernel(
                 if k1 > k0:
                     part = tiles[0][:, SLOTS * (c0 + k0) : SLOTS * (c0 + k1)]
                     engine.tensor_tensor(
-                        side_by_side(part), by_slot(values[:, :, k0:k1]), spread(gains[:, :, row], k1 - k0), ALU.mult
+                        part.rearrange("p (c i t) -> p c t i", i=LINE, t=SLOTS),
+                        by_line(values[:, SLOTS * k0 : SLOTS * k1]),
+                        spread(gains[:, :, row], k1 - k0, LINE),
+                        ALU.mult,
                     )
 
         def quantise_part(tiles, c0, width):

@@ -29,11 +29,12 @@ QUARTER = HALF // 2
 LINE = 4
 RUN = 2
 V2_FIRST_ROW = 8
-E_BANKS = (0, 1, 2)
-GAIN_BANK = 3
-OUT_BANKS = (4, 5, 6, 7)
+E_BANKS = ((0, 1), (2, 3), (7, 4, 5, 6), (7, 4, 5, 6), (7, 4), (5, 7))
+GAIN_BANK = 1
+OUT_BANKS = (0, 2, 3, 6)
 GSIN_ROW, GCOS_ROW, GAIN_ROWS = 0, 2, 4
-VECTOR_RESULTS = 2
+SCALAR_QUARTERS = (1, 2)
+VECTOR_RESULTS = 3
 GPSIMD_COLS = {HALF: 112, QUARTER: 48, CHUNK: 0}
 
 
@@ -74,11 +75,11 @@ def tile_list_fragment_phase_fields_kernel(
         def quantise(words, plane, src):
             nc.vector.quantize_mx(out=words.bitcast(FP8X4), scales=plane, in_=src)
 
-        def side_by_side(dst):
-            return dst.rearrange("p (c i t) -> p c t i", i=RUN, t=SLOTS)
+        def side_by_side(dst, run=RUN):
+            return dst.rearrange("p (c i t) -> p c t i", i=run, t=SLOTS)
 
-        def by_slot(src):
-            return src.rearrange("p t (c i) -> p c t i", i=RUN)
+        def by_slot(src, run=RUN):
+            return src.rearrange("p t (c i) -> p c t i", i=run)
 
         def spread(values, width, run=RUN):
             return values.unsqueeze(1).unsqueeze(3).to_broadcast([P, width // run, SLOTS, run])
@@ -105,6 +106,8 @@ def tile_list_fragment_phase_fields_kernel(
             nc.sync.dma_start(tab2_plane[V2_FIRST_ROW + r : P : 32, :].bitcast(I32), tab2_scales[0, r:16:4, :].bitcast(I32))
         tab_sb = [load_words("tab_sb0", tab_words[0])]
         wq_raw.append(load_rows("wq_raw1", wq, 1))
+        warm = held("warm", [P, 1], F32)
+        nc.scalar.activation(warm[:], identity[:, 0:1], ACT.Sin)
 
         v_rows = held("v_rows", [P, S], U8)
         nc.vector.tensor_copy(v_rows[:], tab_rows[:].indirect(idx[:]))
@@ -131,8 +134,9 @@ def tile_list_fragment_phase_fields_kernel(
 
         wq_words = []
         wq_plane = []
-        v_words = [held("v_words%d" % a, [P, S], U32) for a in range(2)]
+        v_words = {}
         h_banks = {}
+        h_biased = {}
         h_words = held("h_words", [P, S], U32)
         h_plane = held("h_plane", [P, S], U8)
         v2_words = {}
@@ -149,38 +153,52 @@ def tile_list_fragment_phase_fields_kernel(
             wq_words.append(words)
             wq_plane.append(plane)
 
-        def gather_v(a, half):
+        def gather_v(a, half, reuses=None):
+            v_words[a, half] = held("v_words%d%d" % (a, half), [P, HALF], U32, reuses)
             nc.vector.tensor_copy(
-                v_words[a][:, half * HALF : (half + 1) * HALF],
+                v_words[a, half][:],
                 tab_sb[a][:].bitcast(U32).indirect(idx[:, half * LIST_COLS : (half + 1) * LIST_COLS]),
             )
 
-        def h_pass(a, half):
-            for c in range(HALF // CHUNK):
+        def h_pass(a, quarter):
+            for u in range(2):
                 if a == 0:
-                    h_banks[half, c] = bank(SLOTS * half + c)
-                cols = slice(half * HALF + c * CHUNK, half * HALF + (c + 1) * CHUNK)
-                for t in range(SLOTS):
+                    h_banks[quarter, u] = bank(2 * quarter + u)
+                if quarter in SCALAR_QUARTERS:
+                    parts = [(t, quarter * QUARTER, QUARTER) for t in (2 * u, 2 * u + 1)]
+                else:
+                    parts = [(t, quarter * QUARTER + u * CHUNK, CHUNK) for t in range(SLOTS)]
+                for k, (t, j0, width) in enumerate(parts):
                     nc.tensor.matmul_mx(
-                        out=h_banks[half, c][:, t * CHUNK : (t + 1) * CHUNK],
+                        out=h_banks[quarter, u][:, k * width : (k + 1) * width],
                         lhsT=wq_words[a][:, t * P : (t + 1) * P].bitcast(FP8X4),
                         lhsT_scale=wq_plane[a][:, t * P : (t + 1) * P],
-                        rhs=v_words[a][:, cols].bitcast(FP8X4),
-                        rhs_scale=v_plane[a][:, cols],
-                        start=(a == 0 and t == 0),
-                        stop=(a == 1 and t == SLOTS - 1),
+                        rhs=v_words[a, j0 // HALF][:, j0 % HALF : j0 % HALF + width].bitcast(FP8X4),
+                        rhs_scale=v_plane[a][:, j0 : j0 + width],
+                        start=(a == 0 and k == 0),
+                        stop=(a == 1 and k == len(parts) - 1),
                     )
 
-        def h_finish(j0, width):
-            woven = held("h_woven%d" % j0, [P, SLOTS * width], BF16)
-            for c in range(width // CHUNK):
-                source = h_banks[divmod(j0 // CHUNK + c, HALF // CHUNK)][:].rearrange("p (t j) -> p t j", t=SLOTS)
-                part = woven[:, SLOTS * c * CHUNK : SLOTS * (c + 1) * CHUNK]
-                nc.vector.tensor_tensor(side_by_side(part), by_slot(source), spread(bq_sb[:], CHUNK), ALU.add)
-            quantise(h_words[:, j0 : j0 + width], h_plane[:, j0 : j0 + width], woven[:])
+        def h_bias(quarter):
+            h_biased[quarter] = held("h_biased%d" % quarter, [P, SLOTS, QUARTER], BF16)
+            for t in range(SLOTS):
+                source = h_banks[quarter, t // 2][:, (t % 2) * QUARTER : (t % 2 + 1) * QUARTER]
+                nc.scalar.activation(h_biased[quarter][:, t, :], source, ACT.Identity, bias=bq_sb[:, t : t + 1])
 
-        def gather_v2(b):
-            listed = held("v2_listed%d" % b, [P, PASS], U32)
+        def h_finish(quarter, reuses=None):
+            woven = held("h_woven%d" % quarter, [P, SLOTS * QUARTER], BF16, reuses)
+            if quarter in SCALAR_QUARTERS:
+                nc.vector.tensor_copy(side_by_side(woven[:], 2 * RUN), by_slot(h_biased[quarter][:], 2 * RUN))
+            else:
+                for u in range(2):
+                    source = h_banks[quarter, u][:].rearrange("p (t j) -> p t j", t=SLOTS)
+                    part = woven[:, SLOTS * u * CHUNK : SLOTS * (u + 1) * CHUNK]
+                    nc.vector.tensor_tensor(side_by_side(part), by_slot(source), spread(bq_sb[:], CHUNK), ALU.add)
+            cols = slice(quarter * QUARTER, (quarter + 1) * QUARTER)
+            quantise(h_words[:, cols], h_plane[:, cols], woven[:])
+
+        def gather_v2(b, reuses=None):
+            listed = held("v2_listed%d" % b, [P, PASS], U32, reuses)
             nc.vector.tensor_copy(listed[:], tab2_sb[:].bitcast(U32).indirect(idx2[:, b * LIST_COLS : (b + 1) * LIST_COLS]))
             return listed
 
@@ -193,22 +211,23 @@ def tile_list_fragment_phase_fields_kernel(
 
         prepare_wq(0)
         gather_v(0, 0)
-        h_pass(0, 0)
+        for quarter in range(2):
+            h_pass(0, quarter)
         for b in range(2):
             order_v2(b, gather_v2(b))
         gather_v(0, 1)
-        h_pass(0, 1)
+        for quarter in range(2, 4):
+            h_pass(0, quarter)
 
         bq_sb = held("bq_sb", [P, SLOTS], F32, reuses="wq_rounded0")
         nc.sync.dma_start(bq_sb[:], bq.rearrange("(p t) -> p t", t=SLOTS))
         phi_sb = load_by_slot("phi_sb", phi, reuses="v_rows")
         mcos_raw = [load_rows("mcos_raw0", mcos, 0, reuses="tab2_sb"), load_rows("mcos_raw1", mcos, 1, reuses="tab_sb0")]
-        gain_rows = held("gain_rows", [P, PASS], F32, reuses="v2_listed0")
-        nc.vector.memset(gain_rows[:], 0.0)
+        prepare_wq(1)
+        gain_rows = wq_raw[1][:, 0, :]
         for vec, row in ((gsin, GSIN_ROW), (gcos, GCOS_ROW)):
             nc.sync.dma_start(gain_rows[row : row + 2, :], vec.rearrange("(b m) -> b m", b=2))
-        prepare_wq(1)
-        m4_sb = held("m4_sb", [P, 2 * 2 * N], U8, reuses="wq_raw1")
+        m4_sb = held("m4_sb", [P, 2 * 2 * N], U8, reuses="v2_listed1")
         nc.sync.dma_start(
             m4_sb[:].bitcast(I32).rearrange("p (b c) -> p b c", b=2), m4_words.bitcast(I32).rearrange("b p c -> p b c")
         )
@@ -220,19 +239,14 @@ def tile_list_fragment_phase_fields_kernel(
                 m4_scales[:, 4 * q : 4 * q + 4, :].bitcast(I32).rearrange("b r c -> r b c"),
             )
 
-        gather_v(1, 0)
-        h_pass(1, 0)
-        h_finish(0, QUARTER)
-        h_finish(QUARTER, QUARTER)
-        gain_bank = bank(GAIN_BANK)
-        for t in range(SLOTS):
-            nc.tensor.transpose(gain_bank[:, t * P : (t + 1) * P], gain_rows[:, t:PASS:SLOTS], identity[:])
-        gains_psum = gain_bank[:].rearrange("p (t r) -> p t r", t=SLOTS)
-        gains_sbuf = held("gains_sbuf", [P, GAIN_ROWS, SLOTS], F32)[:].rearrange("p r t -> p t r")
-        nc.vector.tensor_copy(gains_sbuf, gains_psum[:, :, 0:GAIN_ROWS])
-        gather_v(1, 1)
-        h_pass(1, 1)
-        h_finish(HALF, HALF)
+        for half in range(2):
+            gather_v(1, half)
+        for quarter in range(4):
+            h_pass(1, quarter)
+        for quarter in SCALAR_QUARTERS:
+            h_bias(quarter)
+        for quarter in (0, 1, 3, 2):
+            h_finish(quarter)
 
         mcos_rounded = held("mcos_rounded", [P, 2 * SLOTS * N], BF16, reuses="woven")
         mcos_words = held("mcos_words", [P, 2 * N], U32)
@@ -253,11 +267,15 @@ def tile_list_fragment_phase_fields_kernel(
             j0, width, b = unit
             last = unit == units[-1]
             sine = turn("sine", [P, SLOTS * width], F32, bufs=3)
-            size = turn("size", [P, SLOTS * width], F32, bufs=2)
+            if unit == units[3]:
+                size = held("late_size", [P, SLOTS * width], F32, reuses="wq_raw0")
+            else:
+                size = turn("size", [P, SLOTS * width], F32, bufs=2)
             per_bank = HALF // width
             sums = []
+            early = 1 if width == HALF else 0
             for t0 in range(0, SLOTS, per_bank):
-                e_banks.append(bank(E_BANKS[len(e_banks) % len(E_BANKS)]))
+                e_banks.append(bank(E_BANKS[units.index(unit)][t0 // per_bank]))
                 for t in range(t0, t0 + per_bank):
                     target = e_banks[-1][:, (t - t0) * width : (t - t0 + 1) * width]
                     sums.append(target.rearrange("p (c i) -> p c i", i=LINE))
@@ -272,18 +290,21 @@ def tile_list_fragment_phase_fields_kernel(
                     )
                 for t in range(t0, t0 + per_bank):
                     nc.scalar.activation(by_line(sine[:])[:, :, t, :], sums[t], ACT.Sin, bias=phi_sb[:, b, t : t + 1])
-                    if not last:
+                    if t < early:
                         nc.scalar.activation(by_line(size[:])[:, :, t, :], sums[t], ACT.Abs, bias=phi_sb[:, b, t : t + 1])
-            if last:
-                for t in range(SLOTS):
-                    nc.scalar.activation(by_line(size[:])[:, :, t, :], sums[t], ACT.Abs, bias=phi_sb[:, b, t : t + 1])
+            for t in range(early, SLOTS):
+                nc.scalar.activation(by_line(size[:])[:, :, t, :], sums[t], ACT.Abs, bias=phi_sb[:, b, t : t + 1])
             sines[unit] = sine
             step = CHUNK if last else width
             cosine = turn("cosine", [P, SLOTS * width], F32, bufs=3)
             cosines[unit] = []
             for c0 in range(0, width, step):
                 piece = cosine[:, SLOTS * c0 : SLOTS * (c0 + step)]
-                nc.scalar.activation(piece, size[:, SLOTS * c0 : SLOTS * (c0 + step)], ACT.Sin, bias=math.pi / 2, scale=-1.0)
+                source = size[:, SLOTS * c0 : SLOTS * (c0 + step)]
+                for t0, t1 in ((0, SLOTS - 1), (SLOTS - 1, SLOTS)) if width == HALF else ((0, SLOTS),):
+                    nc.scalar.activation(
+                        by_line(piece)[:, :, t0:t1, :], by_line(source)[:, :, t0:t1, :], ACT.Sin, bias=math.pi / 2, scale=-1.0
+                    )
                 cosines[unit].append((c0, step, piece))
 
         def operand(name, woven, width):
@@ -309,70 +330,79 @@ def tile_list_fragment_phase_fields_kernel(
             woven, words, plane = tiles
             quantise(words[:, c0 : c0 + width], plane[:, c0 : c0 + width], woven[:, SLOTS * c0 : SLOTS * (c0 + width)])
 
-        def mix_sines(unit, tiles):
-            j0, width, b = unit
-            quantise_part(tiles, 0, width)
-            for c0 in range(0, width, CHUNK):
-                chunk = (j0 + c0) // CHUNK
-                if b == 0:
-                    out_banks[chunk] = bank(OUT_BANKS[chunk % len(OUT_BANKS)])
-                cols = slice(c0, c0 + CHUNK)
-                for n in range(N // P):
-                    nc.tensor.matmul_mx(
-                        out=out_banks[chunk][:, n * CHUNK : (n + 1) * CHUNK],
-                        lhsT=m4_sb[:, 2 * (b * N + n * P) : 2 * (b * N + (n + 1) * P)].bitcast(FP4X4),
-                        lhsT_scale=m4_plane[:, b * N + n * P : b * N + (n + 1) * P],
-                        rhs=tiles[1][:, cols].bitcast(FP8X4),
-                        rhs_scale=tiles[2][:, cols],
-                        start=(b == 0 and n == 0),
-                        stop=False,
-                    )
+        out_rows = out.rearrange("(n p) j -> p n j", p=P)
 
-        def mix_cosines(unit, tiles, k0, width):
+        def mix(unit, tiles, k0, width, sines_pass):
             j0, b = unit[0], unit[2]
             quantise_part(tiles, k0, width)
-            for c0 in range(k0, k0 + width, CHUNK):
+            step = width if j0 < HALF else CHUNK
+            for c0 in range(k0, k0 + width, step):
                 chunk = (j0 + c0) // CHUNK
-                cols = slice(c0, c0 + CHUNK)
+                cols = slice(c0, c0 + step)
                 for n in range(N // P):
+                    if j0 < HALF:
+                        key, at = n, j0 + c0
+                        start, stop = sines_pass and unit == units[0], not sines_pass and b == 1
+                    else:
+                        key, at = chunk, n * CHUNK
+                        start, stop = sines_pass and b == 0 and n == 0, not sines_pass and b == 1 and n == N // P - 1
+                    if start:
+                        out_banks[key] = bank(OUT_BANKS[key % len(OUT_BANKS)])
+                    w0 = b * N + n * P
+                    if sines_pass:
+                        weights, scales = m4_sb[:, 2 * w0 : 2 * (w0 + P)].bitcast(FP4X4), m4_plane[:, w0 : w0 + P]
+                    else:
+                        weights, scales = mcos_words[:, w0 : w0 + P].bitcast(FP8X4), mcos_plane[:, w0 : w0 + P]
                     nc.tensor.matmul_mx(
-                        out=out_banks[chunk][:, n * CHUNK : (n + 1) * CHUNK],
-                        lhsT=mcos_words[:, b * N + n * P : b * N + (n + 1) * P].bitcast(FP8X4),
-                        lhsT_scale=mcos_plane[:, b * N + n * P : b * N + (n + 1) * P],
+                        out=out_banks[key][:, at : at + step],
+                        lhsT=weights,
+                        lhsT_scale=scales,
                         rhs=tiles[1][:, cols].bitcast(FP8X4),
                         rhs_scale=tiles[2][:, cols],
-                        start=False,
-                        stop=(b == 1 and n == N // P - 1),
+                        start=start,
+                        stop=stop,
                     )
-                if b == 1:
-                    result = held("result%d" % chunk, [P, N // P, CHUNK], F32)
-                    source = out_banks[chunk][:, 0:N].rearrange("p (n j) -> p n j", j=CHUNK)
-                    if chunk < VECTOR_RESULTS:
-                        nc.vector.tensor_copy(result[:], source)
-                    else:
-                        nc.scalar.copy(result[:], source)
-                    nc.sync.dma_start(
-                        out.rearrange("(n p) j -> p n j", p=P)[:, :, chunk * CHUNK : (chunk + 1) * CHUNK], result[:]
-                    )
+                    if stop and j0 < HALF:
+                        if n < VECTOR_RESULTS:
+                            result = held("rows%d" % n, [P, HALF], F32)
+                            nc.vector.tensor_copy(result[:], out_banks[key][:])
+                        else:
+                            result = held("rows%d" % n, [P, HALF], F32, reuses="wq_raw0")
+                            nc.scalar.copy(result[:], out_banks[key][:])
+                        nc.sync.dma_start(out_rows[:, n, 0:HALF], result[:])
+                    elif stop:
+                        result = held("result%d" % chunk, [P, N // P, CHUNK], F32)
+                        nc.scalar.copy(result[:], out_banks[key][:, 0:N].rearrange("p (n j) -> p n j", j=CHUNK))
+                        nc.sync.dma_start(out_rows[:, :, chunk * CHUNK : (chunk + 1) * CHUNK], result[:])
 
         phases(units[0])
+        gain_bank = bank(GAIN_BANK)
+        for t in range(SLOTS):
+            nc.tensor.transpose(gain_bank[:, t * P : (t + 1) * P], gain_rows[:, t:PASS:SLOTS], identity[:])
+        gains_psum = gain_bank[:].rearrange("p (t r) -> p t r", t=SLOTS)
+        gains_sbuf = held("gains_sbuf", [P, GAIN_ROWS, SLOTS], F32)[:].rearrange("p r t -> p t r")
+        nc.vector.tensor_copy(gains_sbuf, gains_psum[:, :, 0:GAIN_ROWS])
         waiting = []
         woven = held("woven", [P, 2 * SLOTS * HALF], BF16)
         for g, unit in enumerate(units):
             width, b = unit[1], unit[2]
+            if unit[0] == HALF and b == 0:
+                mix(*waiting[0])
+                waiting = []
+                woven = held("woven", [P, 2 * SLOTS * HALF], BF16)
             if g + 1 < len(units):
                 phases(units[g + 1])
             y_tiles = operand("y", woven[:, SLOTS * HALF :], width)
             gain(y_tiles, sines[unit][:], GSIN_ROW + b, 0, width)
             for args in waiting:
-                mix_cosines(*args)
+                mix(*args)
             waiting = []
-            mix_sines(unit, y_tiles)
+            mix(unit, y_tiles, 0, width, True)
             woven = held("woven" if g + 1 < len(units) else "last_woven", [P, 2 * SLOTS * HALF], BF16)
             x_tiles = operand("x", woven, width)
             for c0, step, piece in cosines[unit]:
                 gain(x_tiles, piece, GCOS_ROW + b, c0, step)
                 if step == width:
-                    waiting.append((unit, x_tiles, c0, step))
+                    waiting.append((unit, x_tiles, c0, step, False))
                 else:
-                    mix_cosines(unit, x_tiles, c0, step)
+                    mix(unit, x_tiles, c0, step, False)

@@ -35,6 +35,7 @@ OUT_BANKS = (0, 2, 3, 6)
 GSIN_ROW, GCOS_ROW, GAIN_ROWS = 0, 2, 4
 SCALAR_QUARTERS = (1, 2)
 VECTOR_RESULTS = 3
+GPSIMD_EXTRA = 64
 GPSIMD_COLS = {HALF: 112, QUARTER: 48, CHUNK: 0}
 
 
@@ -314,8 +315,8 @@ def tile_list_fragment_phase_fields_kernel(
                 codes.tile([P, width], U8, name=name + "_plane", align_bytes=64),
             )
 
-        def gain(tiles, values, row, c0, width):
-            split = width - GPSIMD_COLS[width]
+        def gain(tiles, values, row, c0, width, extra=0):
+            split = width - GPSIMD_COLS[width] - extra
             for engine, gains, k0, k1 in ((nc.vector, gains_psum, 0, split), (nc.gpsimd, gains_sbuf, split, width)):
                 if k1 > k0:
                     part = tiles[0][:, SLOTS * (c0 + k0) : SLOTS * (c0 + k1)]
@@ -393,7 +394,7 @@ def tile_list_fragment_phase_fields_kernel(
             if g + 1 < len(units):
                 phases(units[g + 1])
             y_tiles = operand("y", woven[:, SLOTS * HALF :], width)
-            gain(y_tiles, sines[unit][:], GSIN_ROW + b, 0, width)
+            gain(y_tiles, sines[unit][:], GSIN_ROW + b, 0, width, GPSIMD_EXTRA if g == 3 else 0)
             for args in waiting:
                 mix(*args)
             waiting = []

@@ -34,8 +34,8 @@ GAIN_BANK = 1
 OUT_BANKS = (0, 2, 3, 6)
 GSIN_ROW, GCOS_ROW, GAIN_ROWS = 0, 2, 4
 SCALAR_QUARTERS = (1, 2)
-VECTOR_RESULTS = 3
-GPSIMD_EXTRA = 64
+VECTOR_RESULTS = 2
+GPSIMD_EXTRA = 40
 GPSIMD_COLS = {HALF: 112, QUARTER: 48, CHUNK: 0}
 
 
@@ -242,20 +242,12 @@ def tile_list_fragment_phase_fields_kernel(
 
         for half in range(2):
             gather_v(1, half)
-        for quarter in range(4):
+        for quarter in range(3):
             h_pass(1, quarter)
         for quarter in SCALAR_QUARTERS:
             h_bias(quarter)
-        for quarter in (0, 1, 3, 2):
+        for quarter in range(2):
             h_finish(quarter)
-
-        mcos_rounded = held("mcos_rounded", [P, 2 * SLOTS * N], BF16, reuses="woven")
-        mcos_words = held("mcos_words", [P, 2 * N], U32)
-        mcos_plane = held("mcos_plane", [P, 2 * N], U8)
-        for b in range(2):
-            nc.vector.tensor_copy(side_by_side(mcos_rounded[:, b * SLOTS * N : (b + 1) * SLOTS * N]), by_slot(mcos_raw[b][:]))
-        for c0, c1 in ((0, 512), (512, 2 * N)):
-            quantise(mcos_words[:, c0:c1], mcos_plane[:, c0:c1], mcos_rounded[:, SLOTS * c0 : SLOTS * c1])
 
         units = [(0, QUARTER, 0), (QUARTER, QUARTER, 0), (0, HALF, 1)]
         units.extend([(HALF, HALF, 0), (HALF, QUARTER, 1), (HALF + QUARTER, QUARTER, 1)])
@@ -377,6 +369,17 @@ def tile_list_fragment_phase_fields_kernel(
                         nc.sync.dma_start(out_rows[:, :, chunk * CHUNK : (chunk + 1) * CHUNK], result[:])
 
         phases(units[0])
+        h_pass(1, 3)
+        h_finish(3)
+        h_finish(2)
+        mcos_rounded = held("mcos_rounded", [P, 2 * SLOTS * N], BF16, reuses="woven")
+        mcos_words = held("mcos_words", [P, 2 * N], U32)
+        mcos_plane = held("mcos_plane", [P, 2 * N], U8)
+        for b in range(2):
+            nc.vector.tensor_copy(side_by_side(mcos_rounded[:, b * SLOTS * N : (b + 1) * SLOTS * N]), by_slot(mcos_raw[b][:]))
+        for c0, c1 in ((0, N), (N, 2 * N)):
+            quantise(mcos_words[:, c0:c1], mcos_plane[:, c0:c1], mcos_rounded[:, SLOTS * c0 : SLOTS * c1])
+
         gain_bank = bank(GAIN_BANK)
         for t in range(SLOTS):
             nc.tensor.transpose(gain_bank[:, t * P : (t + 1) * P], gain_rows[:, t:PASS:SLOTS], identity[:])

@@ -26,17 +26,33 @@ HALF = 512
 CHUNK = 128
 LIST_COLS = 512 // 16
 QUARTER = HALF // 2
+GROUPS = 4
+LAP = 32
 LINE = 4
 RUN = 2
 V2_FIRST_ROW = 8
-E_BANKS = ((0, 1), (2, 3), (7, 4, 5, 6), (7, 4, 5, 6), (7, 4), (5, 7))
+E_BANKS = ((0, 1), (2, 3), (4, 5, 6, 7), (4, 5, 6, 7), (4, 5), (6, 4))
 GAIN_BANK = 1
-OUT_BANKS = (0, 2, 3, 6)
+OUT_BANKS = (0, 2, 3, 7)
 GSIN_ROW, GCOS_ROW, GAIN_ROWS = 0, 2, 4
-SCALAR_QUARTERS = (1, 2)
-VECTOR_RESULTS = 2
-GPSIMD_EXTRA = 40
-GPSIMD_COLS = {HALF: 112, QUARTER: 48, CHUNK: 0}
+SCALAR_QUARTERS = (1,)
+AT_WOVEN = 64
+WOVEN = 2 * SLOTS * N + 2 * SLOTS * S
+AT_FIRST = 2 * WOVEN
+AT_TAB0 = AT_FIRST + 4 * HALF
+AT_TAB1 = AT_TAB0
+AT_MCOS0 = AT_TAB0 + 4 * T
+AT_TAB2 = AT_MCOS0 + 4 * SLOTS * N - 64
+AT_MCOS1 = AT_TAB2 + 64
+AT_ROWS = AT_TAB2 + 4 * T2 - 64
+AT_PLANE0 = AT_ROWS + 64
+AT_PLANE1 = AT_PLANE0 + S
+AT_WQ1 = AT_PLANE1 + S
+AT_ROUNDED0 = AT_WQ1 + 4 * SLOTS * H
+AT_ROUNDED1 = AT_ROUNDED0 + 2 * SLOTS * H
+AT_V2 = AT_ROUNDED1 + 2 * SLOTS * H
+TAB1_CUT = T // 4
+GPSIMD_COLS = {HALF: 144, QUARTER: 64, CHUNK: 0}
 
 
 def tile_list_fragment_phase_fields_kernel(
@@ -45,6 +61,7 @@ def tile_list_fragment_phase_fields_kernel(
     nc = tc.nc
     with ExitStack() as ctx:
         keep = ctx.enter_context(tc.tile_pool(name="keep", bufs=1))
+        arena = ctx.enter_context(tc.tile_pool(name="arena", bufs=1))
         ring = ctx.enter_context(tc.tile_pool(name="ring", bufs=2))
         codes = ctx.enter_context(tc.tile_pool(name="codes", bufs=3))
         psum = ctx.enter_context(tc.psum_pool(name="psum", bufs=1))
@@ -58,18 +75,14 @@ def tile_list_fragment_phase_fields_kernel(
         def bank(index):
             return psum.tile([P, HALF], F32, name="bank%d" % index)
 
-        def load_rows(name, matrix, a, reuses=None):
-            raw = held(name, [P, SLOTS, matrix.shape[1]], F32, reuses)
+        def load_rows(raw, matrix, a):
             nc.sync.dma_start(raw[:], matrix[a * PASS : (a + 1) * PASS, :].rearrange("(p t) c -> p t c", t=SLOTS))
             return raw
 
-        def load_words(name, words, reuses=None):
-            sb = held(name, [P, words.shape[1]], I32, reuses)
-            nc.sync.dma_start(sb[:], words.rearrange("p n t -> p (n t)").bitcast(I32))
-            return sb
+        def load_words(sb, words):
+            nc.sync.dma_start(sb, words.rearrange("p n t -> p (n t)").bitcast(I32))
 
-        def load_by_slot(name, vec, reuses):
-            sb = held(name, [P, 2, 2 * SLOTS], F32, reuses)
+        def load_by_slot(sb, vec):
             nc.sync.dma_start(sb[:, :, 0:SLOTS], vec.rearrange("(b p t) -> p b t", b=2, t=SLOTS))
             return sb
 
@@ -88,50 +101,32 @@ def tile_list_fragment_phase_fields_kernel(
         def by_line(flat):
             return flat.rearrange("p (c t i) -> p c t i", t=SLOTS, i=LINE)
 
+        def placed(name, shape, dtype, at):
+            return arena.tile(shape, dtype, name=name, align_bytes=64, offset=at)
+
         idx = held("idx", [P, S // 16], U16)
         idx2 = held("idx2", [P, S2 // 16], U16)
-        tab_rows = held("tab_rows", [P, T], U8)
+        tab_rows = placed("tab_rows", [P, T], U8, AT_ROWS)
         tab2_plane = held("tab2_plane", [P, T2], U8)
-        v_plane = [held("v_plane0", [P, S], U8)]
-        nc.vector.memset(tab_rows[:].bitcast(I32), 0)
-        nc.vector.memset(tab2_plane[:].bitcast(I32), 0)
-        nc.vector.memset(v_plane[0][:].bitcast(I32), 0)
+        v_plane = [held("v_plane%d" % a, [P, S], U8) for a in range(2)]
+        nc.gpsimd.memset(tab2_plane[:].bitcast(I32), 0)
+        nc.vector.memset(tab_rows[64:P, :].bitcast(I32), 0)
+        nc.vector.memset(tab_rows[32:64, :].bitcast(I32), 0)
+        for a in range(2):
+            nc.gpsimd.memset(v_plane[a][:].bitcast(I32), 0)
         identity = held("identity", [P, P], F32)
         make_identity(nc, identity[:])
 
         nc.sync.dma_start(idx[:], offs)
-        wq_raw = [load_rows("wq_raw0", wq, 0)]
-        nc.sync.dma_start(tab_rows[0:P:4, :].bitcast(I32), tab_scales.rearrange("a q t -> (a q) t").bitcast(I32))
+        nc.sync.dma_start(tab_rows[0:32, :].bitcast(I32), tab_scales.rearrange("a q t -> (a q) t").bitcast(I32))
+        tab_sb = [placed("tab_sb0", [P, T], I32, AT_TAB0)]
+        load_words(tab_sb[0][:], tab_words[0])
+        wq_raw = [load_rows(held("wq_raw0", [P, SLOTS, H], F32), wq, 0)]
         nc.sync.dma_start(idx2[:], offs2)
         for r in range(4):
             nc.sync.dma_start(tab2_plane[V2_FIRST_ROW + r : P : 32, :].bitcast(I32), tab2_scales[0, r:16:4, :].bitcast(I32))
-        tab_sb = [load_words("tab_sb0", tab_words[0])]
-        wq_raw.append(load_rows("wq_raw1", wq, 1))
         warm = held("warm", [P, 1], F32)
         nc.scalar.activation(warm[:], identity[:, 0:1], ACT.Sin)
-
-        v_rows = held("v_rows", [P, S], U8)
-        nc.vector.tensor_copy(v_rows[:], tab_rows[:].indirect(idx[:]))
-
-        def place_v_rows(a):
-            for r in range(4):
-                nc.sync.dma_start(
-                    v_plane[a][r:P:32, :].bitcast(I32), v_rows[64 * a + 4 * r : 64 * (a + 1) : 16, :].bitcast(I32)
-                )
-
-        tab2_sb = load_words("tab2_sb", tab2_words[0])
-        place_v_rows(0)
-        v2_plane_listed = held("v2_plane_listed", [P, S2], U8)
-        nc.vector.tensor_copy(v2_plane_listed[:], tab2_plane[:].indirect(idx2[:]))
-        v2_plane = held("v2_plane", [P, S2], U8)
-        nc.vector.tensor_copy(
-            v2_plane[:].rearrange("p (b t c i) -> p b c t i", b=2, t=SLOTS, i=16),
-            v2_plane_listed[:].rearrange("p (b c i t) -> p b c t i", b=2, t=SLOTS, i=16),
-        )
-        tab_sb.append(load_words("tab_sb1", tab_words[1], reuses="tab2_plane"))
-        v_plane.append(held("v_plane1", [P, S], U8, reuses="v2_plane_listed"))
-        nc.vector.memset(v_plane[1][:].bitcast(I32), 0)
-        place_v_rows(1)
 
         wq_words = []
         wq_plane = []
@@ -142,24 +137,28 @@ def tile_list_fragment_phase_fields_kernel(
         h_plane = held("h_plane", [P, S], U8)
         v2_words = {}
 
-        def prepare_wq(a):
-            rounded = held("wq_rounded%d" % a, [P, SLOTS * H], BF16)
-            nc.scalar.copy(
-                rounded[:].rearrange("p (t m j) -> p m t j", t=SLOTS, j=SLOTS),
-                wq_raw[a][:].rearrange("p j (m t) -> p m t j", t=SLOTS),
-            )
+        def place_v_rows(a):
+            for r in range(4):
+                nc.sync.dma_start(v_plane[a][r:P:32, :].bitcast(I32), v_rows[16 * a + r : 16 * (a + 1) : 4, :].bitcast(I32))
+
+        def prepare_wq(a, rounded, vector_share):
+            target = rounded[:].rearrange("p (t m j) -> p m t j", t=SLOTS, j=SLOTS)
+            source = wq_raw[a][:].rearrange("p j (m t) -> p m t j", t=SLOTS)
+            if vector_share:
+                nc.vector.tensor_copy(target[:, 0:vector_share], source[:, 0:vector_share])
+            nc.scalar.copy(target[:, vector_share:P], source[:, vector_share:P])
             words = held("wq_words%d" % a, [P, H], U32)
             plane = held("wq_plane%d" % a, [P, H], U8)
             quantise(words[:], plane[:], rounded[:])
             wq_words.append(words)
             wq_plane.append(plane)
 
-        def gather_v(a, half, reuses=None):
-            v_words[a, half] = held("v_words%d%d" % (a, half), [P, HALF], U32, reuses)
-            nc.vector.tensor_copy(
-                v_words[a, half][:],
-                tab_sb[a][:].bitcast(U32).indirect(idx[:, half * LIST_COLS : (half + 1) * LIST_COLS]),
-            )
+        def gather_v(a, j0, width, at=None):
+            name = "v_words%d_%d" % (a, j0)
+            words = held(name, [P, width], U32) if at is None else placed(name, [P, width], U32, at)
+            nc.vector.tensor_copy(words[:], tab_sb[a][:].bitcast(U32).indirect(idx[:, j0 // 16 : (j0 + width) // 16]))
+            for c0 in range(0, width, QUARTER):
+                v_words[a, (j0 + c0) // QUARTER] = words[:, c0 : c0 + QUARTER]
 
         def h_pass(a, quarter):
             for u in range(2):
@@ -174,7 +173,7 @@ def tile_list_fragment_phase_fields_kernel(
                         out=h_banks[quarter, u][:, k * width : (k + 1) * width],
                         lhsT=wq_words[a][:, t * P : (t + 1) * P].bitcast(FP8X4),
                         lhsT_scale=wq_plane[a][:, t * P : (t + 1) * P],
-                        rhs=v_words[a, j0 // HALF][:, j0 % HALF : j0 % HALF + width].bitcast(FP8X4),
+                        rhs=v_words[a, quarter][:, j0 % QUARTER : j0 % QUARTER + width].bitcast(FP8X4),
                         rhs_scale=v_plane[a][:, j0 : j0 + width],
                         start=(a == 0 and k == 0),
                         stop=(a == 1 and k == len(parts) - 1),
@@ -186,68 +185,74 @@ def tile_list_fragment_phase_fields_kernel(
                 source = h_banks[quarter, t // 2][:, (t % 2) * QUARTER : (t % 2 + 1) * QUARTER]
                 nc.scalar.activation(h_biased[quarter][:, t, :], source, ACT.Identity, bias=bq_sb[:, t : t + 1])
 
-        def h_finish(quarter, reuses=None):
-            woven = held("h_woven%d" % quarter, [P, SLOTS * QUARTER], BF16, reuses)
+        def h_weave(quarter, woven):
             if quarter in SCALAR_QUARTERS:
-                nc.vector.tensor_copy(side_by_side(woven[:], 2 * RUN), by_slot(h_biased[quarter][:], 2 * RUN))
+                nc.vector.tensor_copy(side_by_side(woven, 2 * RUN), by_slot(h_biased[quarter][:], 2 * RUN))
             else:
                 for u in range(2):
                     source = h_banks[quarter, u][:].rearrange("p (t j) -> p t j", t=SLOTS)
                     part = woven[:, SLOTS * u * CHUNK : SLOTS * (u + 1) * CHUNK]
                     nc.vector.tensor_tensor(side_by_side(part), by_slot(source), spread(bq_sb[:], CHUNK), ALU.add)
-            cols = slice(quarter * QUARTER, (quarter + 1) * QUARTER)
-            quantise(h_words[:, cols], h_plane[:, cols], woven[:])
+            return woven
 
-        def gather_v2(b, reuses=None):
-            listed = held("v2_listed%d" % b, [P, PASS], U32, reuses)
-            nc.vector.tensor_copy(listed[:], tab2_sb[:].bitcast(U32).indirect(idx2[:, b * LIST_COLS : (b + 1) * LIST_COLS]))
-            return listed
+        def h_quantise(j0, width, woven):
+            quantise(h_words[:, j0 : j0 + width], h_plane[:, j0 : j0 + width], woven)
 
-        def order_v2(b, listed):
-            v2_words[b] = held("v2_words%d" % b, [P, PASS], U32)
+        def gather_v2(b):
+            v2_words[b] = placed("v2_words%d" % b, [P, PASS], U32, AT_V2 + 2 * 4 * PASS * b)
             nc.vector.tensor_copy(
-                v2_words[b][:].rearrange("p (t c i) -> p c t i", t=SLOTS, i=4),
-                listed[:].rearrange("p (c i t) -> p c t i", t=SLOTS, i=4),
+                v2_words[b][:].rearrange("p (t q) -> p q t", t=SLOTS),
+                tab2_sb[:].bitcast(U32).indirect(idx2[:, b * LIST_COLS : (b + 1) * LIST_COLS]),
             )
 
-        prepare_wq(0)
-        gather_v(0, 0)
-        for quarter in range(2):
-            h_pass(0, quarter)
-        for b in range(2):
-            order_v2(b, gather_v2(b))
-        gather_v(0, 1)
-        for quarter in range(2, 4):
-            h_pass(0, quarter)
-
-        bq_sb = held("bq_sb", [P, SLOTS], F32, reuses="wq_rounded0")
+        v_rows = held("v_rows", [P, S], U8)
+        nc.vector.tensor_copy(v_rows[:], tab_rows[:].indirect(idx[:]))
+        tab2_sb = placed("tab2_sb", [P, T2], I32, AT_TAB2)
+        load_words(tab2_sb[:], tab2_words[0])
+        wq_raw.append(load_rows(placed("wq_raw1", [P, SLOTS, H], F32, AT_WQ1), wq, 1))
+        for half in range(2):
+            gather_v(0, half * HALF, HALF)
+        tab_sb.append(placed("tab_sb1", [P, T], I32, AT_TAB0))
+        load_words(tab_sb[1][:, 0:TAB1_CUT], tab_words[1][:, 0:TAB1_CUT])
+        place_v_rows(0)
+        load_words(tab_sb[1][:, TAB1_CUT:T], tab_words[1][:, TAB1_CUT:T])
+        place_v_rows(1)
+        v2_plane = held("v2_plane", [P, S2], U8)
+        nc.vector.tensor_copy(v2_plane[:].rearrange("p (b t q) -> p b q t", b=2, t=SLOTS), tab2_plane[:].indirect(idx2[:]))
+        prepare_wq(0, placed("wq_rounded0", [P, SLOTS * H], BF16, AT_ROUNDED0), 0)
+        bq_sb = placed("bq_sb", [P, SLOTS], F32, AT_ROUNDED0)
         nc.sync.dma_start(bq_sb[:], bq.rearrange("(p t) -> p t", t=SLOTS))
-        phi_sb = load_by_slot("phi_sb", phi, reuses="v_rows")
-        mcos_raw = [load_rows("mcos_raw0", mcos, 0, reuses="tab2_sb"), load_rows("mcos_raw1", mcos, 1, reuses="tab_sb0")]
-        prepare_wq(1)
-        gain_rows = wq_raw[1][:, 0, :]
+        phi_sb = load_by_slot(placed("phi_sb", [P, 2, 2 * SLOTS], F32, AT_ROUNDED0 + 64), phi)
+        gain_rows = wq_raw[0][:, 0, :]
         for vec, row in ((gsin, GSIN_ROW), (gcos, GCOS_ROW)):
             nc.sync.dma_start(gain_rows[row : row + 2, :], vec.rearrange("(b m) -> b m", b=2))
-        m4_sb = held("m4_sb", [P, 2 * 2 * N], U8, reuses="v2_listed1")
+        for b in range(2):
+            gather_v2(b)
+        mcos_raw = [load_rows(placed("mcos_raw%d" % b, [P, SLOTS, N], F32, at), mcos, b) for b, at in enumerate((AT_MCOS0, AT_MCOS1))]
+        prepare_wq(1, placed("wq_rounded1", [P, SLOTS * H], BF16, AT_ROUNDED1), 0)
+        m4_sb = placed("m4_sb", [P, 2 * 2 * N], U8, AT_ROUNDED1)
         nc.sync.dma_start(
             m4_sb[:].bitcast(I32).rearrange("p (b c) -> p b c", b=2), m4_words.bitcast(I32).rearrange("b p c -> p b c")
         )
-        m4_plane = held("m4_plane", [P, 2 * N], U8, reuses="wq_rounded1")
+        m4_plane = placed("m4_plane", [P, 2 * N], U8, AT_ROUNDED1 + 4 * N)
         nc.gpsimd.memset(m4_plane[:].bitcast(I32), 0)
         for q in range(QUADS):
             nc.sync.dma_start(
                 m4_plane[32 * q : 32 * q + 4, :].bitcast(I32).rearrange("p (b c) -> p b c", b=2),
                 m4_scales[:, 4 * q : 4 * q + 4, :].bitcast(I32).rearrange("b r c -> r b c"),
             )
-
-        for half in range(2):
-            gather_v(1, half)
-        for quarter in range(3):
+        for quarter in range(4):
+            h_pass(0, quarter)
+        for quarter in range(2):
+            gather_v(1, quarter * QUARTER, QUARTER)
             h_pass(1, quarter)
         for quarter in SCALAR_QUARTERS:
             h_bias(quarter)
-        for quarter in range(2):
-            h_finish(quarter)
+        first_woven = h_weave(0, placed("h_woven0", [P, SLOTS * QUARTER], BF16, AT_FIRST)[:])
+        for u in range(2):
+            h_quantise(u * CHUNK, CHUNK, first_woven[:, u * SLOTS * CHUNK : (u + 1) * SLOTS * CHUNK])
+        gather_v(1, HALF, HALF, AT_FIRST)
+        h_quantise(QUARTER, QUARTER, h_weave(1, held("h_woven1", [P, SLOTS * QUARTER], BF16)[:]))
 
         units = [(0, QUARTER, 0), (QUARTER, QUARTER, 0), (0, HALF, 1)]
         units.extend([(HALF, HALF, 0), (HALF, QUARTER, 1), (HALF + QUARTER, QUARTER, 1)])
@@ -260,8 +265,8 @@ def tile_list_fragment_phase_fields_kernel(
             j0, width, b = unit
             last = unit == units[-1]
             sine = turn("sine", [P, SLOTS * width], F32, bufs=3)
-            if unit == units[3]:
-                size = held("late_size", [P, SLOTS * width], F32, reuses="wq_raw0")
+            if last:
+                size = placed("late_size", [P, SLOTS * width], F32, AT_WQ1 + 1024)
             else:
                 size = turn("size", [P, SLOTS * width], F32, bufs=2)
             per_bank = HALF // width
@@ -300,24 +305,32 @@ def tile_list_fragment_phase_fields_kernel(
                     )
                 cosines[unit].append((c0, step, piece))
 
-        def operand(name, woven, width):
+        def operand(name, woven, width, words=None):
             return (
-                woven[:, 0 : SLOTS * width],
-                codes.tile([P, width], U32, name=name + "_words", align_bytes=64),
+                woven,
+                codes.tile([P, width], U32, name=name + "_words", align_bytes=64) if words is None else words,
                 codes.tile([P, width], U8, name=name + "_plane", align_bytes=64),
             )
 
-        def gain(tiles, values, row, c0, width, extra=0):
-            split = width - GPSIMD_COLS[width] - extra
-            for engine, gains, k0, k1 in ((nc.vector, gains_psum, 0, split), (nc.gpsimd, gains_sbuf, split, width)):
-                if k1 > k0:
-                    part = tiles[0][:, SLOTS * (c0 + k0) : SLOTS * (c0 + k1)]
-                    engine.tensor_tensor(
-                        part.rearrange("p (c i t) -> p c t i", i=LINE, t=SLOTS),
-                        by_line(values[:, SLOTS * k0 : SLOTS * k1]),
-                        spread(gains[:, :, row], k1 - k0, LINE),
-                        ALU.mult,
-                    )
+        def gain(tiles, values, row, c0, width, share, gpsimd_first):
+            part = tiles[0][:, SLOTS * c0 : SLOTS * (c0 + width)]
+            cut = SLOTS * (share if gpsimd_first else width - share)
+            low, high = slice(0, cut), slice(cut, SLOTS * width)
+            mine, other = (high, low) if gpsimd_first else (low, high)
+            if share < width:
+                nc.vector.tensor_tensor(
+                    part[:, mine].rearrange("p (c i t) -> p c t i", i=LINE, t=SLOTS),
+                    by_line(values[:, mine]),
+                    spread(gains_psum[:, :, row], width - share, LINE),
+                    ALU.mult,
+                )
+            if share > 0:
+                nc.gpsimd.tensor_tensor(
+                    part[:, other].rearrange("p (a c i t) -> p a c t i", c=GROUPS, i=LINE, t=SLOTS),
+                    values[:, other].rearrange("p (a c t i) -> p a c t i", c=GROUPS, t=SLOTS, i=LINE),
+                    gains_sbuf[:, row].unsqueeze(1).to_broadcast([P, share // (GROUPS * LINE), GROUPS, SLOTS, LINE]),
+                    ALU.mult,
+                )
 
         def quantise_part(tiles, c0, width):
             woven, words, plane = tiles
@@ -356,23 +369,23 @@ def tile_list_fragment_phase_fields_kernel(
                         stop=stop,
                     )
                     if stop and j0 < HALF:
-                        if n < VECTOR_RESULTS:
-                            result = held("rows%d" % n, [P, HALF], F32)
-                            nc.vector.tensor_copy(result[:], out_banks[key][:])
-                        else:
-                            result = held("rows%d" % n, [P, HALF], F32, reuses="wq_raw0")
-                            nc.scalar.copy(result[:], out_banks[key][:])
+                        result = held("rows%d" % n, [P, HALF], F32)
+                        nc.vector.tensor_copy(result[:], out_banks[key][:])
                         nc.sync.dma_start(out_rows[:, n, 0:HALF], result[:])
                     elif stop:
-                        result = held("result%d" % chunk, [P, N // P, CHUNK], F32)
+                        result = placed("result%d" % chunk, [P, N // P, CHUNK], F32, AT_WQ1 + 4 * N * (chunk % 4))
                         nc.scalar.copy(result[:], out_banks[key][:, 0:N].rearrange("p (n j) -> p n j", j=CHUNK))
                         nc.sync.dma_start(out_rows[:, :, chunk * CHUNK : (chunk + 1) * CHUNK], result[:])
 
         phases(units[0])
-        h_pass(1, 3)
-        h_finish(3)
-        h_finish(2)
-        mcos_rounded = held("mcos_rounded", [P, 2 * SLOTS * N], BF16, reuses="woven")
+        for quarter in (2, 3):
+            h_pass(1, quarter)
+        late_woven = held("h_woven2", [P, SLOTS * HALF], BF16)
+        for quarter in (2, 3):
+            h_weave(quarter, late_woven[:, (quarter - 2) * SLOTS * QUARTER : (quarter - 1) * SLOTS * QUARTER])
+        h_quantise(HALF, HALF, late_woven[:])
+        woven = placed("woven", [P, WOVEN], BF16, AT_WOVEN)
+        mcos_rounded = woven[:, 0 : 2 * SLOTS * N]
         mcos_words = held("mcos_words", [P, 2 * N], U32)
         mcos_plane = held("mcos_plane", [P, 2 * N], U8)
         for b in range(2):
@@ -384,28 +397,35 @@ def tile_list_fragment_phase_fields_kernel(
         for t in range(SLOTS):
             nc.tensor.transpose(gain_bank[:, t * P : (t + 1) * P], gain_rows[:, t:PASS:SLOTS], identity[:])
         gains_psum = gain_bank[:].rearrange("p (t r) -> p t r", t=SLOTS)
-        gains_sbuf = held("gains_sbuf", [P, GAIN_ROWS, SLOTS], F32)[:].rearrange("p r t -> p t r")
-        nc.vector.tensor_copy(gains_sbuf, gains_psum[:, :, 0:GAIN_ROWS])
+        gains_sbuf = held("gains_sbuf", [P, GAIN_ROWS, GROUPS, SLOTS, LINE], F32)
+        by_row = gains_psum[:, :, 0:GAIN_ROWS].rearrange("p t r -> p r t").unsqueeze(2).unsqueeze(4)
+        nc.vector.tensor_copy(gains_sbuf[:], by_row.to_broadcast([P, GAIN_ROWS, GROUPS, SLOTS, LINE]))
+        late_words = {
+            ("x", 1): placed("x1_words", [P, QUARTER], U32, AT_V2),
+            ("y", 2): placed("y2_words", [P, HALF], U32, AT_V2 + 4 * QUARTER),
+            ("x", 2): h_words[:, QUARTER : QUARTER + HALF],
+        }
         waiting = []
-        woven = held("woven", [P, 2 * SLOTS * HALF], BF16)
+        y_end = 2 * SLOTS * N
         for g, unit in enumerate(units):
             width, b = unit[1], unit[2]
-            if unit[0] == HALF and b == 0:
-                mix(*waiting[0])
-                waiting = []
-                woven = held("woven", [P, 2 * SLOTS * HALF], BF16)
             if g + 1 < len(units):
                 phases(units[g + 1])
-            y_tiles = operand("y", woven[:, SLOTS * HALF :], width)
-            gain(y_tiles, sines[unit][:], GSIN_ROW + b, 0, width, GPSIMD_EXTRA if g == 3 else 0)
+            y_tiles = operand("y", woven[:, y_end - LAP : y_end - LAP + SLOTS * width], width, late_words.get(("y", g)))
+            gain(y_tiles, sines[unit][:], GSIN_ROW + b, 0, width, GPSIMD_COLS[width], True)
             for args in waiting:
                 mix(*args)
             waiting = []
             mix(unit, y_tiles, 0, width, True)
-            woven = held("woven" if g + 1 < len(units) else "last_woven", [P, 2 * SLOTS * HALF], BF16)
-            x_tiles = operand("x", woven, width)
+            y_end = y_end - LAP + SLOTS * width
+            if g + 1 < len(units):
+                x_end = y_end - SLOTS * width + LAP
+                x_woven = woven[:, x_end - SLOTS * width : x_end]
+            else:
+                x_woven = held("last_woven", [P, SLOTS * width], BF16)[:]
+            x_tiles = operand("x", x_woven, width, late_words.get(("x", g)))
             for c0, step, piece in cosines[unit]:
-                gain(x_tiles, piece, GCOS_ROW + b, c0, step)
+                gain(x_tiles, piece, GCOS_ROW + b, c0, step, GPSIMD_COLS[step], False)
                 if step == width:
                     waiting.append((unit, x_tiles, c0, step, False))
                 else:

@@ -51,6 +51,11 @@ AT_WQ1 = AT_PLANE1 + S
 AT_ROUNDED0 = AT_WQ1 + 4 * SLOTS * H
 AT_ROUNDED1 = AT_ROUNDED0 + 2 * SLOTS * H
 AT_V2 = AT_ROUNDED1 + 2 * SLOTS * H
+AT_SECOND = AT_V2 + 4 * 4 * PASS
+AT_HALVES = AT_SECOND + 4 * SLOTS * QUARTER
+HALF_ANGLE = (0,)
+TWICE_ROW = 32
+Y_SHARES = (64, 128, 144, 144, 64, 64)
 TAB1_CUT = T // 4
 GPSIMD_COLS = {HALF: 144, QUARTER: 64, CHUNK: 0}
 
@@ -226,6 +231,11 @@ def tile_list_fragment_phase_fields_kernel(
         gain_rows = wq_raw[0][:, 0, :]
         for vec, row in ((gsin, GSIN_ROW), (gcos, GCOS_ROW)):
             nc.sync.dma_start(gain_rows[row : row + 2, :], vec.rearrange("(b m) -> b m", b=2))
+        twice = gain_rows[TWICE_ROW : TWICE_ROW + 1, :]
+        nc.sync.dma_start(twice, gcos[0:PASS].rearrange("(b m) -> b m", b=1))
+        nc.scalar.activation(twice, twice, ACT.Copy, scale=-2.0)
+        half_phi = held("half_phi", [P, SLOTS], F32)
+        nc.scalar.activation(half_phi[:], phi_sb[:, 0, 0:SLOTS], ACT.Copy, scale=0.5)
         for b in range(2):
             gather_v2(b)
         mcos_raw = [load_rows(placed("mcos_raw%d" % b, [P, SLOTS, N], F32, at), mcos, b) for b, at in enumerate((AT_MCOS0, AT_MCOS1))]
@@ -252,12 +262,14 @@ def tile_list_fragment_phase_fields_kernel(
         for u in range(2):
             h_quantise(u * CHUNK, CHUNK, first_woven[:, u * SLOTS * CHUNK : (u + 1) * SLOTS * CHUNK])
         gather_v(1, HALF, HALF, AT_FIRST)
-        h_quantise(QUARTER, QUARTER, h_weave(1, held("h_woven1", [P, SLOTS * QUARTER], BF16)[:]))
+        h_quantise(QUARTER, QUARTER, h_weave(1, placed("h_woven1", [P, SLOTS * QUARTER], BF16, AT_SECOND)[:]))
 
         units = [(0, QUARTER, 0), (QUARTER, QUARTER, 0), (0, HALF, 1)]
         units.extend([(HALF, HALF, 0), (HALF, QUARTER, 1), (HALF + QUARTER, QUARTER, 1)])
         sines = {}
         cosines = {}
+        halves = {}
+        squares = {}
         out_banks = {}
         e_banks = []
 
@@ -265,7 +277,10 @@ def tile_list_fragment_phase_fields_kernel(
             j0, width, b = unit
             last = unit == units[-1]
             sine = turn("sine", [P, SLOTS * width], F32, bufs=3)
-            if last:
+            halved = units.index(unit) in HALF_ANGLE
+            if halved:
+                size = placed("halves%d" % j0, [P, SLOTS * width], F32, AT_HALVES + 4 * SLOTS * j0)
+            elif last:
                 size = placed("late_size", [P, SLOTS * width], F32, AT_WQ1 + 1024)
             else:
                 size = turn("size", [P, SLOTS * width], F32, bufs=2)
@@ -287,12 +302,20 @@ def tile_list_fragment_phase_fields_kernel(
                         stop=True,
                     )
                 for t in range(t0, t0 + per_bank):
-                    nc.scalar.activation(by_line(sine[:])[:, :, t, :], sums[t], ACT.Sin, bias=phi_sb[:, b, t : t + 1])
+                    if halved:
+                        nc.scalar.activation(by_line(size[:])[:, :, t, :], sums[t], ACT.Sin, bias=half_phi[:, t : t + 1], scale=0.5)
+                    else:
+                        nc.scalar.activation(by_line(sine[:])[:, :, t, :], sums[t], ACT.Sin, bias=phi_sb[:, b, t : t + 1])
                     if t < early:
                         nc.scalar.activation(by_line(size[:])[:, :, t, :], sums[t], ACT.Abs, bias=phi_sb[:, b, t : t + 1])
+            sines[unit] = sine
+            if halved:
+                for t in range(SLOTS):
+                    nc.scalar.activation(by_line(sine[:])[:, :, t, :], sums[t], ACT.Sin, bias=phi_sb[:, b, t : t + 1])
+                halves[unit] = size
+                return
             for t in range(early, SLOTS):
                 nc.scalar.activation(by_line(size[:])[:, :, t, :], sums[t], ACT.Abs, bias=phi_sb[:, b, t : t + 1])
-            sines[unit] = sine
             step = CHUNK if last else width
             cosine = turn("cosine", [P, SLOTS * width], F32, bufs=3)
             cosines[unit] = []
@@ -304,6 +327,11 @@ def tile_list_fragment_phase_fields_kernel(
                         by_line(piece)[:, :, t0:t1, :], by_line(source)[:, :, t0:t1, :], ACT.Sin, bias=math.pi / 2, scale=-1.0
                     )
                 cosines[unit].append((c0, step, piece))
+
+        def square(unit, target):
+            source = by_line(halves[unit][:])
+            nc.gpsimd.tensor_tensor(target.rearrange("p (c i t) -> p c t i", i=LINE, t=SLOTS), source, source, ALU.mult)
+            squares[unit] = target
 
         def operand(name, woven, width, words=None):
             return (
@@ -378,6 +406,7 @@ def tile_list_fragment_phase_fields_kernel(
                         nc.sync.dma_start(out_rows[:, :, chunk * CHUNK : (chunk + 1) * CHUNK], result[:])
 
         phases(units[0])
+        square(units[0], placed("squares0", [P, SLOTS * QUARTER], F32, AT_SECOND)[:])
         for quarter in (2, 3):
             h_pass(1, quarter)
         late_woven = held("h_woven2", [P, SLOTS * HALF], BF16)
@@ -412,7 +441,7 @@ def tile_list_fragment_phase_fields_kernel(
             if g + 1 < len(units):
                 phases(units[g + 1])
             y_tiles = operand("y", woven[:, y_end - LAP : y_end - LAP + SLOTS * width], width, late_words.get(("y", g)))
-            gain(y_tiles, sines[unit][:], GSIN_ROW + b, 0, width, GPSIMD_COLS[width], True)
+            gain(y_tiles, sines[unit][:], GSIN_ROW + b, 0, width, Y_SHARES[g], True)
             for args in waiting:
                 mix(*args)
             waiting = []
@@ -424,7 +453,17 @@ def tile_list_fragment_phase_fields_kernel(
             else:
                 x_woven = held("last_woven", [P, SLOTS * width], BF16)[:]
             x_tiles = operand("x", x_woven, width, late_words.get(("x", g)))
-            for c0, step, piece in cosines[unit]:
+            if unit in squares:
+                nc.vector.scalar_tensor_tensor(
+                    x_woven.rearrange("p (c t) -> p c t", t=SLOTS),
+                    squares[unit].rearrange("p (c t) -> p c t", t=SLOTS),
+                    -0.5,
+                    gains_psum[:, :, TWICE_ROW].unsqueeze(1).to_broadcast([P, width, SLOTS]),
+                    ALU.add,
+                    ALU.mult,
+                )
+                waiting.append((unit, x_tiles, 0, width, False))
+            for c0, step, piece in cosines.get(unit, ()):
                 gain(x_tiles, piece, GCOS_ROW + b, c0, step, GPSIMD_COLS[step], False)
                 if step == width:
                     waiting.append((unit, x_tiles, c0, step, False))

@@ -56,6 +56,7 @@ AT_HALVES = AT_SECOND + 4 * SLOTS * QUARTER
 HALF_ANGLE = (0,)
 TWICE_ROW = 32
 Y_SHARES = (64, 128, 144, 144, 64, 64)
+VECTOR_RESULTS = 1
 TAB1_CUT = T // 4
 GPSIMD_COLS = {HALF: 144, QUARTER: 64, CHUNK: 0}
 
@@ -280,6 +281,8 @@ def tile_list_fragment_phase_fields_kernel(
             halved = units.index(unit) in HALF_ANGLE
             if halved:
                 size = placed("halves%d" % j0, [P, SLOTS * width], F32, AT_HALVES + 4 * SLOTS * j0)
+            elif unit == units[4]:
+                size = placed("held_size", [P, SLOTS * width], F32, AT_TAB0 + 4 * HALF)
             elif last:
                 size = placed("late_size", [P, SLOTS * width], F32, AT_WQ1 + 1024)
             else:
@@ -397,8 +400,12 @@ def tile_list_fragment_phase_fields_kernel(
                         stop=stop,
                     )
                     if stop and j0 < HALF:
-                        result = held("rows%d" % n, [P, HALF], F32)
-                        nc.vector.tensor_copy(result[:], out_banks[key][:])
+                        if n < VECTOR_RESULTS:
+                            result = held("rows%d" % n, [P, HALF], F32)
+                            nc.vector.tensor_copy(result[:], out_banks[key][:])
+                        else:
+                            result = placed("rows%d" % n, [P, HALF], F32, AT_TAB0 + 4 * HALF * n)
+                            nc.scalar.copy(result[:], out_banks[key][:])
                         nc.sync.dma_start(out_rows[:, n, 0:HALF], result[:])
                     elif stop:
                         result = placed("result%d" % chunk, [P, N // P, CHUNK], F32, AT_WQ1 + 4 * N * (chunk % 4))

@@ -56,7 +56,7 @@ AT_HALVES = AT_SECOND + 4 * SLOTS * QUARTER
 HALF_ANGLE = (0,)
 TWICE_ROW = 32
 Y_SHARES = (64, 128, 144, 144, 64, 64)
-VECTOR_RESULTS = 1
+VECTOR_RESULTS = 2
 TAB1_CUT = T // 4
 GPSIMD_COLS = {HALF: 144, QUARTER: 64, CHUNK: 0}
 
@@ -129,6 +129,8 @@ def tile_list_fragment_phase_fields_kernel(
         load_words(tab_sb[0][:], tab_words[0])
         wq_raw = [load_rows(held("wq_raw0", [P, SLOTS, H], F32), wq, 0)]
         nc.sync.dma_start(idx2[:], offs2)
+        bq_sb = held("bq_sb", [P, SLOTS], F32)
+        nc.sync.dma_start(bq_sb[:], bq.rearrange("(p t) -> p t", t=SLOTS))
         for r in range(4):
             nc.sync.dma_start(tab2_plane[V2_FIRST_ROW + r : P : 32, :].bitcast(I32), tab2_scales[0, r:16:4, :].bitcast(I32))
         warm = held("warm", [P, 1], F32)
@@ -226,15 +228,13 @@ def tile_list_fragment_phase_fields_kernel(
         v2_plane = held("v2_plane", [P, S2], U8)
         nc.vector.tensor_copy(v2_plane[:].rearrange("p (b t q) -> p b q t", b=2, t=SLOTS), tab2_plane[:].indirect(idx2[:]))
         prepare_wq(0, placed("wq_rounded0", [P, SLOTS * H], BF16, AT_ROUNDED0), 0)
-        bq_sb = placed("bq_sb", [P, SLOTS], F32, AT_ROUNDED0)
-        nc.sync.dma_start(bq_sb[:], bq.rearrange("(p t) -> p t", t=SLOTS))
-        phi_sb = load_by_slot(placed("phi_sb", [P, 2, 2 * SLOTS], F32, AT_ROUNDED0 + 64), phi)
         gain_rows = wq_raw[0][:, 0, :]
-        for vec, row in ((gsin, GSIN_ROW), (gcos, GCOS_ROW)):
-            nc.sync.dma_start(gain_rows[row : row + 2, :], vec.rearrange("(b m) -> b m", b=2))
         twice = gain_rows[TWICE_ROW : TWICE_ROW + 1, :]
         nc.sync.dma_start(twice, gcos[0:PASS].rearrange("(b m) -> b m", b=1))
         nc.scalar.activation(twice, twice, ACT.Copy, scale=-2.0)
+        phi_sb = load_by_slot(placed("phi_sb", [P, 2, 2 * SLOTS], F32, AT_ROUNDED0 + 64), phi)
+        for vec, row in ((gsin, GSIN_ROW), (gcos, GCOS_ROW)):
+            nc.sync.dma_start(gain_rows[row : row + 2, :], vec.rearrange("(b m) -> b m", b=2))
         half_phi = held("half_phi", [P, SLOTS], F32)
         nc.scalar.activation(half_phi[:], phi_sb[:, 0, 0:SLOTS], ACT.Copy, scale=0.5)
         for b in range(2):
@@ -419,6 +419,15 @@ def tile_list_fragment_phase_fields_kernel(
         late_woven = held("h_woven2", [P, SLOTS * HALF], BF16)
         for quarter in (2, 3):
             h_weave(quarter, late_woven[:, (quarter - 2) * SLOTS * QUARTER : (quarter - 1) * SLOTS * QUARTER])
+        gain_bank = bank(GAIN_BANK)
+        for t in range(SLOTS):
+            nc.tensor.transpose(gain_bank[:, t * P : (t + 1) * P], gain_rows[:, t:PASS:SLOTS], identity[:])
+        gains_psum = gain_bank[:].rearrange("p (t r) -> p t r", t=SLOTS)
+        gains_sbuf = held("gains_sbuf", [P, GAIN_ROWS, GROUPS, SLOTS, LINE], F32)
+        by_row = gains_psum[:, :, 0:GAIN_ROWS].rearrange("p t r -> p r t").unsqueeze(2).unsqueeze(4)
+        nc.vector.tensor_copy(gains_sbuf[:], by_row.to_broadcast([P, GAIN_ROWS, GROUPS, SLOTS, LINE]))
+        first_y = operand("y", held("first_y", [P, SLOTS * QUARTER], BF16)[:], QUARTER)
+        gain(first_y, sines[units[0]][:], GSIN_ROW, 0, QUARTER, Y_SHARES[0], True)
         h_quantise(HALF, HALF, late_woven[:])
         woven = placed("woven", [P, WOVEN], BF16, AT_WOVEN)
         mcos_rounded = woven[:, 0 : 2 * SLOTS * N]
@@ -429,13 +438,6 @@ def tile_list_fragment_phase_fields_kernel(
         for c0, c1 in ((0, N), (N, 2 * N)):
             quantise(mcos_words[:, c0:c1], mcos_plane[:, c0:c1], mcos_rounded[:, SLOTS * c0 : SLOTS * c1])
 
-        gain_bank = bank(GAIN_BANK)
-        for t in range(SLOTS):
-            nc.tensor.transpose(gain_bank[:, t * P : (t + 1) * P], gain_rows[:, t:PASS:SLOTS], identity[:])
-        gains_psum = gain_bank[:].rearrange("p (t r) -> p t r", t=SLOTS)
-        gains_sbuf = held("gains_sbuf", [P, GAIN_ROWS, GROUPS, SLOTS, LINE], F32)
-        by_row = gains_psum[:, :, 0:GAIN_ROWS].rearrange("p t r -> p r t").unsqueeze(2).unsqueeze(4)
-        nc.vector.tensor_copy(gains_sbuf[:], by_row.to_broadcast([P, GAIN_ROWS, GROUPS, SLOTS, LINE]))
         late_words = {
             ("x", 1): placed("x1_words", [P, QUARTER], U32, AT_V2),
             ("y", 2): placed("y2_words", [P, HALF], U32, AT_V2 + 4 * QUARTER),
@@ -447,18 +449,21 @@ def tile_list_fragment_phase_fields_kernel(
             width, b = unit[1], unit[2]
             if g + 1 < len(units):
                 phases(units[g + 1])
-            y_tiles = operand("y", woven[:, y_end - LAP : y_end - LAP + SLOTS * width], width, late_words.get(("y", g)))
-            gain(y_tiles, sines[unit][:], GSIN_ROW + b, 0, width, Y_SHARES[g], True)
+            if g == 0:
+                y_tiles = first_y
+            else:
+                y_tiles = operand("y", woven[:, y_end - LAP : y_end - LAP + SLOTS * width], width, late_words.get(("y", g)))
+                gain(y_tiles, sines[unit][:], GSIN_ROW + b, 0, width, Y_SHARES[g], True)
+                y_end = y_end - LAP + SLOTS * width
             for args in waiting:
                 mix(*args)
             waiting = []
             mix(unit, y_tiles, 0, width, True)
-            y_end = y_end - LAP + SLOTS * width
-            if g + 1 < len(units):
+            if 0 < g < len(units) - 1:
                 x_end = y_end - SLOTS * width + LAP
                 x_woven = woven[:, x_end - SLOTS * width : x_end]
             else:
-                x_woven = held("last_woven", [P, SLOTS * width], BF16)[:]
+                x_woven = held("x_woven%d" % g, [P, SLOTS * width], BF16)[:]
             x_tiles = operand("x", x_woven, width, late_words.get(("x", g)))
             if unit in squares:
                 nc.vector.scalar_tensor_tensor(

@@ -55,10 +55,10 @@ AT_SECOND = AT_V2 + 4 * 4 * PASS
 AT_HALVES = AT_SECOND + 4 * SLOTS * QUARTER
 HALF_ANGLE = (0,)
 TWICE_ROW = 32
-Y_SHARES = (64, 128, 144, 144, 64, 64)
+Y_SHARES = (48, 128, 128, 128, 48, 64)
 VECTOR_RESULTS = 2
 TAB1_CUT = T // 4
-GPSIMD_COLS = {HALF: 144, QUARTER: 64, CHUNK: 0}
+GPSIMD_COLS = {HALF: 128, QUARTER: 64, CHUNK: 0}
 
 
 def tile_list_fragment_phase_fields_kernel(
@@ -124,15 +124,15 @@ def tile_list_fragment_phase_fields_kernel(
         make_identity(nc, identity[:])
 
         nc.sync.dma_start(idx[:], offs)
-        nc.sync.dma_start(tab_rows[0:32, :].bitcast(I32), tab_scales.rearrange("a q t -> (a q) t").bitcast(I32))
+        nc.scalar.dma_start(tab_rows[0:32, :].bitcast(I32), tab_scales.rearrange("a q t -> (a q) t").bitcast(I32))
         tab_sb = [placed("tab_sb0", [P, T], I32, AT_TAB0)]
         load_words(tab_sb[0][:], tab_words[0])
         wq_raw = [load_rows(held("wq_raw0", [P, SLOTS, H], F32), wq, 0)]
         nc.sync.dma_start(idx2[:], offs2)
         bq_sb = held("bq_sb", [P, SLOTS], F32)
-        nc.sync.dma_start(bq_sb[:], bq.rearrange("(p t) -> p t", t=SLOTS))
+        nc.scalar.dma_start(bq_sb[:], bq.rearrange("(p t) -> p t", t=SLOTS))
         for r in range(4):
-            nc.sync.dma_start(tab2_plane[V2_FIRST_ROW + r : P : 32, :].bitcast(I32), tab2_scales[0, r:16:4, :].bitcast(I32))
+            nc.scalar.dma_start(tab2_plane[V2_FIRST_ROW + r : P : 32, :].bitcast(I32), tab2_scales[0, r:16:4, :].bitcast(I32))
         warm = held("warm", [P, 1], F32)
         nc.scalar.activation(warm[:], identity[:, 0:1], ACT.Sin)
 

@@ -56,9 +56,8 @@ AT_HALVES = AT_SECOND + 4 * SLOTS * QUARTER
 HALF_ANGLE = (0,)
 TWICE_ROW = 32
 Y_SHARES = (48, 128, 128, 128, 48, 64)
-VECTOR_RESULTS = 2
-TAB1_CUT = T // 4
-GPSIMD_COLS = {HALF: 128, QUARTER: 64, CHUNK: 0}
+VECTOR_RESULTS = 3
+X_SHARES = (0, 64, 128, 192, 64, 0)
 
 
 def tile_list_fragment_phase_fields_kernel(
@@ -145,9 +144,9 @@ def tile_list_fragment_phase_fields_kernel(
         h_plane = held("h_plane", [P, S], U8)
         v2_words = {}
 
-        def place_v_rows(a):
+        def place_v_rows(a, queue):
             for r in range(4):
-                nc.sync.dma_start(v_plane[a][r:P:32, :].bitcast(I32), v_rows[16 * a + r : 16 * (a + 1) : 4, :].bitcast(I32))
+                queue.dma_start(v_plane[a][r:P:32, :].bitcast(I32), v_rows[16 * a + r : 16 * (a + 1) : 4, :].bitcast(I32))
 
         def prepare_wq(a, rounded, vector_share):
             target = rounded[:].rearrange("p (t m j) -> p m t j", t=SLOTS, j=SLOTS)
@@ -156,7 +155,7 @@ def tile_list_fragment_phase_fields_kernel(
                 nc.vector.tensor_copy(target[:, 0:vector_share], source[:, 0:vector_share])
             nc.scalar.copy(target[:, vector_share:P], source[:, vector_share:P])
             words = held("wq_words%d" % a, [P, H], U32)
-            plane = held("wq_plane%d" % a, [P, H], U8)
+            plane = placed("wq_plane%d" % a, [P, H], U8, AT_MCOS1 + 4 * SLOTS * N + H * a)
             quantise(words[:], plane[:], rounded[:])
             wq_words.append(words)
             wq_plane.append(plane)
@@ -218,15 +217,16 @@ def tile_list_fragment_phase_fields_kernel(
         tab2_sb = placed("tab2_sb", [P, T2], I32, AT_TAB2)
         load_words(tab2_sb[:], tab2_words[0])
         wq_raw.append(load_rows(placed("wq_raw1", [P, SLOTS, H], F32, AT_WQ1), wq, 1))
+        place_v_rows(0, nc.scalar)
         for half in range(2):
             gather_v(0, half * HALF, HALF)
         tab_sb.append(placed("tab_sb1", [P, T], I32, AT_TAB0))
-        load_words(tab_sb[1][:, 0:TAB1_CUT], tab_words[1][:, 0:TAB1_CUT])
-        place_v_rows(0)
-        load_words(tab_sb[1][:, TAB1_CUT:T], tab_words[1][:, TAB1_CUT:T])
-        place_v_rows(1)
+        load_words(tab_sb[1][:], tab_words[1])
+        place_v_rows(1, nc.sync)
         v2_plane = held("v2_plane", [P, S2], U8)
         nc.vector.tensor_copy(v2_plane[:].rearrange("p (b t q) -> p b q t", b=2, t=SLOTS), tab2_plane[:].indirect(idx2[:]))
+        for b in range(2):
+            gather_v2(b)
         prepare_wq(0, placed("wq_rounded0", [P, SLOTS * H], BF16, AT_ROUNDED0), 0)
         gain_rows = wq_raw[0][:, 0, :]
         twice = gain_rows[TWICE_ROW : TWICE_ROW + 1, :]
@@ -237,8 +237,6 @@ def tile_list_fragment_phase_fields_kernel(
             nc.sync.dma_start(gain_rows[row : row + 2, :], vec.rearrange("(b m) -> b m", b=2))
         half_phi = held("half_phi", [P, SLOTS], F32)
         nc.scalar.activation(half_phi[:], phi_sb[:, 0, 0:SLOTS], ACT.Copy, scale=0.5)
-        for b in range(2):
-            gather_v2(b)
         mcos_raw = [load_rows(placed("mcos_raw%d" % b, [P, SLOTS, N], F32, at), mcos, b) for b, at in enumerate((AT_MCOS0, AT_MCOS1))]
         prepare_wq(1, placed("wq_rounded1", [P, SLOTS * H], BF16, AT_ROUNDED1), 0)
         m4_sb = placed("m4_sb", [P, 2 * 2 * N], U8, AT_ROUNDED1)
@@ -476,7 +474,7 @@ def tile_list_fragment_phase_fields_kernel(
                 )
                 waiting.append((unit, x_tiles, 0, width, False))
             for c0, step, piece in cosines.get(unit, ()):
-                gain(x_tiles, piece, GCOS_ROW + b, c0, step, GPSIMD_COLS[step], False)
+                gain(x_tiles, piece, GCOS_ROW + b, c0, step, X_SHARES[g], False)
                 if step == width:
                     waiting.append((unit, x_tiles, c0, step, False))
                 else:

@@ -23,41 +23,45 @@ SLOTS = 4
 PASS = P * SLOTS
 QUADS = 4
 HALF = 512
-CHUNK = 128
-LIST_COLS = 512 // 16
 QUARTER = HALF // 2
-GROUPS = 4
-LAP = 32
+CHUNK = 128
+LIST_ROWS = 16
 LINE = 4
 RUN = 2
+GROUPS = 4
 V2_FIRST_ROW = 8
+SCALAR_QUARTER = 1
+GSIN_ROW, GCOS_ROW, GAIN_ROWS = 0, 2, 4
+TWICE_ROW = 32
+
 E_BANKS = ((0, 1), (2, 3), (4, 5, 6, 7), (4, 5, 6, 7), (4, 5), (6, 4))
 GAIN_BANK = 1
 OUT_BANKS = (0, 2, 3, 7)
-GSIN_ROW, GCOS_ROW, GAIN_ROWS = 0, 2, 4
-SCALAR_QUARTERS = (1,)
-AT_WOVEN = 64
+
+WIDE, SHORT = 128, 64
+FIRST = 32
+BESIDE_COPIES = 192
+Y_SHARES = (FIRST, 2 * SHORT, WIDE, WIDE, SHORT, SHORT)
+X_SHARES = (0, SHORT, WIDE, BESIDE_COPIES, SHORT, 0)
+
+OVER = 64
+LAP = OVER // 2
 WOVEN = 2 * SLOTS * N + 2 * SLOTS * S
+AT_WOVEN = OVER
 AT_FIRST = 2 * WOVEN
-AT_TAB0 = AT_FIRST + 4 * HALF
-AT_TAB1 = AT_TAB0
-AT_MCOS0 = AT_TAB0 + 4 * T
-AT_TAB2 = AT_MCOS0 + 4 * SLOTS * N - 64
-AT_MCOS1 = AT_TAB2 + 64
-AT_ROWS = AT_TAB2 + 4 * T2 - 64
-AT_PLANE0 = AT_ROWS + 64
-AT_PLANE1 = AT_PLANE0 + S
-AT_WQ1 = AT_PLANE1 + S
+AT_TAB = AT_FIRST + 4 * HALF
+AT_MCOS0 = AT_TAB + 4 * T
+AT_TAB2 = AT_MCOS0 + 4 * SLOTS * N - OVER
+AT_MCOS1 = AT_TAB2 + OVER
+AT_WQ_PLANES = AT_MCOS1 + 4 * SLOTS * N
+AT_ROWS = AT_TAB2 + 4 * T2 - OVER
+AT_WQ1 = AT_ROWS + OVER + T // 2
+AT_LAST_SIZE = AT_WQ1 + 2 * HALF
 AT_ROUNDED0 = AT_WQ1 + 4 * SLOTS * H
 AT_ROUNDED1 = AT_ROUNDED0 + 2 * SLOTS * H
 AT_V2 = AT_ROUNDED1 + 2 * SLOTS * H
 AT_SECOND = AT_V2 + 4 * 4 * PASS
 AT_HALVES = AT_SECOND + 4 * SLOTS * QUARTER
-HALF_ANGLE = (0,)
-TWICE_ROW = 32
-Y_SHARES = (48, 128, 128, 128, 48, 64)
-VECTOR_RESULTS = 3
-X_SHARES = (0, 64, 128, 192, 64, 0)
 
 
 def tile_list_fragment_phase_fields_kernel(
@@ -71,8 +75,11 @@ def tile_list_fragment_phase_fields_kernel(
         codes = ctx.enter_context(tc.tile_pool(name="codes", bufs=3))
         psum = ctx.enter_context(tc.psum_pool(name="psum", bufs=1))
 
-        def held(name, shape, dtype, reuses=None):
-            return keep.tile(shape, dtype, name=name, tag=reuses or name, align_bytes=64)
+        def held(name, shape, dtype):
+            return keep.tile(shape, dtype, name=name, tag=name, align_bytes=64)
+
+        def placed(name, shape, dtype, at):
+            return arena.tile(shape, dtype, name=name, align_bytes=64, offset=at)
 
         def turn(name, shape, dtype, bufs):
             return ring.tile(shape, dtype, name=name, align_bytes=64, bufs=bufs)
@@ -85,11 +92,7 @@ def tile_list_fragment_phase_fields_kernel(
             return raw
 
         def load_words(sb, words):
-            nc.sync.dma_start(sb, words.rearrange("p n t -> p (n t)").bitcast(I32))
-
-        def load_by_slot(sb, vec):
-            nc.sync.dma_start(sb[:, :, 0:SLOTS], vec.rearrange("(b p t) -> p b t", b=2, t=SLOTS))
-            return sb
+            nc.sync.dma_start(sb[:], words.rearrange("p n t -> p (n t)").bitcast(I32))
 
         def quantise(words, plane, src):
             nc.vector.quantize_mx(out=words.bitcast(FP8X4), scales=plane, in_=src)
@@ -106,9 +109,6 @@ def tile_list_fragment_phase_fields_kernel(
         def by_line(flat):
             return flat.rearrange("p (c t i) -> p c t i", t=SLOTS, i=LINE)
 
-        def placed(name, shape, dtype, at):
-            return arena.tile(shape, dtype, name=name, align_bytes=64, offset=at)
-
         idx = held("idx", [P, S // 16], U16)
         idx2 = held("idx2", [P, S2 // 16], U16)
         tab_rows = placed("tab_rows", [P, T], U8, AT_ROWS)
@@ -124,8 +124,8 @@ def tile_list_fragment_phase_fields_kernel(
 
         nc.sync.dma_start(idx[:], offs)
         nc.scalar.dma_start(tab_rows[0:32, :].bitcast(I32), tab_scales.rearrange("a q t -> (a q) t").bitcast(I32))
-        tab_sb = [placed("tab_sb0", [P, T], I32, AT_TAB0)]
-        load_words(tab_sb[0][:], tab_words[0])
+        tab_sb = [placed("tab_sb0", [P, T], I32, AT_TAB)]
+        load_words(tab_sb[0], tab_words[0])
         wq_raw = [load_rows(held("wq_raw0", [P, SLOTS, H], F32), wq, 0)]
         nc.sync.dma_start(idx2[:], offs2)
         bq_sb = held("bq_sb", [P, SLOTS], F32)
@@ -139,7 +139,6 @@ def tile_list_fragment_phase_fields_kernel(
         wq_plane = []
         v_words = {}
         h_banks = {}
-        h_biased = {}
         h_words = held("h_words", [P, S], U32)
         h_plane = held("h_plane", [P, S], U8)
         v2_words = {}
@@ -148,22 +147,18 @@ def tile_list_fragment_phase_fields_kernel(
             for r in range(4):
                 queue.dma_start(v_plane[a][r:P:32, :].bitcast(I32), v_rows[16 * a + r : 16 * (a + 1) : 4, :].bitcast(I32))
 
-        def prepare_wq(a, rounded, vector_share):
+        def prepare_wq(a, rounded):
             target = rounded[:].rearrange("p (t m j) -> p m t j", t=SLOTS, j=SLOTS)
-            source = wq_raw[a][:].rearrange("p j (m t) -> p m t j", t=SLOTS)
-            if vector_share:
-                nc.vector.tensor_copy(target[:, 0:vector_share], source[:, 0:vector_share])
-            nc.scalar.copy(target[:, vector_share:P], source[:, vector_share:P])
+            nc.scalar.copy(target, wq_raw[a][:].rearrange("p j (m t) -> p m t j", t=SLOTS))
             words = held("wq_words%d" % a, [P, H], U32)
-            plane = placed("wq_plane%d" % a, [P, H], U8, AT_MCOS1 + 4 * SLOTS * N + H * a)
+            plane = placed("wq_plane%d" % a, [P, H], U8, AT_WQ_PLANES + H * a)
             quantise(words[:], plane[:], rounded[:])
             wq_words.append(words)
             wq_plane.append(plane)
 
-        def gather_v(a, j0, width, at=None):
-            name = "v_words%d_%d" % (a, j0)
-            words = held(name, [P, width], U32) if at is None else placed(name, [P, width], U32, at)
-            nc.vector.tensor_copy(words[:], tab_sb[a][:].bitcast(U32).indirect(idx[:, j0 // 16 : (j0 + width) // 16]))
+        def gather_v(a, j0, width, words):
+            offsets = idx[:, j0 // LIST_ROWS : (j0 + width) // LIST_ROWS]
+            nc.vector.tensor_copy(words[:], tab_sb[a][:].bitcast(U32).indirect(offsets))
             for c0 in range(0, width, QUARTER):
                 v_words[a, (j0 + c0) // QUARTER] = words[:, c0 : c0 + QUARTER]
 
@@ -171,7 +166,7 @@ def tile_list_fragment_phase_fields_kernel(
             for u in range(2):
                 if a == 0:
                     h_banks[quarter, u] = bank(2 * quarter + u)
-                if quarter in SCALAR_QUARTERS:
+                if quarter == SCALAR_QUARTER:
                     parts = [(t, quarter * QUARTER, QUARTER) for t in (2 * u, 2 * u + 1)]
                 else:
                     parts = [(t, quarter * QUARTER + u * CHUNK, CHUNK) for t in range(SLOTS)]
@@ -186,21 +181,11 @@ def tile_list_fragment_phase_fields_kernel(
                         stop=(a == 1 and k == len(parts) - 1),
                     )
 
-        def h_bias(quarter):
-            h_biased[quarter] = held("h_biased%d" % quarter, [P, SLOTS, QUARTER], BF16)
-            for t in range(SLOTS):
-                source = h_banks[quarter, t // 2][:, (t % 2) * QUARTER : (t % 2 + 1) * QUARTER]
-                nc.scalar.activation(h_biased[quarter][:, t, :], source, ACT.Identity, bias=bq_sb[:, t : t + 1])
-
         def h_weave(quarter, woven):
-            if quarter in SCALAR_QUARTERS:
-                nc.vector.tensor_copy(side_by_side(woven, 2 * RUN), by_slot(h_biased[quarter][:], 2 * RUN))
-            else:
-                for u in range(2):
-                    source = h_banks[quarter, u][:].rearrange("p (t j) -> p t j", t=SLOTS)
-                    part = woven[:, SLOTS * u * CHUNK : SLOTS * (u + 1) * CHUNK]
-                    nc.vector.tensor_tensor(side_by_side(part), by_slot(source), spread(bq_sb[:], CHUNK), ALU.add)
-            return woven
+            for u in range(2):
+                source = h_banks[quarter, u][:].rearrange("p (t j) -> p t j", t=SLOTS)
+                part = woven[:, SLOTS * u * CHUNK : SLOTS * (u + 1) * CHUNK]
+                nc.vector.tensor_tensor(side_by_side(part), by_slot(source), spread(bq_sb[:], CHUNK), ALU.add)
 
         def h_quantise(j0, width, woven):
             quantise(h_words[:, j0 : j0 + width], h_plane[:, j0 : j0 + width], woven)
@@ -209,36 +194,39 @@ def tile_list_fragment_phase_fields_kernel(
             v2_words[b] = placed("v2_words%d" % b, [P, PASS], U32, AT_V2 + 2 * 4 * PASS * b)
             nc.vector.tensor_copy(
                 v2_words[b][:].rearrange("p (t q) -> p q t", t=SLOTS),
-                tab2_sb[:].bitcast(U32).indirect(idx2[:, b * LIST_COLS : (b + 1) * LIST_COLS]),
+                tab2_sb[:].bitcast(U32).indirect(idx2[:, b * PASS // LIST_ROWS : (b + 1) * PASS // LIST_ROWS]),
             )
 
         v_rows = held("v_rows", [P, S], U8)
         nc.vector.tensor_copy(v_rows[:], tab_rows[:].indirect(idx[:]))
         tab2_sb = placed("tab2_sb", [P, T2], I32, AT_TAB2)
-        load_words(tab2_sb[:], tab2_words[0])
+        load_words(tab2_sb, tab2_words[0])
         wq_raw.append(load_rows(placed("wq_raw1", [P, SLOTS, H], F32, AT_WQ1), wq, 1))
         place_v_rows(0, nc.scalar)
         for half in range(2):
-            gather_v(0, half * HALF, HALF)
-        tab_sb.append(placed("tab_sb1", [P, T], I32, AT_TAB0))
-        load_words(tab_sb[1][:], tab_words[1])
+            gather_v(0, half * HALF, HALF, held("v_words0_%d" % half, [P, HALF], U32))
+        tab_sb.append(placed("tab_sb1", [P, T], I32, AT_TAB))
+        load_words(tab_sb[1], tab_words[1])
         place_v_rows(1, nc.sync)
         v2_plane = held("v2_plane", [P, S2], U8)
         nc.vector.tensor_copy(v2_plane[:].rearrange("p (b t q) -> p b q t", b=2, t=SLOTS), tab2_plane[:].indirect(idx2[:]))
         for b in range(2):
             gather_v2(b)
-        prepare_wq(0, placed("wq_rounded0", [P, SLOTS * H], BF16, AT_ROUNDED0), 0)
+        prepare_wq(0, placed("wq_rounded0", [P, SLOTS * H], BF16, AT_ROUNDED0))
         gain_rows = wq_raw[0][:, 0, :]
         twice = gain_rows[TWICE_ROW : TWICE_ROW + 1, :]
         nc.sync.dma_start(twice, gcos[0:PASS].rearrange("(b m) -> b m", b=1))
         nc.scalar.activation(twice, twice, ACT.Copy, scale=-2.0)
-        phi_sb = load_by_slot(placed("phi_sb", [P, 2, 2 * SLOTS], F32, AT_ROUNDED0 + 64), phi)
+        phi_sb = placed("phi_sb", [P, 2, 2 * SLOTS], F32, AT_ROUNDED0 + OVER)
+        nc.sync.dma_start(phi_sb[:, :, 0:SLOTS], phi.rearrange("(b p t) -> p b t", b=2, t=SLOTS))
         for vec, row in ((gsin, GSIN_ROW), (gcos, GCOS_ROW)):
             nc.sync.dma_start(gain_rows[row : row + 2, :], vec.rearrange("(b m) -> b m", b=2))
         half_phi = held("half_phi", [P, SLOTS], F32)
         nc.scalar.activation(half_phi[:], phi_sb[:, 0, 0:SLOTS], ACT.Copy, scale=0.5)
-        mcos_raw = [load_rows(placed("mcos_raw%d" % b, [P, SLOTS, N], F32, at), mcos, b) for b, at in enumerate((AT_MCOS0, AT_MCOS1))]
-        prepare_wq(1, placed("wq_rounded1", [P, SLOTS * H], BF16, AT_ROUNDED1), 0)
+        mcos_raw = []
+        for b, at in enumerate((AT_MCOS0, AT_MCOS1)):
+            mcos_raw.append(load_rows(placed("mcos_raw%d" % b, [P, SLOTS, N], F32, at), mcos, b))
+        prepare_wq(1, placed("wq_rounded1", [P, SLOTS * H], BF16, AT_ROUNDED1))
         m4_sb = placed("m4_sb", [P, 2 * 2 * N], U8, AT_ROUNDED1)
         nc.sync.dma_start(
             m4_sb[:].bitcast(I32).rearrange("p (b c) -> p b c", b=2), m4_words.bitcast(I32).rearrange("b p c -> p b c")
@@ -253,45 +241,46 @@ def tile_list_fragment_phase_fields_kernel(
         for quarter in range(4):
             h_pass(0, quarter)
         for quarter in range(2):
-            gather_v(1, quarter * QUARTER, QUARTER)
+            gather_v(1, quarter * QUARTER, QUARTER, held("v_words1_%d" % quarter, [P, QUARTER], U32))
             h_pass(1, quarter)
-        for quarter in SCALAR_QUARTERS:
-            h_bias(quarter)
-        first_woven = h_weave(0, placed("h_woven0", [P, SLOTS * QUARTER], BF16, AT_FIRST)[:])
+        h_biased = held("h_biased", [P, SLOTS, QUARTER], BF16)
+        for t in range(SLOTS):
+            source = h_banks[SCALAR_QUARTER, t // 2][:, (t % 2) * QUARTER : (t % 2 + 1) * QUARTER]
+            nc.scalar.activation(h_biased[:, t, :], source, ACT.Identity, bias=bq_sb[:, t : t + 1])
+        first_woven = placed("h_woven0", [P, SLOTS * QUARTER], BF16, AT_FIRST)
+        h_weave(0, first_woven)
         for u in range(2):
             h_quantise(u * CHUNK, CHUNK, first_woven[:, u * SLOTS * CHUNK : (u + 1) * SLOTS * CHUNK])
-        gather_v(1, HALF, HALF, AT_FIRST)
-        h_quantise(QUARTER, QUARTER, h_weave(1, placed("h_woven1", [P, SLOTS * QUARTER], BF16, AT_SECOND)[:]))
+        gather_v(1, HALF, HALF, placed("v_words1_last", [P, HALF], U32, AT_FIRST))
+        second_woven = placed("h_woven1", [P, SLOTS * QUARTER], BF16, AT_SECOND)
+        nc.vector.tensor_copy(side_by_side(second_woven[:], 2 * RUN), by_slot(h_biased[:], 2 * RUN))
+        h_quantise(QUARTER, QUARTER, second_woven[:])
 
         units = [(0, QUARTER, 0), (QUARTER, QUARTER, 0), (0, HALF, 1)]
         units.extend([(HALF, HALF, 0), (HALF, QUARTER, 1), (HALF + QUARTER, QUARTER, 1)])
         sines = {}
         cosines = {}
-        halves = {}
-        squares = {}
         out_banks = {}
-        e_banks = []
 
         def phases(unit):
             j0, width, b = unit
-            last = unit == units[-1]
+            first, last = unit == units[0], unit == units[-1]
             sine = turn("sine", [P, SLOTS * width], F32, bufs=3)
-            halved = units.index(unit) in HALF_ANGLE
-            if halved:
-                size = placed("halves%d" % j0, [P, SLOTS * width], F32, AT_HALVES + 4 * SLOTS * j0)
-            elif unit == units[4]:
-                size = placed("held_size", [P, SLOTS * width], F32, AT_TAB0 + 4 * HALF)
+            if first:
+                size = halves
+            elif unit == units[-2]:
+                size = placed("fifth_size", [P, SLOTS * width], F32, AT_TAB + 4 * HALF)
             elif last:
-                size = placed("late_size", [P, SLOTS * width], F32, AT_WQ1 + 1024)
+                size = placed("last_size", [P, SLOTS * width], F32, AT_LAST_SIZE)
             else:
                 size = turn("size", [P, SLOTS * width], F32, bufs=2)
             per_bank = HALF // width
             sums = []
             early = 1 if width == HALF else 0
             for t0 in range(0, SLOTS, per_bank):
-                e_banks.append(bank(E_BANKS[units.index(unit)][t0 // per_bank]))
+                e_bank = bank(E_BANKS[units.index(unit)][t0 // per_bank])
                 for t in range(t0, t0 + per_bank):
-                    target = e_banks[-1][:, (t - t0) * width : (t - t0 + 1) * width]
+                    target = e_bank[:, (t - t0) * width : (t - t0 + 1) * width]
                     sums.append(target.rearrange("p (c i) -> p c i", i=LINE))
                     nc.tensor.matmul_mx(
                         out=target,
@@ -303,17 +292,16 @@ def tile_list_fragment_phase_fields_kernel(
                         stop=True,
                     )
                 for t in range(t0, t0 + per_bank):
-                    if halved:
+                    if first:
                         nc.scalar.activation(by_line(size[:])[:, :, t, :], sums[t], ACT.Sin, bias=half_phi[:, t : t + 1], scale=0.5)
                     else:
                         nc.scalar.activation(by_line(sine[:])[:, :, t, :], sums[t], ACT.Sin, bias=phi_sb[:, b, t : t + 1])
                     if t < early:
                         nc.scalar.activation(by_line(size[:])[:, :, t, :], sums[t], ACT.Abs, bias=phi_sb[:, b, t : t + 1])
             sines[unit] = sine
-            if halved:
+            if first:
                 for t in range(SLOTS):
                     nc.scalar.activation(by_line(sine[:])[:, :, t, :], sums[t], ACT.Sin, bias=phi_sb[:, b, t : t + 1])
-                halves[unit] = size
                 return
             for t in range(early, SLOTS):
                 nc.scalar.activation(by_line(size[:])[:, :, t, :], sums[t], ACT.Abs, bias=phi_sb[:, b, t : t + 1])
@@ -329,11 +317,6 @@ def tile_list_fragment_phase_fields_kernel(
                     )
                 cosines[unit].append((c0, step, piece))
 
-        def square(unit, target):
-            source = by_line(halves[unit][:])
-            nc.gpsimd.tensor_tensor(target.rearrange("p (c i t) -> p c t i", i=LINE, t=SLOTS), source, source, ALU.mult)
-            squares[unit] = target
-
         def operand(name, woven, width, words=None):
             return (
                 woven,
@@ -346,13 +329,12 @@ def tile_list_fragment_phase_fields_kernel(
             cut = SLOTS * (share if gpsimd_first else width - share)
             low, high = slice(0, cut), slice(cut, SLOTS * width)
             mine, other = (high, low) if gpsimd_first else (low, high)
-            if share < width:
-                nc.vector.tensor_tensor(
-                    part[:, mine].rearrange("p (c i t) -> p c t i", i=LINE, t=SLOTS),
-                    by_line(values[:, mine]),
-                    spread(gains_psum[:, :, row], width - share, LINE),
-                    ALU.mult,
-                )
+            nc.vector.tensor_tensor(
+                side_by_side(part[:, mine], LINE),
+                by_line(values[:, mine]),
+                spread(gains_psum[:, :, row], width - share, LINE),
+                ALU.mult,
+            )
             if share > 0:
                 nc.gpsimd.tensor_tensor(
                     part[:, other].rearrange("p (a c i t) -> p a c t i", c=GROUPS, i=LINE, t=SLOTS),
@@ -361,15 +343,12 @@ def tile_list_fragment_phase_fields_kernel(
                     ALU.mult,
                 )
 
-        def quantise_part(tiles, c0, width):
-            woven, words, plane = tiles
-            quantise(words[:, c0 : c0 + width], plane[:, c0 : c0 + width], woven[:, SLOTS * c0 : SLOTS * (c0 + width)])
-
         out_rows = out.rearrange("(n p) j -> p n j", p=P)
 
         def mix(unit, tiles, k0, width, sines_pass):
             j0, b = unit[0], unit[2]
-            quantise_part(tiles, k0, width)
+            values, words, plane = tiles
+            quantise(words[:, k0 : k0 + width], plane[:, k0 : k0 + width], values[:, SLOTS * k0 : SLOTS * (k0 + width)])
             step = width if j0 < HALF else CHUNK
             for c0 in range(k0, k0 + width, step):
                 chunk = (j0 + c0) // CHUNK
@@ -392,26 +371,24 @@ def tile_list_fragment_phase_fields_kernel(
                         out=out_banks[key][:, at : at + step],
                         lhsT=weights,
                         lhsT_scale=scales,
-                        rhs=tiles[1][:, cols].bitcast(FP8X4),
-                        rhs_scale=tiles[2][:, cols],
+                        rhs=words[:, cols].bitcast(FP8X4),
+                        rhs_scale=plane[:, cols],
                         start=start,
                         stop=stop,
                     )
                     if stop and j0 < HALF:
-                        if n < VECTOR_RESULTS:
-                            result = held("rows%d" % n, [P, HALF], F32)
-                            nc.vector.tensor_copy(result[:], out_banks[key][:])
-                        else:
-                            result = placed("rows%d" % n, [P, HALF], F32, AT_TAB0 + 4 * HALF * n)
-                            nc.scalar.copy(result[:], out_banks[key][:])
+                        result = held("rows%d" % n, [P, HALF], F32)
+                        nc.vector.tensor_copy(result[:], out_banks[key][:])
                         nc.sync.dma_start(out_rows[:, n, 0:HALF], result[:])
                     elif stop:
-                        result = placed("result%d" % chunk, [P, N // P, CHUNK], F32, AT_WQ1 + 4 * N * (chunk % 4))
+                        result = placed("result%d" % chunk, [P, N // P, CHUNK], F32, AT_WQ1 + 4 * N * (chunk - HALF // CHUNK))
                         nc.scalar.copy(result[:], out_banks[key][:, 0:N].rearrange("p (n j) -> p n j", j=CHUNK))
                         nc.sync.dma_start(out_rows[:, :, chunk * CHUNK : (chunk + 1) * CHUNK], result[:])
 
+        halves = placed("halves", [P, SLOTS * QUARTER], F32, AT_HALVES)
         phases(units[0])
-        square(units[0], placed("squares0", [P, SLOTS * QUARTER], F32, AT_SECOND)[:])
+        squares = placed("squares", [P, SLOTS * QUARTER], F32, AT_SECOND)
+        nc.gpsimd.tensor_tensor(side_by_side(squares[:], LINE), by_line(halves[:]), by_line(halves[:]), ALU.mult)
         for quarter in (2, 3):
             h_pass(1, quarter)
         late_woven = held("h_woven2", [P, SLOTS * HALF], BF16)
@@ -423,7 +400,7 @@ def tile_list_fragment_phase_fields_kernel(
         gains_psum = gain_bank[:].rearrange("p (t r) -> p t r", t=SLOTS)
         gains_sbuf = held("gains_sbuf", [P, GAIN_ROWS, GROUPS, SLOTS, LINE], F32)
         by_row = gains_psum[:, :, 0:GAIN_ROWS].rearrange("p t r -> p r t").unsqueeze(2).unsqueeze(4)
-        nc.vector.tensor_copy(gains_sbuf[:], by_row.to_broadcast([P, GAIN_ROWS, GROUPS, SLOTS, LINE]))
+        nc.scalar.copy(gains_sbuf[:], by_row.to_broadcast([P, GAIN_ROWS, GROUPS, SLOTS, LINE]))
         first_y = operand("y", held("first_y", [P, SLOTS * QUARTER], BF16)[:], QUARTER)
         gain(first_y, sines[units[0]][:], GSIN_ROW, 0, QUARTER, Y_SHARES[0], True)
         h_quantise(HALF, HALF, late_woven[:])
@@ -433,8 +410,8 @@ def tile_list_fragment_phase_fields_kernel(
         mcos_plane = held("mcos_plane", [P, 2 * N], U8)
         for b in range(2):
             nc.vector.tensor_copy(side_by_side(mcos_rounded[:, b * SLOTS * N : (b + 1) * SLOTS * N]), by_slot(mcos_raw[b][:]))
-        for c0, c1 in ((0, N), (N, 2 * N)):
-            quantise(mcos_words[:, c0:c1], mcos_plane[:, c0:c1], mcos_rounded[:, SLOTS * c0 : SLOTS * c1])
+        for c0 in (0, N):
+            quantise(mcos_words[:, c0 : c0 + N], mcos_plane[:, c0 : c0 + N], mcos_rounded[:, SLOTS * c0 : SLOTS * (c0 + N)])
 
         late_words = {
             ("x", 1): placed("x1_words", [P, QUARTER], U32, AT_V2),
@@ -463,10 +440,10 @@ def tile_list_fragment_phase_fields_kernel(
             else:
                 x_woven = held("x_woven%d" % g, [P, SLOTS * width], BF16)[:]
             x_tiles = operand("x", x_woven, width, late_words.get(("x", g)))
-            if unit in squares:
+            if g == 0:
                 nc.vector.scalar_tensor_tensor(
                     x_woven.rearrange("p (c t) -> p c t", t=SLOTS),
-                    squares[unit].rearrange("p (c t) -> p c t", t=SLOTS),
+                    squares[:].rearrange("p (c t) -> p c t", t=SLOTS),
                     -0.5,
                     gains_psum[:, :, TWICE_ROW].unsqueeze(1).to_broadcast([P, width, SLOTS]),
                     ALU.add,

@@ -34,21 +34,18 @@ SCALAR_QUARTER = 1
 GSIN_ROW, GCOS_ROW, GAIN_ROWS = 0, 2, 4
 TWICE_ROW = 32
 
-E_BANKS = ((0, 1), (2, 3), (4, 5, 6, 7), (4, 5, 6, 7), (4, 5), (6, 4))
+E_BANKS = ((0, 1), (2, 3), (4, 5, 6, 7), (4, 5, 6, 7), (4, 5), (0, 2))
 GAIN_BANK = 1
-OUT_BANKS = (0, 2, 3, 7)
+OUT_BANKS = ((0, 2, 3), (6, 7, 3, 4))
+SCALAR_ROWS = 1
 
-WIDE, SHORT = 128, 64
-FIRST = 32
-BESIDE_COPIES = 192
-Y_SHARES = (FIRST, 2 * SHORT, WIDE, WIDE, SHORT, SHORT)
-X_SHARES = (0, SHORT, WIDE, BESIDE_COPIES, SHORT, 0)
+AFTER_SQUARES = 96
+WIDE = 144
+BESIDE_COPIES = (192, 192)
+SHORT = 64
 
 OVER = 64
-LAP = OVER // 2
-WOVEN = 2 * SLOTS * N + 2 * SLOTS * S
-AT_WOVEN = OVER
-AT_FIRST = 2 * WOVEN
+AT_FIRST = 0
 AT_TAB = AT_FIRST + 4 * HALF
 AT_MCOS0 = AT_TAB + 4 * T
 AT_TAB2 = AT_MCOS0 + 4 * SLOTS * N - OVER
@@ -59,9 +56,11 @@ AT_WQ1 = AT_ROWS + OVER + T // 2
 AT_LAST_SIZE = AT_WQ1 + 2 * HALF
 AT_ROUNDED0 = AT_WQ1 + 4 * SLOTS * H
 AT_ROUNDED1 = AT_ROUNDED0 + 2 * SLOTS * H
-AT_V2 = AT_ROUNDED1 + 2 * SLOTS * H
-AT_SECOND = AT_V2 + 4 * 4 * PASS
-AT_HALVES = AT_SECOND + 4 * SLOTS * QUARTER
+AT_HALVES = AT_ROUNDED1 + 2 * SLOTS * H
+AT_MCOS_ROUNDED = AT_HALVES + 4 * SLOTS * QUARTER - OVER
+AT_SQUARES = AT_MCOS_ROUNDED + 4 * SLOTS * N - OVER
+AT_LATE_PLANE = AT_SQUARES + OVER
+AT_SECOND = AT_SQUARES + 4 * SLOTS * QUARTER - OVER
 
 
 def tile_list_fragment_phase_fields_kernel(
@@ -72,7 +71,6 @@ def tile_list_fragment_phase_fields_kernel(
         keep = ctx.enter_context(tc.tile_pool(name="keep", bufs=1))
         arena = ctx.enter_context(tc.tile_pool(name="arena", bufs=1))
         ring = ctx.enter_context(tc.tile_pool(name="ring", bufs=2))
-        codes = ctx.enter_context(tc.tile_pool(name="codes", bufs=3))
         psum = ctx.enter_context(tc.psum_pool(name="psum", bufs=1))
 
         def held(name, shape, dtype):
@@ -139,8 +137,8 @@ def tile_list_fragment_phase_fields_kernel(
         wq_plane = []
         v_words = {}
         h_banks = {}
-        h_words = held("h_words", [P, S], U32)
-        h_plane = held("h_plane", [P, S], U8)
+        h_words = {0: held("h_words", [P, HALF], U32)}
+        h_plane = {0: held("h_plane", [P, HALF], U8)}
         v2_words = {}
 
         def place_v_rows(a, queue):
@@ -181,17 +179,16 @@ def tile_list_fragment_phase_fields_kernel(
                         stop=(a == 1 and k == len(parts) - 1),
                     )
 
-        def h_weave(quarter, woven):
-            for u in range(2):
-                source = h_banks[quarter, u][:].rearrange("p (t j) -> p t j", t=SLOTS)
-                part = woven[:, SLOTS * u * CHUNK : SLOTS * (u + 1) * CHUNK]
-                nc.vector.tensor_tensor(side_by_side(part), by_slot(source), spread(bq_sb[:], CHUNK), ALU.add)
+        def h_weave(quarter, u, part):
+            source = h_banks[quarter, u][:].rearrange("p (t j) -> p t j", t=SLOTS)
+            nc.vector.tensor_tensor(side_by_side(part), by_slot(source), spread(bq_sb[:], CHUNK), ALU.add)
 
         def h_quantise(j0, width, woven):
-            quantise(h_words[:, j0 : j0 + width], h_plane[:, j0 : j0 + width], woven)
+            half, c0 = divmod(j0, HALF)
+            quantise(h_words[half][:, c0 : c0 + width], h_plane[half][:, c0 : c0 + width], woven)
 
         def gather_v2(b):
-            v2_words[b] = placed("v2_words%d" % b, [P, PASS], U32, AT_V2 + 2 * 4 * PASS * b)
+            v2_words[b] = held("v2_words%d" % b, [P, PASS], U32)
             nc.vector.tensor_copy(
                 v2_words[b][:].rearrange("p (t q) -> p q t", t=SLOTS),
                 tab2_sb[:].bitcast(U32).indirect(idx2[:, b * PASS // LIST_ROWS : (b + 1) * PASS // LIST_ROWS]),
@@ -247,33 +244,25 @@ def tile_list_fragment_phase_fields_kernel(
         for t in range(SLOTS):
             source = h_banks[SCALAR_QUARTER, t // 2][:, (t % 2) * QUARTER : (t % 2 + 1) * QUARTER]
             nc.scalar.activation(h_biased[:, t, :], source, ACT.Identity, bias=bq_sb[:, t : t + 1])
-        first_woven = placed("h_woven0", [P, SLOTS * QUARTER], BF16, AT_FIRST)
-        h_weave(0, first_woven)
+        first_woven = [placed("h_woven0_%d" % u, [P, SLOTS * CHUNK], BF16, AT_FIRST + 2 * SLOTS * CHUNK * u) for u in range(2)]
         for u in range(2):
-            h_quantise(u * CHUNK, CHUNK, first_woven[:, u * SLOTS * CHUNK : (u + 1) * SLOTS * CHUNK])
-        gather_v(1, HALF, HALF, placed("v_words1_last", [P, HALF], U32, AT_FIRST))
-        second_woven = placed("h_woven1", [P, SLOTS * QUARTER], BF16, AT_SECOND)
-        nc.vector.tensor_copy(side_by_side(second_woven[:], 2 * RUN), by_slot(h_biased[:], 2 * RUN))
-        h_quantise(QUARTER, QUARTER, second_woven[:])
+            h_weave(0, u, first_woven[u][:])
+        for u in range(2):
+            h_quantise(u * CHUNK, CHUNK, first_woven[u][:])
 
         units = [(0, QUARTER, 0), (QUARTER, QUARTER, 0), (0, HALF, 1)]
         units.extend([(HALF, HALF, 0), (HALF, QUARTER, 1), (HALF + QUARTER, QUARTER, 1)])
-        sines = {}
-        cosines = {}
-        out_banks = {}
+        sines = {(half, b): held("sine%d_%d" % (half, b), [P, SLOTS * HALF], F32) for half in range(2) for b in range(2)}
+        cosines = {key: held("cosine%d_%d" % key, [P, SLOTS * HALF], F32) for key in sines if key != (0, 0)}
 
-        def phases(unit):
+        def columns(tile, c0, width):
+            return tile[:, SLOTS * c0 : SLOTS * (c0 + width)]
+
+        def phases(unit, size):
             j0, width, b = unit
-            first, last = unit == units[0], unit == units[-1]
-            sine = turn("sine", [P, SLOTS * width], F32, bufs=3)
-            if first:
-                size = halves
-            elif unit == units[-2]:
-                size = placed("fifth_size", [P, SLOTS * width], F32, AT_TAB + 4 * HALF)
-            elif last:
-                size = placed("last_size", [P, SLOTS * width], F32, AT_LAST_SIZE)
-            else:
-                size = turn("size", [P, SLOTS * width], F32, bufs=2)
+            half, c0 = divmod(j0, HALF)
+            halved, last = (half, b) == (0, 0), unit == units[-1]
+            sine = columns(sines[half, b], c0, width)
             per_bank = HALF // width
             sums = []
             early = 1 if width == HALF else 0
@@ -286,114 +275,53 @@ def tile_list_fragment_phase_fields_kernel(
                         out=target,
                         lhsT=v2_words[b][:, t * P : (t + 1) * P].bitcast(FP8X4),
                         lhsT_scale=v2_plane[V2_FIRST_ROW:P, b * PASS + t * P : b * PASS + (t + 1) * P],
-                        rhs=h_words[:, j0 : j0 + width].bitcast(FP8X4),
-                        rhs_scale=h_plane[:, j0 : j0 + width],
+                        rhs=h_words[half][:, c0 : c0 + width].bitcast(FP8X4),
+                        rhs_scale=h_plane[half][:, c0 : c0 + width],
                         start=True,
                         stop=True,
                     )
                 for t in range(t0, t0 + per_bank):
-                    if first:
+                    if halved:
                         nc.scalar.activation(by_line(size[:])[:, :, t, :], sums[t], ACT.Sin, bias=half_phi[:, t : t + 1], scale=0.5)
                     else:
-                        nc.scalar.activation(by_line(sine[:])[:, :, t, :], sums[t], ACT.Sin, bias=phi_sb[:, b, t : t + 1])
+                        nc.scalar.activation(by_line(sine)[:, :, t, :], sums[t], ACT.Sin, bias=phi_sb[:, b, t : t + 1])
                     if t < early:
                         nc.scalar.activation(by_line(size[:])[:, :, t, :], sums[t], ACT.Abs, bias=phi_sb[:, b, t : t + 1])
-            sines[unit] = sine
-            if first:
+            if halved:
                 for t in range(SLOTS):
-                    nc.scalar.activation(by_line(sine[:])[:, :, t, :], sums[t], ACT.Sin, bias=phi_sb[:, b, t : t + 1])
+                    nc.scalar.activation(by_line(sine)[:, :, t, :], sums[t], ACT.Sin, bias=phi_sb[:, b, t : t + 1])
                 return
             for t in range(early, SLOTS):
                 nc.scalar.activation(by_line(size[:])[:, :, t, :], sums[t], ACT.Abs, bias=phi_sb[:, b, t : t + 1])
             step = CHUNK if last else width
-            cosine = turn("cosine", [P, SLOTS * width], F32, bufs=3)
-            cosines[unit] = []
-            for c0 in range(0, width, step):
-                piece = cosine[:, SLOTS * c0 : SLOTS * (c0 + step)]
-                source = size[:, SLOTS * c0 : SLOTS * (c0 + step)]
+            for k0 in range(0, width, step):
+                piece = columns(cosines[half, b], c0 + k0, step)
+                source = columns(size, k0, step)
                 for t0, t1 in ((0, SLOTS - 1), (SLOTS - 1, SLOTS)) if width == HALF else ((0, SLOTS),):
                     nc.scalar.activation(
                         by_line(piece)[:, :, t0:t1, :], by_line(source)[:, :, t0:t1, :], ACT.Sin, bias=math.pi / 2, scale=-1.0
                     )
-                cosines[unit].append((c0, step, piece))
 
-        def operand(name, woven, width, words=None):
-            return (
-                woven,
-                codes.tile([P, width], U32, name=name + "_words", align_bytes=64) if words is None else words,
-                codes.tile([P, width], U8, name=name + "_plane", align_bytes=64),
-            )
+        def square(target, halves):
+            nc.gpsimd.tensor_tensor(side_by_side(target[:], LINE), by_line(halves[:]), by_line(halves[:]), ALU.mult)
 
-        def gain(tiles, values, row, c0, width, share, gpsimd_first):
-            part = tiles[0][:, SLOTS * c0 : SLOTS * (c0 + width)]
-            cut = SLOTS * (share if gpsimd_first else width - share)
-            low, high = slice(0, cut), slice(cut, SLOTS * width)
-            mine, other = (high, low) if gpsimd_first else (low, high)
-            nc.vector.tensor_tensor(
-                side_by_side(part[:, mine], LINE),
-                by_line(values[:, mine]),
-                spread(gains_psum[:, :, row], width - share, LINE),
-                ALU.mult,
-            )
-            if share > 0:
-                nc.gpsimd.tensor_tensor(
-                    part[:, other].rearrange("p (a c i t) -> p a c t i", c=GROUPS, i=LINE, t=SLOTS),
-                    values[:, other].rearrange("p (a c t i) -> p a c t i", c=GROUPS, t=SLOTS, i=LINE),
-                    gains_sbuf[:, row].unsqueeze(1).to_broadcast([P, share // (GROUPS * LINE), GROUPS, SLOTS, LINE]),
-                    ALU.mult,
-                )
-
-        out_rows = out.rearrange("(n p) j -> p n j", p=P)
-
-        def mix(unit, tiles, k0, width, sines_pass):
-            j0, b = unit[0], unit[2]
-            values, words, plane = tiles
-            quantise(words[:, k0 : k0 + width], plane[:, k0 : k0 + width], values[:, SLOTS * k0 : SLOTS * (k0 + width)])
-            step = width if j0 < HALF else CHUNK
-            for c0 in range(k0, k0 + width, step):
-                chunk = (j0 + c0) // CHUNK
-                cols = slice(c0, c0 + step)
-                for n in range(N // P):
-                    if j0 < HALF:
-                        key, at = n, j0 + c0
-                        start, stop = sines_pass and unit == units[0], not sines_pass and b == 1
-                    else:
-                        key, at = chunk, n * CHUNK
-                        start, stop = sines_pass and b == 0 and n == 0, not sines_pass and b == 1 and n == N // P - 1
-                    if start:
-                        out_banks[key] = bank(OUT_BANKS[key % len(OUT_BANKS)])
-                    w0 = b * N + n * P
-                    if sines_pass:
-                        weights, scales = m4_sb[:, 2 * w0 : 2 * (w0 + P)].bitcast(FP4X4), m4_plane[:, w0 : w0 + P]
-                    else:
-                        weights, scales = mcos_words[:, w0 : w0 + P].bitcast(FP8X4), mcos_plane[:, w0 : w0 + P]
-                    nc.tensor.matmul_mx(
-                        out=out_banks[key][:, at : at + step],
-                        lhsT=weights,
-                        lhsT_scale=scales,
-                        rhs=words[:, cols].bitcast(FP8X4),
-                        rhs_scale=plane[:, cols],
-                        start=start,
-                        stop=stop,
-                    )
-                    if stop and j0 < HALF:
-                        result = held("rows%d" % n, [P, HALF], F32)
-                        nc.vector.tensor_copy(result[:], out_banks[key][:])
-                        nc.sync.dma_start(out_rows[:, n, 0:HALF], result[:])
-                    elif stop:
-                        result = placed("result%d" % chunk, [P, N // P, CHUNK], F32, AT_WQ1 + 4 * N * (chunk - HALF // CHUNK))
-                        nc.scalar.copy(result[:], out_banks[key][:, 0:N].rearrange("p (n j) -> p n j", j=CHUNK))
-                        nc.sync.dma_start(out_rows[:, :, chunk * CHUNK : (chunk + 1) * CHUNK], result[:])
-
-        halves = placed("halves", [P, SLOTS * QUARTER], F32, AT_HALVES)
-        phases(units[0])
-        squares = placed("squares", [P, SLOTS * QUARTER], F32, AT_SECOND)
-        nc.gpsimd.tensor_tensor(side_by_side(squares[:], LINE), by_line(halves[:]), by_line(halves[:]), ALU.mult)
-        for quarter in (2, 3):
-            h_pass(1, quarter)
+        halves = [held("halves0", [P, SLOTS * QUARTER], F32), placed("halves1", [P, SLOTS * QUARTER], F32, AT_HALVES)]
+        phases(units[0], halves[0])
+        second_woven = placed("h_woven1", [P, SLOTS * QUARTER], BF16, AT_SECOND)
+        nc.vector.tensor_copy(side_by_side(second_woven[:], 2 * RUN), by_slot(h_biased[:], 2 * RUN))
+        gather_v(1, 2 * QUARTER, QUARTER, placed("v_words1_2", [P, QUARTER], U32, AT_FIRST))
+        h_quantise(QUARTER, QUARTER, second_woven[:])
+        gather_v(1, 3 * QUARTER, QUARTER, placed("v_words1_3", [P, QUARTER], U32, AT_FIRST + 4 * QUARTER))
+        phases(units[1], halves[1])
+        squares = [placed("squares0", [P, SLOTS * QUARTER], F32, AT_SQUARES), held("squares1", [P, SLOTS * QUARTER], F32)]
+        for k in range(2):
+            square(squares[k], halves[k])
         late_woven = held("h_woven2", [P, SLOTS * HALF], BF16)
         for quarter in (2, 3):
-            h_weave(quarter, late_woven[:, (quarter - 2) * SLOTS * QUARTER : (quarter - 1) * SLOTS * QUARTER])
+            h_pass(1, quarter)
+        for quarter in (2, 3):
+            for u in range(2):
+                h_weave(quarter, u, columns(late_woven, (quarter - 2) * QUARTER + u * CHUNK, CHUNK))
         gain_bank = bank(GAIN_BANK)
         for t in range(SLOTS):
             nc.tensor.transpose(gain_bank[:, t * P : (t + 1) * P], gain_rows[:, t:PASS:SLOTS], identity[:])
@@ -401,11 +329,42 @@ def tile_list_fragment_phase_fields_kernel(
         gains_sbuf = held("gains_sbuf", [P, GAIN_ROWS, GROUPS, SLOTS, LINE], F32)
         by_row = gains_psum[:, :, 0:GAIN_ROWS].rearrange("p t r -> p r t").unsqueeze(2).unsqueeze(4)
         nc.scalar.copy(gains_sbuf[:], by_row.to_broadcast([P, GAIN_ROWS, GROUPS, SLOTS, LINE]))
-        first_y = operand("y", held("first_y", [P, SLOTS * QUARTER], BF16)[:], QUARTER)
-        gain(first_y, sines[units[0]][:], GSIN_ROW, 0, QUARTER, Y_SHARES[0], True)
+        phases(units[2], turn("size", [P, SLOTS * HALF], F32, bufs=2))
+
+        y_woven = held("y_woven", [P, SLOTS * HALF], BF16)
+        x_woven = held("x_woven", [P, SLOTS * HALF], BF16)
+
+        def gain(woven, values, row, c0, width, share):
+            mine = width - share
+            nc.vector.tensor_tensor(
+                side_by_side(columns(woven, c0, mine), LINE),
+                by_line(columns(values, c0, mine)),
+                spread(gains_psum[:, :, row], mine, LINE),
+                ALU.mult,
+            )
+            if share > 0:
+                nc.gpsimd.tensor_tensor(
+                    columns(woven, c0 + mine, share).rearrange("p (a c i t) -> p a c t i", c=GROUPS, i=LINE, t=SLOTS),
+                    columns(values, c0 + mine, share).rearrange("p (a c t i) -> p a c t i", c=GROUPS, t=SLOTS, i=LINE),
+                    gains_sbuf[:, row].unsqueeze(1).to_broadcast([P, share // (GROUPS * LINE), GROUPS, SLOTS, LINE]),
+                    ALU.mult,
+                )
+
+        for k in range(2):
+            gain(y_woven, sines[0, 0], GSIN_ROW, k * QUARTER, QUARTER, k * AFTER_SQUARES)
+            nc.vector.scalar_tensor_tensor(
+                columns(x_woven, k * QUARTER, QUARTER).rearrange("p (c t) -> p c t", t=SLOTS),
+                squares[k][:].rearrange("p (c t) -> p c t", t=SLOTS),
+                -0.5,
+                gains_psum[:, :, TWICE_ROW].unsqueeze(1).to_broadcast([P, QUARTER, SLOTS]),
+                ALU.add,
+                ALU.mult,
+            )
+        h_words[1] = placed("h_words_late", [P, HALF], U32, AT_HALVES)
+        h_plane[1] = placed("h_plane_late", [P, HALF], U8, AT_LATE_PLANE)
         h_quantise(HALF, HALF, late_woven[:])
-        woven = placed("woven", [P, WOVEN], BF16, AT_WOVEN)
-        mcos_rounded = woven[:, 0 : 2 * SLOTS * N]
+        phases(units[3], turn("size", [P, SLOTS * HALF], F32, bufs=2))
+        mcos_rounded = placed("mcos_rounded", [P, 2 * SLOTS * N], BF16, AT_MCOS_ROUNDED)
         mcos_words = held("mcos_words", [P, 2 * N], U32)
         mcos_plane = held("mcos_plane", [P, 2 * N], U8)
         for b in range(2):
@@ -413,46 +372,66 @@ def tile_list_fragment_phase_fields_kernel(
         for c0 in (0, N):
             quantise(mcos_words[:, c0 : c0 + N], mcos_plane[:, c0 : c0 + N], mcos_rounded[:, SLOTS * c0 : SLOTS * (c0 + N)])
 
-        late_words = {
-            ("x", 1): placed("x1_words", [P, QUARTER], U32, AT_V2),
-            ("y", 2): placed("y2_words", [P, HALF], U32, AT_V2 + 4 * QUARTER),
-            ("x", 2): h_words[:, QUARTER : QUARTER + HALF],
-        }
-        waiting = []
-        y_end = 2 * SLOTS * N
-        for g, unit in enumerate(units):
-            width, b = unit[1], unit[2]
-            if g + 1 < len(units):
-                phases(units[g + 1])
-            if g == 0:
-                y_tiles = first_y
-            else:
-                y_tiles = operand("y", woven[:, y_end - LAP : y_end - LAP + SLOTS * width], width, late_words.get(("y", g)))
-                gain(y_tiles, sines[unit][:], GSIN_ROW + b, 0, width, Y_SHARES[g], True)
-                y_end = y_end - LAP + SLOTS * width
-            for args in waiting:
-                mix(*args)
-            waiting = []
-            mix(unit, y_tiles, 0, width, True)
-            if 0 < g < len(units) - 1:
-                x_end = y_end - SLOTS * width + LAP
-                x_woven = woven[:, x_end - SLOTS * width : x_end]
-            else:
-                x_woven = held("x_woven%d" % g, [P, SLOTS * width], BF16)[:]
-            x_tiles = operand("x", x_woven, width, late_words.get(("x", g)))
-            if g == 0:
-                nc.vector.scalar_tensor_tensor(
-                    x_woven.rearrange("p (c t) -> p c t", t=SLOTS),
-                    squares[:].rearrange("p (c t) -> p c t", t=SLOTS),
-                    -0.5,
-                    gains_psum[:, :, TWICE_ROW].unsqueeze(1).to_broadcast([P, width, SLOTS]),
-                    ALU.add,
-                    ALU.mult,
-                )
-                waiting.append((unit, x_tiles, 0, width, False))
-            for c0, step, piece in cosines.get(unit, ()):
-                gain(x_tiles, piece, GCOS_ROW + b, c0, step, X_SHARES[g], False)
-                if step == width:
-                    waiting.append((unit, x_tiles, c0, step, False))
-                else:
-                    mix(unit, x_tiles, c0, step, False)
+        out_rows = out.rearrange("(n p) j -> p n j", p=P)
+        out_banks = {}
+
+        def mix(name, half, b, c0, width, closing):
+            words = held("%s_words%d_%d_%d" % (name, half, b, c0), [P, width], U32)
+            plane = held("%s_plane%d_%d_%d" % (name, half, b, c0), [P, width], U8)
+            quantise(words[:], plane[:], columns(y_woven if name == "y" else x_woven, c0, width))
+            step = CHUNK if half else width
+            for k0 in range(0, width, step):
+                chunk = (half * HALF + c0 + k0) // CHUNK
+                for n in range(N // P):
+                    key, at = (chunk, n * CHUNK) if half else (n, 0)
+                    start = name == "y" and b == 0 and at == 0
+                    stop = chunk in closing and (half == 0 or n == N // P - 1)
+                    if start:
+                        out_banks[key] = bank(OUT_BANKS[half][key % QUADS])
+                    w0 = b * N + n * P
+                    if name == "y":
+                        weights, scales = m4_sb[:, 2 * w0 : 2 * (w0 + P)].bitcast(FP4X4), m4_plane[:, w0 : w0 + P]
+                    else:
+                        weights, scales = mcos_words[:, w0 : w0 + P].bitcast(FP8X4), mcos_plane[:, w0 : w0 + P]
+                    nc.tensor.matmul_mx(
+                        out=out_banks[key][:, at : at + step],
+                        lhsT=weights,
+                        lhsT_scale=scales,
+                        rhs=words[:, k0 : k0 + step].bitcast(FP8X4),
+                        rhs_scale=plane[:, k0 : k0 + step],
+                        start=start,
+                        stop=stop,
+                    )
+                    if stop and half:
+                        result = placed("result%d" % chunk, [P, N // P, CHUNK], F32, AT_WQ1 + 4 * N * (chunk - HALF // CHUNK))
+                        nc.scalar.copy(result[:], out_banks[key][:, 0:N].rearrange("p (n j) -> p n j", j=CHUNK))
+                        nc.sync.dma_start(out_rows[:, :, chunk * CHUNK : (chunk + 1) * CHUNK], result[:])
+
+        mix("y", 0, 0, 0, HALF, ())
+        mix("x", 0, 0, 0, HALF, ())
+        phases(units[4], turn("size", [P, SLOTS * QUARTER], F32, bufs=2))
+        gain(y_woven, sines[0, 1], GSIN_ROW + 1, 0, HALF, WIDE)
+        gain(x_woven, cosines[0, 1], GCOS_ROW + 1, 0, HALF, WIDE)
+        mix("y", 0, 1, 0, HALF, ())
+        mix("x", 0, 1, 0, HALF, (0,))
+        rows = [held("rows%d" % n, [P, HALF], F32) for n in range(N // P)]
+        for n in range(SCALAR_ROWS):
+            nc.scalar.copy(rows[n][:], out_banks[n][:])
+            nc.sync.dma_start(out_rows[:, n, 0:HALF], rows[n][:])
+        phases(units[5], placed("last_size", [P, SLOTS * QUARTER], F32, AT_LAST_SIZE))
+        gain(y_woven, sines[1, 0], GSIN_ROW, 0, HALF, BESIDE_COPIES[0])
+        for n in range(SCALAR_ROWS, N // P):
+            nc.vector.tensor_copy(rows[n][:], out_banks[n][:])
+            nc.sync.dma_start(out_rows[:, n, 0:HALF], rows[n][:])
+        gain(x_woven, cosines[1, 0], GCOS_ROW, 0, HALF, BESIDE_COPIES[1])
+        mix("y", 1, 0, 0, HALF, ())
+        mix("x", 1, 0, 0, HALF, ())
+        gain(y_woven, sines[1, 1], GSIN_ROW + 1, 0, QUARTER, SHORT)
+        gain(x_woven, cosines[1, 1], GCOS_ROW + 1, 0, QUARTER, SHORT)
+        gain(y_woven, sines[1, 1], GSIN_ROW + 1, QUARTER, QUARTER, SHORT)
+        mix("x", 1, 1, 0, QUARTER, ())
+        mix("y", 1, 1, 0, HALF, (4, 5))
+        for c0 in (QUARTER, QUARTER + CHUNK):
+            gain(x_woven, cosines[1, 1], GCOS_ROW + 1, c0, CHUNK, 0)
+        for c0 in (QUARTER, QUARTER + CHUNK):
+            mix("x", 1, 1, c0, CHUNK, (6, 7))

@@ -39,10 +39,8 @@ GAIN_BANK = 1
 OUT_BANKS = ((0, 2, 3), (6, 7, 3, 4))
 SCALAR_ROWS = 1
 
-AFTER_SQUARES = 96
-WIDE = 144
-BESIDE_COPIES = (192, 192)
-SHORT = 64
+Y_SHARES = {2: 48, 3: 128, 4: 64, 5: 48}
+X_SHARES = {3: 192, 4: 64}
 
 OVER = 64
 AT_FIRST = 0
@@ -57,10 +55,16 @@ AT_LAST_SIZE = AT_WQ1 + 2 * HALF
 AT_ROUNDED0 = AT_WQ1 + 4 * SLOTS * H
 AT_ROUNDED1 = AT_ROUNDED0 + 2 * SLOTS * H
 AT_HALVES = AT_ROUNDED1 + 2 * SLOTS * H
-AT_MCOS_ROUNDED = AT_HALVES + 4 * SLOTS * QUARTER - OVER
-AT_SQUARES = AT_MCOS_ROUNDED + 4 * SLOTS * N - OVER
-AT_LATE_PLANE = AT_SQUARES + OVER
+AT_SQUARES = AT_HALVES + 4 * SLOTS * QUARTER
+AT_LATE_PLANE = AT_SQUARES
 AT_SECOND = AT_SQUARES + 4 * SLOTS * QUARTER - OVER
+AT_SINE2 = AT_SECOND + 2 * SLOTS * QUARTER
+AT_SINE4 = AT_SINE2 + 4 * SLOTS * HALF
+AT_LATE = AT_SINE4 + 4 * SLOTS * QUARTER
+AT_X4 = AT_LATE - OVER
+AT_SINE3 = AT_LATE + 2 * SLOTS * N
+AT_RESULTS = AT_SINE3 + 2 * SLOTS * HALF
+SINES_AT = {2: AT_SINE2, 3: AT_SINE3, 4: AT_SINE4}
 
 
 def tile_list_fragment_phase_fields_kernel(
@@ -252,8 +256,9 @@ def tile_list_fragment_phase_fields_kernel(
 
         units = [(0, QUARTER, 0), (QUARTER, QUARTER, 0), (0, HALF, 1)]
         units.extend([(HALF, HALF, 0), (HALF, QUARTER, 1), (HALF + QUARTER, QUARTER, 1)])
-        sines = {(half, b): held("sine%d_%d" % (half, b), [P, SLOTS * HALF], F32) for half in range(2) for b in range(2)}
-        cosines = {key: held("cosine%d_%d" % key, [P, SLOTS * HALF], F32) for key in sines if key != (0, 0)}
+        first_sines = held("first_sines", [P, SLOTS * HALF], F32)
+        sines = [first_sines[:, 0 : SLOTS * QUARTER], first_sines[:, SLOTS * QUARTER : SLOTS * HALF]]
+        cosines = {}
 
         def columns(tile, c0, width):
             return tile[:, SLOTS * c0 : SLOTS * (c0 + width)]
@@ -262,12 +267,17 @@ def tile_list_fragment_phase_fields_kernel(
             j0, width, b = unit
             half, c0 = divmod(j0, HALF)
             halved, last = (half, b) == (0, 0), unit == units[-1]
-            sine = columns(sines[half, b], c0, width)
+            g = units.index(unit)
+            if g in SINES_AT:
+                sines.append(placed("sine%d" % g, [P, SLOTS * width], F32, SINES_AT[g])[:])
+            elif not halved:
+                sines.append(held("sine%d" % g, [P, SLOTS * width], F32)[:])
+            sine = sines[g]
             per_bank = HALF // width
             sums = []
             early = 1 if width == HALF else 0
             for t0 in range(0, SLOTS, per_bank):
-                e_bank = bank(E_BANKS[units.index(unit)][t0 // per_bank])
+                e_bank = bank(E_BANKS[g][t0 // per_bank])
                 for t in range(t0, t0 + per_bank):
                     target = e_bank[:, (t - t0) * width : (t - t0 + 1) * width]
                     sums.append(target.rearrange("p (c i) -> p c i", i=LINE))
@@ -294,8 +304,9 @@ def tile_list_fragment_phase_fields_kernel(
             for t in range(early, SLOTS):
                 nc.scalar.activation(by_line(size[:])[:, :, t, :], sums[t], ACT.Abs, bias=phi_sb[:, b, t : t + 1])
             step = CHUNK if last else width
+            cosines[g] = held("cosine%d" % g, [P, SLOTS * width], F32)
             for k0 in range(0, width, step):
-                piece = columns(cosines[half, b], c0 + k0, step)
+                piece = columns(cosines[g], k0, step)
                 source = columns(size, k0, step)
                 for t0, t1 in ((0, SLOTS - 1), (SLOTS - 1, SLOTS)) if width == HALF else ((0, SLOTS),):
                     nc.scalar.activation(
@@ -316,7 +327,7 @@ def tile_list_fragment_phase_fields_kernel(
         squares = [placed("squares0", [P, SLOTS * QUARTER], F32, AT_SQUARES), held("squares1", [P, SLOTS * QUARTER], F32)]
         for k in range(2):
             square(squares[k], halves[k])
-        late_woven = held("h_woven2", [P, SLOTS * HALF], BF16)
+        late_woven = placed("h_woven2", [P, SLOTS * HALF], BF16, AT_LATE)
         for quarter in (2, 3):
             h_pass(1, quarter)
         for quarter in (2, 3):
@@ -332,64 +343,80 @@ def tile_list_fragment_phase_fields_kernel(
         phases(units[2], turn("size", [P, SLOTS * HALF], F32, bufs=2))
 
         y_woven = held("y_woven", [P, SLOTS * HALF], BF16)
-        x_woven = held("x_woven", [P, SLOTS * HALF], BF16)
 
-        def gain(woven, values, row, c0, width, share):
+        def gain(woven, values, row, width, share):
             mine = width - share
             nc.vector.tensor_tensor(
-                side_by_side(columns(woven, c0, mine), LINE),
-                by_line(columns(values, c0, mine)),
+                side_by_side(columns(woven, 0, mine), LINE),
+                by_line(columns(values, 0, mine)),
                 spread(gains_psum[:, :, row], mine, LINE),
                 ALU.mult,
             )
             if share > 0:
                 nc.gpsimd.tensor_tensor(
-                    columns(woven, c0 + mine, share).rearrange("p (a c i t) -> p a c t i", c=GROUPS, i=LINE, t=SLOTS),
-                    columns(values, c0 + mine, share).rearrange("p (a c t i) -> p a c t i", c=GROUPS, t=SLOTS, i=LINE),
+                    columns(woven, mine, share).rearrange("p (a c i t) -> p a c t i", c=GROUPS, i=LINE, t=SLOTS),
+                    columns(values, mine, share).rearrange("p (a c t i) -> p a c t i", c=GROUPS, t=SLOTS, i=LINE),
                     gains_sbuf[:, row].unsqueeze(1).to_broadcast([P, share // (GROUPS * LINE), GROUPS, SLOTS, LINE]),
                     ALU.mult,
                 )
 
-        for k in range(2):
-            gain(y_woven, sines[0, 0], GSIN_ROW, k * QUARTER, QUARTER, k * AFTER_SQUARES)
+        def gain_y(g):
+            j0, width, b = units[g]
+            woven = columns(y_woven, 0 if g > 1 else j0, width)
+            gain(woven, sines[g], GSIN_ROW + b, width, Y_SHARES.get(g, 0))
+            return woven
+
+        def gain_x(g, woven):
+            gain(woven, cosines[g], GCOS_ROW + units[g][2], units[g][1], X_SHARES.get(g, 0))
+
+        first_x = held("first_x", [P, SLOTS * HALF], BF16)
+
+        def gain_squares(k):
             nc.vector.scalar_tensor_tensor(
-                columns(x_woven, k * QUARTER, QUARTER).rearrange("p (c t) -> p c t", t=SLOTS),
+                columns(first_x, k * QUARTER, QUARTER).rearrange("p (c t) -> p c t", t=SLOTS),
                 squares[k][:].rearrange("p (c t) -> p c t", t=SLOTS),
                 -0.5,
                 gains_psum[:, :, TWICE_ROW].unsqueeze(1).to_broadcast([P, QUARTER, SLOTS]),
                 ALU.add,
                 ALU.mult,
             )
-        h_words[1] = placed("h_words_late", [P, HALF], U32, AT_HALVES)
-        h_plane[1] = placed("h_plane_late", [P, HALF], U8, AT_LATE_PLANE)
-        h_quantise(HALF, HALF, late_woven[:])
-        phases(units[3], turn("size", [P, SLOTS * HALF], F32, bufs=2))
-        mcos_rounded = placed("mcos_rounded", [P, 2 * SLOTS * N], BF16, AT_MCOS_ROUNDED)
+
         mcos_words = held("mcos_words", [P, 2 * N], U32)
         mcos_plane = held("mcos_plane", [P, 2 * N], U8)
-        for b in range(2):
-            nc.vector.tensor_copy(side_by_side(mcos_rounded[:, b * SLOTS * N : (b + 1) * SLOTS * N]), by_slot(mcos_raw[b][:]))
-        for c0 in (0, N):
-            quantise(mcos_words[:, c0 : c0 + N], mcos_plane[:, c0 : c0 + N], mcos_rounded[:, SLOTS * c0 : SLOTS * (c0 + N)])
+
+        def round_mcos(b):
+            rounded = placed("mcos_rounded%d" % b, [P, SLOTS * N], BF16, AT_LATE)
+            source = mcos_raw[b][:].rearrange("p t c -> p c t")
+            nc.gpsimd.tensor_scalar(rounded[:].rearrange("p (c t) -> p c t", t=SLOTS), source, 1.0, 0.0, ALU.mult, ALU.add)
+            return rounded
+
+        def quantise_mcos(b, rounded):
+            quantise(mcos_words[:, b * N : (b + 1) * N], mcos_plane[:, b * N : (b + 1) * N], rounded[:])
 
         out_rows = out.rearrange("(n p) j -> p n j", p=P)
         out_banks = {}
 
-        def mix(name, half, b, c0, width, closing):
-            words = held("%s_words%d_%d_%d" % (name, half, b, c0), [P, width], U32)
-            plane = held("%s_plane%d_%d_%d" % (name, half, b, c0), [P, width], U8)
-            quantise(words[:], plane[:], columns(y_woven if name == "y" else x_woven, c0, width))
+        def codes(name, woven, width, at=None):
+            shape = [P, width]
+            words = held(name + "_words", shape, U32) if at is None else placed(name + "_words", shape, U32, at)
+            plane = held(name + "_plane", shape, U8)
+            quantise(words[:], plane[:], woven)
+            return words, plane
+
+        def mix(operand, sines_pass, j0, width, b):
+            words, plane = operand
+            half = j0 // HALF
             step = CHUNK if half else width
             for k0 in range(0, width, step):
-                chunk = (half * HALF + c0 + k0) // CHUNK
+                chunk = (j0 + k0) // CHUNK
                 for n in range(N // P):
                     key, at = (chunk, n * CHUNK) if half else (n, 0)
-                    start = name == "y" and b == 0 and at == 0
-                    stop = chunk in closing and (half == 0 or n == N // P - 1)
+                    start = sines_pass and b == 0 and at == 0
+                    stop = not sines_pass and b == 1 and (half == 0 or n == N // P - 1)
                     if start:
                         out_banks[key] = bank(OUT_BANKS[half][key % QUADS])
                     w0 = b * N + n * P
-                    if name == "y":
+                    if sines_pass:
                         weights, scales = m4_sb[:, 2 * w0 : 2 * (w0 + P)].bitcast(FP4X4), m4_plane[:, w0 : w0 + P]
                     else:
                         weights, scales = mcos_words[:, w0 : w0 + P].bitcast(FP8X4), mcos_plane[:, w0 : w0 + P]
@@ -407,31 +434,52 @@ def tile_list_fragment_phase_fields_kernel(
                         nc.scalar.copy(result[:], out_banks[key][:, 0:N].rearrange("p (n j) -> p n j", j=CHUNK))
                         nc.sync.dma_start(out_rows[:, :, chunk * CHUNK : (chunk + 1) * CHUNK], result[:])
 
-        mix("y", 0, 0, 0, HALF, ())
-        mix("x", 0, 0, 0, HALF, ())
+        gain_y(0)
+        gain_squares(0)
+        gain_y(1)
+        h_words[1] = placed("h_words_late", [P, HALF], U32, AT_HALVES)
+        h_plane[1] = placed("h_plane_late", [P, HALF], U8, AT_LATE_PLANE)
+        h_quantise(HALF, HALF, late_woven[:])
+        phases(units[3], turn("size", [P, SLOTS * HALF], F32, bufs=2))
+        mix(codes("y01", y_woven[:], HALF, AT_HALVES + 4 * HALF), True, 0, HALF, 0)
+        rounded = round_mcos(0)
+        gain_squares(1)
+        y = gain_y(2)
+        x_codes = codes("x01", first_x[:], HALF)
+        quantise_mcos(0, rounded)
+        mix(x_codes, False, 0, HALF, 0)
         phases(units[4], turn("size", [P, SLOTS * QUARTER], F32, bufs=2))
-        gain(y_woven, sines[0, 1], GSIN_ROW + 1, 0, HALF, WIDE)
-        gain(x_woven, cosines[0, 1], GCOS_ROW + 1, 0, HALF, WIDE)
-        mix("y", 0, 1, 0, HALF, ())
-        mix("x", 0, 1, 0, HALF, (0,))
-        rows = [held("rows%d" % n, [P, HALF], F32) for n in range(N // P)]
+        mix(codes("y2", y, HALF), True, *units[2])
+        rounded = round_mcos(1)
+        x = placed("x2", [P, SLOTS * HALF], BF16, AT_SINE2)
+        gain_x(2, x)
+        y = gain_y(3)
+        x_codes = codes("x2", x[:], HALF)
+        quantise_mcos(1, rounded)
+        mix(x_codes, False, *units[2])
+        y_codes = codes("y3", y, HALF)
         for n in range(SCALAR_ROWS):
-            nc.scalar.copy(rows[n][:], out_banks[n][:])
-            nc.sync.dma_start(out_rows[:, n, 0:HALF], rows[n][:])
-        phases(units[5], placed("last_size", [P, SLOTS * QUARTER], F32, AT_LAST_SIZE))
-        gain(y_woven, sines[1, 0], GSIN_ROW, 0, HALF, BESIDE_COPIES[0])
+            rows = held("rows%d" % n, [P, HALF], F32)
+            nc.scalar.copy(rows[:], out_banks[n][:])
+            nc.sync.dma_start(out_rows[:, n, 0:HALF], rows[:])
+        x = placed("x3", [P, SLOTS * HALF], BF16, AT_LATE)
+        gain_x(3, x)
         for n in range(SCALAR_ROWS, N // P):
-            nc.vector.tensor_copy(rows[n][:], out_banks[n][:])
-            nc.sync.dma_start(out_rows[:, n, 0:HALF], rows[n][:])
-        gain(x_woven, cosines[1, 0], GCOS_ROW, 0, HALF, BESIDE_COPIES[1])
-        mix("y", 1, 0, 0, HALF, ())
-        mix("x", 1, 0, 0, HALF, ())
-        gain(y_woven, sines[1, 1], GSIN_ROW + 1, 0, QUARTER, SHORT)
-        gain(x_woven, cosines[1, 1], GCOS_ROW + 1, 0, QUARTER, SHORT)
-        gain(y_woven, sines[1, 1], GSIN_ROW + 1, QUARTER, QUARTER, SHORT)
-        mix("x", 1, 1, 0, QUARTER, ())
-        mix("y", 1, 1, 0, HALF, (4, 5))
-        for c0 in (QUARTER, QUARTER + CHUNK):
-            gain(x_woven, cosines[1, 1], GCOS_ROW + 1, c0, CHUNK, 0)
-        for c0 in (QUARTER, QUARTER + CHUNK):
-            mix("x", 1, 1, c0, CHUNK, (6, 7))
+            rows = placed("rows%d" % n, [P, HALF], F32, AT_RESULTS + 4 * HALF * (n - SCALAR_ROWS))
+            nc.vector.tensor_copy(rows[:], out_banks[n][:])
+            nc.sync.dma_start(out_rows[:, n, 0:HALF], rows[:])
+        phases(units[5], placed("last_size", [P, SLOTS * QUARTER], F32, AT_LAST_SIZE))
+        mix(y_codes, True, *units[3])
+        y = gain_y(4)
+        mix(codes("x3", x[:], HALF), False, *units[3])
+        mix(codes("y4", y, QUARTER), True, *units[4])
+        x = placed("x4", [P, SLOTS * QUARTER], BF16, AT_X4)
+        gain_x(4, x)
+        y = gain_y(5)
+        mix(codes("x4", x[:], QUARTER), False, *units[4])
+        mix(codes("y5", y, QUARTER), True, *units[5])
+        x = held("x5", [P, SLOTS * QUARTER], BF16)
+        for c0 in (0, CHUNK):
+            gain(columns(x, c0, CHUNK), columns(cosines[5], c0, CHUNK), GCOS_ROW + 1, CHUNK, 0)
+        for c0 in (0, CHUNK):
+            mix(codes("x5_%d" % c0, columns(x, c0, CHUNK), CHUNK), False, units[5][0] + c0, CHUNK, 1)

@@ -314,7 +314,8 @@ def tile_list_fragment_phase_fields_kernel(
                     )
 
         def square(target, halves):
-            nc.gpsimd.tensor_tensor(side_by_side(target[:], LINE), by_line(halves[:]), by_line(halves[:]), ALU.mult)
+            source = halves[:].rearrange("p (c t i) -> p c i t", t=SLOTS, i=LINE)
+            nc.gpsimd.tensor_tensor(target[:].rearrange("p (c i t) -> p c i t", t=SLOTS, i=LINE), source, source, ALU.mult)
 
         halves = [held("halves0", [P, SLOTS * QUARTER], F32), placed("halves1", [P, SLOTS * QUARTER], F32, AT_HALVES)]
         phases(units[0], halves[0])

@@ -25,6 +25,7 @@ QUADS = 4
 HALF = 512
 QUARTER = HALF // 2
 CHUNK = 128
+LAST_CHUNK = S // CHUNK - 1
 LIST_ROWS = 16
 LINE = 4
 RUN = 2
@@ -36,11 +37,12 @@ TWICE_ROW = 32
 
 E_BANKS = ((0, 1), (2, 3), (4, 5, 6, 7), (4, 5, 6, 7), (4, 5), (0, 2))
 GAIN_BANK = 1
-OUT_BANKS = ((0, 2, 3), (6, 7, 3, 4))
+OUT_BANKS = ((0, 2, 3), (6, 7, 3, 4, 5))
 SCALAR_ROWS = 1
 
-Y_SHARES = {2: 48, 3: 128, 4: 64, 5: 48}
+Y_SHARES = {2: 192, 3: 128, 4: 64, 5: 48}
 X_SHARES = {3: 192, 4: 64}
+LAST_STEPS = (CHUNK, CHUNK // 2, CHUNK // 2)
 
 OVER = 64
 AT_FIRST = 0
@@ -55,10 +57,9 @@ AT_LAST_SIZE = AT_WQ1 + 2 * HALF
 AT_ROUNDED0 = AT_WQ1 + 4 * SLOTS * H
 AT_ROUNDED1 = AT_ROUNDED0 + 2 * SLOTS * H
 AT_HALVES = AT_ROUNDED1 + 2 * SLOTS * H
-AT_SQUARES = AT_HALVES + 4 * SLOTS * QUARTER
+AT_SQUARES = AT_TAB
 AT_LATE_PLANE = AT_SQUARES
-AT_SECOND = AT_SQUARES + 4 * SLOTS * QUARTER - OVER
-AT_SINE2 = AT_SECOND + 2 * SLOTS * QUARTER
+AT_SINE2 = AT_HALVES + 4 * SLOTS * QUARTER
 AT_SINE4 = AT_SINE2 + 4 * SLOTS * HALF
 AT_LATE = AT_SINE4 + 4 * SLOTS * QUARTER
 AT_X4 = AT_LATE - OVER
@@ -216,12 +217,12 @@ def tile_list_fragment_phase_fields_kernel(
         prepare_wq(0, placed("wq_rounded0", [P, SLOTS * H], BF16, AT_ROUNDED0))
         gain_rows = wq_raw[0][:, 0, :]
         twice = gain_rows[TWICE_ROW : TWICE_ROW + 1, :]
-        nc.sync.dma_start(twice, gcos[0:PASS].rearrange("(b m) -> b m", b=1))
+        nc.scalar.dma_start(twice, gcos[0:PASS].rearrange("(b m) -> b m", b=1))
         nc.scalar.activation(twice, twice, ACT.Copy, scale=-2.0)
         phi_sb = placed("phi_sb", [P, 2, 2 * SLOTS], F32, AT_ROUNDED0 + OVER)
         nc.sync.dma_start(phi_sb[:, :, 0:SLOTS], phi.rearrange("(b p t) -> p b t", b=2, t=SLOTS))
         for vec, row in ((gsin, GSIN_ROW), (gcos, GCOS_ROW)):
-            nc.sync.dma_start(gain_rows[row : row + 2, :], vec.rearrange("(b m) -> b m", b=2))
+            nc.scalar.dma_start(gain_rows[row : row + 2, :], vec.rearrange("(b m) -> b m", b=2))
         half_phi = held("half_phi", [P, SLOTS], F32)
         nc.scalar.activation(half_phi[:], phi_sb[:, 0, 0:SLOTS], ACT.Copy, scale=0.5)
         mcos_raw = []
@@ -303,9 +304,10 @@ def tile_list_fragment_phase_fields_kernel(
                 return
             for t in range(early, SLOTS):
                 nc.scalar.activation(by_line(size[:])[:, :, t, :], sums[t], ACT.Abs, bias=phi_sb[:, b, t : t + 1])
-            step = CHUNK if last else width
+            steps = LAST_STEPS if last else (width,)
             cosines[g] = held("cosine%d" % g, [P, SLOTS * width], F32)
-            for k0 in range(0, width, step):
+            for k, step in enumerate(steps):
+                k0 = sum(steps[:k])
                 piece = columns(cosines[g], k0, step)
                 source = columns(size, k0, step)
                 for t0, t1 in ((0, SLOTS - 1), (SLOTS - 1, SLOTS)) if width == HALF else ((0, SLOTS),):
@@ -319,16 +321,25 @@ def tile_list_fragment_phase_fields_kernel(
 
         halves = [held("halves0", [P, SLOTS * QUARTER], F32), placed("halves1", [P, SLOTS * QUARTER], F32, AT_HALVES)]
         phases(units[0], halves[0])
-        second_woven = placed("h_woven1", [P, SLOTS * QUARTER], BF16, AT_SECOND)
+        second_woven = held("h_woven1", [P, SLOTS * QUARTER], BF16)
         nc.vector.tensor_copy(side_by_side(second_woven[:], 2 * RUN), by_slot(h_biased[:], 2 * RUN))
         gather_v(1, 2 * QUARTER, QUARTER, placed("v_words1_2", [P, QUARTER], U32, AT_FIRST))
         h_quantise(QUARTER, QUARTER, second_woven[:])
-        gather_v(1, 3 * QUARTER, QUARTER, placed("v_words1_3", [P, QUARTER], U32, AT_FIRST + 4 * QUARTER))
         phases(units[1], halves[1])
+        mcos_words = held("mcos_words", [P, 2 * N], U32)
+        mcos_plane = held("mcos_plane", [P, 2 * N], U8)
+
+        def quantise_mcos(b, rounded):
+            quantise(mcos_words[:, b * N : (b + 1) * N], mcos_plane[:, b * N : (b + 1) * N], rounded[:])
+
+        rounded = held("mcos_rounded0", [P, SLOTS * N], BF16)
+        nc.vector.tensor_copy(side_by_side(rounded[:]), by_slot(mcos_raw[0][:]))
+        gather_v(1, 3 * QUARTER, QUARTER, placed("v_words1_3", [P, QUARTER], U32, AT_FIRST + 4 * QUARTER))
+        quantise_mcos(0, rounded)
         squares = [placed("squares0", [P, SLOTS * QUARTER], F32, AT_SQUARES), held("squares1", [P, SLOTS * QUARTER], F32)]
         for k in range(2):
             square(squares[k], halves[k])
-        late_woven = placed("h_woven2", [P, SLOTS * HALF], BF16, AT_LATE)
+        late_woven = placed("h_woven2", [P, SLOTS * HALF], BF16, AT_MCOS0)
         for quarter in (2, 3):
             h_pass(1, quarter)
         for quarter in (2, 3):
@@ -370,7 +381,7 @@ def tile_list_fragment_phase_fields_kernel(
         def gain_x(g, woven):
             gain(woven, cosines[g], GCOS_ROW + units[g][2], units[g][1], X_SHARES.get(g, 0))
 
-        first_x = held("first_x", [P, SLOTS * HALF], BF16)
+        first_x = placed("first_x", [P, SLOTS * HALF], BF16, AT_SINE3 - 2 * SLOTS * HALF)
 
         def gain_squares(k):
             nc.vector.scalar_tensor_tensor(
@@ -382,17 +393,11 @@ def tile_list_fragment_phase_fields_kernel(
                 ALU.mult,
             )
 
-        mcos_words = held("mcos_words", [P, 2 * N], U32)
-        mcos_plane = held("mcos_plane", [P, 2 * N], U8)
-
         def round_mcos(b):
             rounded = placed("mcos_rounded%d" % b, [P, SLOTS * N], BF16, AT_LATE)
             source = mcos_raw[b][:].rearrange("p t c -> p c t")
             nc.gpsimd.tensor_scalar(rounded[:].rearrange("p (c t) -> p c t", t=SLOTS), source, 1.0, 0.0, ALU.mult, ALU.add)
             return rounded
-
-        def quantise_mcos(b, rounded):
-            quantise(mcos_words[:, b * N : (b + 1) * N], mcos_plane[:, b * N : (b + 1) * N], rounded[:])
 
         out_rows = out.rearrange("(n p) j -> p n j", p=P)
         out_banks = {}
@@ -411,11 +416,13 @@ def tile_list_fragment_phase_fields_kernel(
             for k0 in range(0, width, step):
                 chunk = (j0 + k0) // CHUNK
                 for n in range(N // P):
-                    key, at = (chunk, n * CHUNK) if half else (n, 0)
+                    apart = chunk == LAST_CHUNK and n == N // P - 1
+                    key, at = (chunk + apart, 0 if apart else n * CHUNK) if half else (n, 0)
+                    tiles = 1 if apart else N // P - (chunk == LAST_CHUNK)
                     start = sines_pass and b == 0 and at == 0
-                    stop = not sines_pass and b == 1 and (half == 0 or n == N // P - 1)
+                    stop = not sines_pass and b == 1 and (half == 0 or apart or n == tiles - 1)
                     if start:
-                        out_banks[key] = bank(OUT_BANKS[half][key % QUADS])
+                        out_banks[key] = bank(OUT_BANKS[half][key - half * HALF // CHUNK])
                     w0 = b * N + n * P
                     if sines_pass:
                         weights, scales = m4_sb[:, 2 * w0 : 2 * (w0 + P)].bitcast(FP4X4), m4_plane[:, w0 : w0 + P]
@@ -431,24 +438,26 @@ def tile_list_fragment_phase_fields_kernel(
                         stop=stop,
                     )
                     if stop and half:
-                        result = placed("result%d" % chunk, [P, N // P, CHUNK], F32, AT_WQ1 + 4 * N * (chunk - HALF // CHUNK))
-                        nc.scalar.copy(result[:], out_banks[key][:, 0:N].rearrange("p (n j) -> p n j", j=CHUNK))
-                        nc.sync.dma_start(out_rows[:, :, chunk * CHUNK : (chunk + 1) * CHUNK], result[:])
+                        result = placed("result%d" % key, [P, tiles, CHUNK], F32, AT_WQ1 + 4 * N * (key - HALF // CHUNK))
+                        sums = out_banks[key][:, 0 : tiles * CHUNK].rearrange("p (n j) -> p n j", j=CHUNK)
+                        if apart:
+                            nc.vector.tensor_copy(result[:], sums)
+                        else:
+                            nc.scalar.copy(result[:], sums)
+                        nc.sync.dma_start(out_rows[:, n + 1 - tiles : n + 1, chunk * CHUNK : (chunk + 1) * CHUNK], result[:])
 
         gain_y(0)
         gain_squares(0)
         gain_y(1)
+        y_codes = codes("y01", y_woven[:], HALF, AT_HALVES + 4 * HALF)
         h_words[1] = placed("h_words_late", [P, HALF], U32, AT_HALVES)
         h_plane[1] = placed("h_plane_late", [P, HALF], U8, AT_LATE_PLANE)
         h_quantise(HALF, HALF, late_woven[:])
         phases(units[3], turn("size", [P, SLOTS * HALF], F32, bufs=2))
-        mix(codes("y01", y_woven[:], HALF, AT_HALVES + 4 * HALF), True, 0, HALF, 0)
-        rounded = round_mcos(0)
+        mix(y_codes, True, 0, HALF, 0)
         gain_squares(1)
         y = gain_y(2)
-        x_codes = codes("x01", first_x[:], HALF)
-        quantise_mcos(0, rounded)
-        mix(x_codes, False, 0, HALF, 0)
+        mix(codes("x01", first_x[:], HALF), False, 0, HALF, 0)
         phases(units[4], turn("size", [P, SLOTS * QUARTER], F32, bufs=2))
         mix(codes("y2", y, HALF), True, *units[2])
         rounded = round_mcos(1)
@@ -480,7 +489,8 @@ def tile_list_fragment_phase_fields_kernel(
         mix(codes("x4", x[:], QUARTER), False, *units[4])
         mix(codes("y5", y, QUARTER), True, *units[5])
         x = held("x5", [P, SLOTS * QUARTER], BF16)
-        for c0 in (0, CHUNK):
-            gain(columns(x, c0, CHUNK), columns(cosines[5], c0, CHUNK), GCOS_ROW + 1, CHUNK, 0)
+        for k, step in enumerate(LAST_STEPS):
+            c0 = sum(LAST_STEPS[:k])
+            gain(columns(x, c0, step), columns(cosines[5], c0, step), GCOS_ROW + 1, step, 0)
         for c0 in (0, CHUNK):
             mix(codes("x5_%d" % c0, columns(x, c0, CHUNK), CHUNK), False, units[5][0] + c0, CHUNK, 1)

@@ -35,13 +35,14 @@ SCALAR_QUARTER = 1
 GSIN_ROW, GCOS_ROW, GAIN_ROWS = 0, 2, 4
 TWICE_ROW = 32
 
-E_BANKS = ((0, 1), (2, 3), (4, 5, 6, 7), (4, 5, 6, 7), (4, 5), (0, 2))
-GAIN_BANK = 1
-OUT_BANKS = ((0, 2, 3), (6, 7, 3, 4, 5))
-SCALAR_ROWS = 1
+H_BANKS = ((0, 1), (2, 3), (4, 5), (6, 0))
+E_BANKS = ((0, 1), (2, 3), (4, 5, 6, 1), (4, 5, 6, 1), (4, 5), (4, 5))
+GAIN_BANK = 7
+OUT_BANKS = ((0, 2, 3), (6, 1, 3, 0, 2))
+SCALAR_ROWS = 2
 
 Y_SHARES = {2: 192, 3: 128, 4: 64, 5: 48}
-X_SHARES = {3: 192, 4: 64}
+X_SHARES = {3: 160, 4: 64}
 LAST_STEPS = (CHUNK, CHUNK // 2, CHUNK // 2)
 
 OVER = 64
@@ -57,14 +58,19 @@ AT_LAST_SIZE = AT_WQ1 + 2 * HALF
 AT_ROUNDED0 = AT_WQ1 + 4 * SLOTS * H
 AT_ROUNDED1 = AT_ROUNDED0 + 2 * SLOTS * H
 AT_HALVES = AT_ROUNDED1 + 2 * SLOTS * H
-AT_SQUARES = AT_TAB
+AT_LATE_WORDS = AT_HALVES + HALF
+AT_FIRST_WORDS = AT_LATE_WORDS + 4 * HALF
+AT_SQUARES = AT_FIRST_WORDS + 4 * HALF
+AT_SECOND = AT_SQUARES + 4 * SLOTS * QUARTER - OVER
+AT_LATE_WOVEN = AT_SECOND + OVER
 AT_LATE_PLANE = AT_SQUARES
-AT_SINE2 = AT_HALVES + 4 * SLOTS * QUARTER
+AT_SINE2 = AT_LATE_WOVEN + 2 * SLOTS * HALF
 AT_SINE4 = AT_SINE2 + 4 * SLOTS * HALF
 AT_LATE = AT_SINE4 + 4 * SLOTS * QUARTER
 AT_X4 = AT_LATE - OVER
 AT_SINE3 = AT_LATE + 2 * SLOTS * N
 AT_RESULTS = AT_SINE3 + 2 * SLOTS * HALF
+AT_BIASED = AT_SINE3 + 4 * SLOTS * HALF
 SINES_AT = {2: AT_SINE2, 3: AT_SINE3, 4: AT_SINE4}
 
 
@@ -165,10 +171,10 @@ def tile_list_fragment_phase_fields_kernel(
             for c0 in range(0, width, QUARTER):
                 v_words[a, (j0 + c0) // QUARTER] = words[:, c0 : c0 + QUARTER]
 
-        def h_pass(a, quarter):
-            for u in range(2):
-                if a == 0:
-                    h_banks[quarter, u] = bank(2 * quarter + u)
+        def h_pass(a, quarter, banks=(0, 1), first=0):
+            for u in banks:
+                if a == first:
+                    h_banks[quarter, u] = bank(H_BANKS[quarter][u])
                 if quarter == SCALAR_QUARTER:
                     parts = [(t, quarter * QUARTER, QUARTER) for t in (2 * u, 2 * u + 1)]
                 else:
@@ -180,8 +186,8 @@ def tile_list_fragment_phase_fields_kernel(
                         lhsT_scale=wq_plane[a][:, t * P : (t + 1) * P],
                         rhs=v_words[a, quarter][:, j0 % QUARTER : j0 % QUARTER + width].bitcast(FP8X4),
                         rhs_scale=v_plane[a][:, j0 : j0 + width],
-                        start=(a == 0 and k == 0),
-                        stop=(a == 1 and k == len(parts) - 1),
+                        start=(a == first and k == 0),
+                        stop=(a != first and k == len(parts) - 1),
                     )
 
         def h_weave(quarter, u, part):
@@ -223,6 +229,13 @@ def tile_list_fragment_phase_fields_kernel(
         nc.sync.dma_start(phi_sb[:, :, 0:SLOTS], phi.rearrange("(b p t) -> p b t", b=2, t=SLOTS))
         for vec, row in ((gsin, GSIN_ROW), (gcos, GCOS_ROW)):
             nc.scalar.dma_start(gain_rows[row : row + 2, :], vec.rearrange("(b m) -> b m", b=2))
+        gain_bank = bank(GAIN_BANK)
+        for t in range(SLOTS):
+            nc.tensor.transpose(gain_bank[:, t * P : (t + 1) * P], gain_rows[:, t:PASS:SLOTS], identity[:])
+        gains_psum = gain_bank[:].rearrange("p (t r) -> p t r", t=SLOTS)
+        gains_sbuf = held("gains_sbuf", [P, GAIN_ROWS, GROUPS, SLOTS, LINE], F32)
+        by_row = gains_psum[:, :, 0:GAIN_ROWS].rearrange("p t r -> p r t").unsqueeze(2).unsqueeze(4)
+        nc.scalar.copy(gains_sbuf[:], by_row.to_broadcast([P, GAIN_ROWS, GROUPS, SLOTS, LINE]))
         half_phi = held("half_phi", [P, SLOTS], F32)
         nc.scalar.activation(half_phi[:], phi_sb[:, 0, 0:SLOTS], ACT.Copy, scale=0.5)
         mcos_raw = []
@@ -240,12 +253,13 @@ def tile_list_fragment_phase_fields_kernel(
                 m4_plane[32 * q : 32 * q + 4, :].bitcast(I32).rearrange("p (b c) -> p b c", b=2),
                 m4_scales[:, 4 * q : 4 * q + 4, :].bitcast(I32).rearrange("b r c -> r b c"),
             )
-        for quarter in range(4):
+        for quarter in range(3):
             h_pass(0, quarter)
+        h_pass(0, 3, (0,))
         for quarter in range(2):
             gather_v(1, quarter * QUARTER, QUARTER, held("v_words1_%d" % quarter, [P, QUARTER], U32))
             h_pass(1, quarter)
-        h_biased = held("h_biased", [P, SLOTS, QUARTER], BF16)
+        h_biased = placed("h_biased", [P, SLOTS, QUARTER], BF16, AT_BIASED)
         for t in range(SLOTS):
             source = h_banks[SCALAR_QUARTER, t // 2][:, (t % 2) * QUARTER : (t % 2 + 1) * QUARTER]
             nc.scalar.activation(h_biased[:, t, :], source, ACT.Identity, bias=bq_sb[:, t : t + 1])
@@ -321,40 +335,35 @@ def tile_list_fragment_phase_fields_kernel(
 
         halves = [held("halves0", [P, SLOTS * QUARTER], F32), placed("halves1", [P, SLOTS * QUARTER], F32, AT_HALVES)]
         phases(units[0], halves[0])
-        second_woven = held("h_woven1", [P, SLOTS * QUARTER], BF16)
+        second_woven = placed("h_woven1", [P, SLOTS * QUARTER], BF16, AT_SECOND)
         nc.vector.tensor_copy(side_by_side(second_woven[:], 2 * RUN), by_slot(h_biased[:], 2 * RUN))
         gather_v(1, 2 * QUARTER, QUARTER, placed("v_words1_2", [P, QUARTER], U32, AT_FIRST))
+        gather_v(1, 3 * QUARTER, QUARTER, placed("v_words1_3", [P, QUARTER], U32, AT_FIRST + 4 * QUARTER))
         h_quantise(QUARTER, QUARTER, second_woven[:])
         phases(units[1], halves[1])
         mcos_words = held("mcos_words", [P, 2 * N], U32)
-        mcos_plane = held("mcos_plane", [P, 2 * N], U8)
+        mcos_plane = {}
 
         def quantise_mcos(b, rounded):
-            quantise(mcos_words[:, b * N : (b + 1) * N], mcos_plane[:, b * N : (b + 1) * N], rounded[:])
+            mcos_plane[b] = held("mcos_plane1", [P, N], U8) if b else placed("mcos_plane0", [P, N], U8, AT_HALVES)
+            quantise(mcos_words[:, b * N : (b + 1) * N], mcos_plane[b][:], rounded[:])
 
-        rounded = held("mcos_rounded0", [P, SLOTS * N], BF16)
+        rounded = placed("mcos_rounded0", [P, SLOTS * N], BF16, AT_BIASED)
         nc.vector.tensor_copy(side_by_side(rounded[:]), by_slot(mcos_raw[0][:]))
-        gather_v(1, 3 * QUARTER, QUARTER, placed("v_words1_3", [P, QUARTER], U32, AT_FIRST + 4 * QUARTER))
-        quantise_mcos(0, rounded)
         squares = [placed("squares0", [P, SLOTS * QUARTER], F32, AT_SQUARES), held("squares1", [P, SLOTS * QUARTER], F32)]
         for k in range(2):
             square(squares[k], halves[k])
-        late_woven = placed("h_woven2", [P, SLOTS * HALF], BF16, AT_MCOS0)
-        for quarter in (2, 3):
-            h_pass(1, quarter)
+        late_woven = placed("h_woven2", [P, SLOTS * HALF], BF16, AT_LATE_WOVEN)
+        h_pass(1, 2)
+        h_pass(1, 3, (0,))
+        for a in range(2):
+            h_pass(a, 3, (1,))
         for quarter in (2, 3):
             for u in range(2):
                 h_weave(quarter, u, columns(late_woven, (quarter - 2) * QUARTER + u * CHUNK, CHUNK))
-        gain_bank = bank(GAIN_BANK)
-        for t in range(SLOTS):
-            nc.tensor.transpose(gain_bank[:, t * P : (t + 1) * P], gain_rows[:, t:PASS:SLOTS], identity[:])
-        gains_psum = gain_bank[:].rearrange("p (t r) -> p t r", t=SLOTS)
-        gains_sbuf = held("gains_sbuf", [P, GAIN_ROWS, GROUPS, SLOTS, LINE], F32)
-        by_row = gains_psum[:, :, 0:GAIN_ROWS].rearrange("p t r -> p r t").unsqueeze(2).unsqueeze(4)
-        nc.scalar.copy(gains_sbuf[:], by_row.to_broadcast([P, GAIN_ROWS, GROUPS, SLOTS, LINE]))
         phases(units[2], turn("size", [P, SLOTS * HALF], F32, bufs=2))
 
-        y_woven = held("y_woven", [P, SLOTS * HALF], BF16)
+        first_y = held("first_y", [P, SLOTS * HALF], BF16)
 
         def gain(woven, values, row, width, share):
             mine = width - share
@@ -372,9 +381,11 @@ def tile_list_fragment_phase_fields_kernel(
                     ALU.mult,
                 )
 
+        later_y = []
+
         def gain_y(g):
             j0, width, b = units[g]
-            woven = columns(y_woven, 0 if g > 1 else j0, width)
+            woven = columns(later_y[0], 0, width) if g > 1 else columns(first_y, j0, width)
             gain(woven, sines[g], GSIN_ROW + b, width, Y_SHARES.get(g, 0))
             return woven
 
@@ -427,7 +438,7 @@ def tile_list_fragment_phase_fields_kernel(
                     if sines_pass:
                         weights, scales = m4_sb[:, 2 * w0 : 2 * (w0 + P)].bitcast(FP4X4), m4_plane[:, w0 : w0 + P]
                     else:
-                        weights, scales = mcos_words[:, w0 : w0 + P].bitcast(FP8X4), mcos_plane[:, w0 : w0 + P]
+                        weights, scales = mcos_words[:, w0 : w0 + P].bitcast(FP8X4), mcos_plane[b][:, n * P : (n + 1) * P]
                     nc.tensor.matmul_mx(
                         out=out_banks[key][:, at : at + step],
                         lhsT=weights,
@@ -449,12 +460,13 @@ def tile_list_fragment_phase_fields_kernel(
         gain_y(0)
         gain_squares(0)
         gain_y(1)
-        y_codes = codes("y01", y_woven[:], HALF, AT_HALVES + 4 * HALF)
-        h_words[1] = placed("h_words_late", [P, HALF], U32, AT_HALVES)
+        quantise_mcos(0, rounded)
+        h_words[1] = placed("h_words_late", [P, HALF], U32, AT_LATE_WORDS)
         h_plane[1] = placed("h_plane_late", [P, HALF], U8, AT_LATE_PLANE)
         h_quantise(HALF, HALF, late_woven[:])
         phases(units[3], turn("size", [P, SLOTS * HALF], F32, bufs=2))
-        mix(y_codes, True, 0, HALF, 0)
+        mix(codes("y01", first_y[:], HALF, AT_FIRST_WORDS), True, 0, HALF, 0)
+        later_y.append(placed("later_y", [P, SLOTS * HALF], BF16, AT_LATE_WOVEN))
         gain_squares(1)
         y = gain_y(2)
         mix(codes("x01", first_x[:], HALF), False, 0, HALF, 0)

@@ -41,7 +41,7 @@ GAIN_BANK = 7
 OUT_BANKS = ((0, 2, 3), (6, 1, 3, 0, 2))
 SCALAR_ROWS = 2
 
-Y_SHARES = {2: 192, 3: 128, 4: 64, 5: 48}
+Y_SHARES = {2: 192, 3: 96, 4: 64, 5: 48}
 X_SHARES = {3: 160, 4: 64}
 LAST_STEPS = (CHUNK, CHUNK // 2, CHUNK // 2)
 
@@ -290,6 +290,7 @@ def tile_list_fragment_phase_fields_kernel(
             sine = sines[g]
             per_bank = HALF // width
             sums = []
+            sizes = size[:].rearrange("p (t c i) -> p c t i", t=SLOTS, i=LINE)
             early = 1 if width == HALF else 0
             for t0 in range(0, SLOTS, per_bank):
                 e_bank = bank(E_BANKS[g][t0 // per_bank])
@@ -311,22 +312,22 @@ def tile_list_fragment_phase_fields_kernel(
                     else:
                         nc.scalar.activation(by_line(sine)[:, :, t, :], sums[t], ACT.Sin, bias=phi_sb[:, b, t : t + 1])
                     if t < early:
-                        nc.scalar.activation(by_line(size[:])[:, :, t, :], sums[t], ACT.Abs, bias=phi_sb[:, b, t : t + 1])
+                        nc.scalar.activation(sizes[:, :, t, :], sums[t], ACT.Abs, bias=phi_sb[:, b, t : t + 1])
             if halved:
                 for t in range(SLOTS):
                     nc.scalar.activation(by_line(sine)[:, :, t, :], sums[t], ACT.Sin, bias=phi_sb[:, b, t : t + 1])
                 return
             for t in range(early, SLOTS):
-                nc.scalar.activation(by_line(size[:])[:, :, t, :], sums[t], ACT.Abs, bias=phi_sb[:, b, t : t + 1])
+                nc.scalar.activation(sizes[:, :, t, :], sums[t], ACT.Abs, bias=phi_sb[:, b, t : t + 1])
             steps = LAST_STEPS if last else (width,)
             cosines[g] = held("cosine%d" % g, [P, SLOTS * width], F32)
             for k, step in enumerate(steps):
                 k0 = sum(steps[:k])
                 piece = columns(cosines[g], k0, step)
-                source = columns(size, k0, step)
-                for t0, t1 in ((0, SLOTS - 1), (SLOTS - 1, SLOTS)) if width == HALF else ((0, SLOTS),):
+                source = sizes[:, k0 // LINE : (k0 + step) // LINE]
+                for t0, t1 in ((0, SLOTS - 1), (SLOTS - 1, SLOTS)) if k == 0 else ((0, SLOTS),):
                     nc.scalar.activation(
-                        by_line(piece)[:, :, t0:t1, :], by_line(source)[:, :, t0:t1, :], ACT.Sin, bias=math.pi / 2, scale=-1.0
+                        by_line(piece)[:, :, t0:t1, :], source[:, :, t0:t1, :], ACT.Sin, bias=math.pi / 2, scale=-1.0
                     )
 
         def square(target, halves):
@@ -455,7 +456,8 @@ def tile_list_fragment_phase_fields_kernel(
                             nc.vector.tensor_copy(result[:], sums)
                         else:
                             nc.scalar.copy(result[:], sums)
-                        nc.sync.dma_start(out_rows[:, n + 1 - tiles : n + 1, chunk * CHUNK : (chunk + 1) * CHUNK], result[:])
+                        queue = nc.scalar if key == LAST_CHUNK else nc.sync
+                        queue.dma_start(out_rows[:, n + 1 - tiles : n + 1, chunk * CHUNK : (chunk + 1) * CHUNK], result[:])
 
         gain_y(0)
         gain_squares(0)

@@ -39,10 +39,10 @@ H_BANKS = ((0, 1), (2, 3), (4, 5), (6, 0))
 E_BANKS = ((0, 1), (2, 3), (4, 5, 6, 1), (4, 5, 6, 1), (4, 5), (4, 5))
 GAIN_BANK = 7
 OUT_BANKS = ((0, 2, 3), (6, 1, 3, 0, 2))
-SCALAR_ROWS = 2
+SCALAR_ROWS = 1
 
 Y_SHARES = {2: 192, 3: 96, 4: 64, 5: 48}
-X_SHARES = {3: 160, 4: 64}
+X_SHARES = {3: 192, 4: 64}
 LAST_STEPS = (CHUNK, CHUNK // 2, CHUNK // 2)
 
 OVER = 64

@@ -41,8 +41,8 @@ GAIN_BANK = 7
 OUT_BANKS = ((0, 2, 3), (6, 1, 3, 0, 2))
 SCALAR_ROWS = 1
 
-Y_SHARES = {2: 192, 3: 96, 4: 64, 5: 48}
-X_SHARES = {3: 192, 4: 64}
+Y_SHARES = {2: 208}
+X_SHARES = {2: 112, 3: 272, 4: 128}
 LAST_STEPS = (CHUNK, CHUNK // 2, CHUNK // 2)
 
 OVER = 64
@@ -117,6 +117,9 @@ def tile_list_fragment_phase_fields_kernel(
 
         def by_line(flat):
             return flat.rearrange("p (c t i) -> p c t i", t=SLOTS, i=LINE)
+
+        def by_region(flat):
+            return flat.rearrange("p (t c i) -> p c t i", t=SLOTS, i=LINE)
 
         idx = held("idx", [P, S // 16], U16)
         idx2 = held("idx2", [P, S2 // 16], U16)
@@ -287,10 +290,10 @@ def tile_list_fragment_phase_fields_kernel(
                 sines.append(placed("sine%d" % g, [P, SLOTS * width], F32, SINES_AT[g])[:])
             elif not halved:
                 sines.append(held("sine%d" % g, [P, SLOTS * width], F32)[:])
-            sine = sines[g]
+            sine = by_line(sines[g]) if g in Y_SHARES else by_region(sines[g])
             per_bank = HALF // width
             sums = []
-            sizes = size[:].rearrange("p (t c i) -> p c t i", t=SLOTS, i=LINE)
+            sizes = by_region(size[:])
             early = 1 if width == HALF else 0
             for t0 in range(0, SLOTS, per_bank):
                 e_bank = bank(E_BANKS[g][t0 // per_bank])
@@ -310,12 +313,12 @@ def tile_list_fragment_phase_fields_kernel(
                     if halved:
                         nc.scalar.activation(by_line(size[:])[:, :, t, :], sums[t], ACT.Sin, bias=half_phi[:, t : t + 1], scale=0.5)
                     else:
-                        nc.scalar.activation(by_line(sine)[:, :, t, :], sums[t], ACT.Sin, bias=phi_sb[:, b, t : t + 1])
+                        nc.scalar.activation(sine[:, :, t, :], sums[t], ACT.Sin, bias=phi_sb[:, b, t : t + 1])
                     if t < early:
                         nc.scalar.activation(sizes[:, :, t, :], sums[t], ACT.Abs, bias=phi_sb[:, b, t : t + 1])
             if halved:
                 for t in range(SLOTS):
-                    nc.scalar.activation(by_line(sine)[:, :, t, :], sums[t], ACT.Sin, bias=phi_sb[:, b, t : t + 1])
+                    nc.scalar.activation(sine[:, :, t, :], sums[t], ACT.Sin, bias=phi_sb[:, b, t : t + 1])
                 return
             for t in range(early, SLOTS):
                 nc.scalar.activation(sizes[:, :, t, :], sums[t], ACT.Abs, bias=phi_sb[:, b, t : t + 1])
@@ -366,11 +369,11 @@ def tile_list_fragment_phase_fields_kernel(
 
         first_y = held("first_y", [P, SLOTS * HALF], BF16)
 
-        def gain(woven, values, row, width, share):
+        def gain(woven, values, row, width, share, regions=False):
             mine = width - share
             nc.vector.tensor_tensor(
                 side_by_side(columns(woven, 0, mine), LINE),
-                by_line(columns(values, 0, mine)),
+                by_region(values) if regions else by_line(columns(values, 0, mine)),
                 spread(gains_psum[:, :, row], mine, LINE),
                 ALU.mult,
             )
@@ -387,7 +390,7 @@ def tile_list_fragment_phase_fields_kernel(
         def gain_y(g):
             j0, width, b = units[g]
             woven = columns(later_y[0], 0, width) if g > 1 else columns(first_y, j0, width)
-            gain(woven, sines[g], GSIN_ROW + b, width, Y_SHARES.get(g, 0))
+            gain(woven, sines[g], GSIN_ROW + b, width, Y_SHARES.get(g, 0), g not in Y_SHARES)
             return woven
 
         def gain_x(g, woven):

import math
from contextlib import ExitStack

import concourse.mybir as mybir
from concourse.masks import make_identity

K, H, N, T, S, T2, S2 = 1024, 512, 384, 4096, 1024, 2048, 1024
FLOPS = 2 * (K * H * S + H * S2 * S + 2 * S2 * N * S)

F32 = mybir.dt.float32
BF16 = mybir.dt.bfloat16
I32 = mybir.dt.int32
U32 = mybir.dt.uint32
U16 = mybir.dt.uint16
U8 = mybir.dt.uint8
FP8X4 = mybir.dt.float8_e4m3fn_x4
FP4X4 = mybir.dt.float4_e2m1fn_x4
ACT = mybir.ActivationFunctionType
ALU = mybir.AluOpType

P = 128
SLOTS = 4
PASS = P * SLOTS
QUADS = 4
HALF = 512
QUARTER = HALF // 2
CHUNK = 128
LAST_CHUNK = S // CHUNK - 1
LIST_ROWS = 16
LINE = 4
RUN = 2
GROUPS = 4
V2_FIRST_ROW = 8
SCALAR_QUARTER = 1
GSIN_ROW, GCOS_ROW, GAIN_ROWS = 0, 2, 4
TWICE_ROW = 32

H_BANKS = ((0, 1), (2, 3), (4, 5), (6, 0))
E_BANKS = ((0, 1), (2, 3), (4, 5, 6, 1), (4, 5, 6, 1), (4, 5), (4, 5))
GAIN_BANK = 7
OUT_BANKS = ((0, 2, 3), (6, 1, 3, 0, 2))
SCALAR_ROWS = 1

Y_SHARES = {2: 208}
X_SHARES = {2: 112, 3: 272, 4: 128}
LAST_STEPS = (CHUNK, CHUNK // 2, CHUNK // 2)

OVER = 64
AT_FIRST = 0
AT_TAB = AT_FIRST + 4 * HALF
AT_MCOS0 = AT_TAB + 4 * T
AT_TAB2 = AT_MCOS0 + 4 * SLOTS * N - OVER
AT_MCOS1 = AT_TAB2 + OVER
AT_WQ_PLANES = AT_MCOS1 + 4 * SLOTS * N
AT_ROWS = AT_TAB2 + 4 * T2 - OVER
AT_WQ1 = AT_ROWS + OVER + T // 2
AT_LAST_SIZE = AT_WQ1 + 2 * HALF
AT_ROUNDED0 = AT_WQ1 + 4 * SLOTS * H
AT_ROUNDED1 = AT_ROUNDED0 + 2 * SLOTS * H
AT_HALVES = AT_ROUNDED1 + 2 * SLOTS * H
AT_LATE_WORDS = AT_HALVES + HALF
AT_FIRST_WORDS = AT_LATE_WORDS + 4 * HALF
AT_SQUARES = AT_FIRST_WORDS + 4 * HALF
AT_SECOND = AT_SQUARES + 4 * SLOTS * QUARTER - OVER
AT_LATE_WOVEN = AT_SECOND + OVER
AT_LATE_PLANE = AT_SQUARES
AT_SINE2 = AT_LATE_WOVEN + 2 * SLOTS * HALF
AT_SINE4 = AT_SINE2 + 4 * SLOTS * HALF
AT_LATE = AT_SINE4 + 4 * SLOTS * QUARTER
AT_X4 = AT_LATE - OVER
AT_SINE3 = AT_LATE + 2 * SLOTS * N
AT_RESULTS = AT_SINE3 + 2 * SLOTS * HALF
AT_BIASED = AT_SINE3 + 4 * SLOTS * HALF
SINES_AT = {2: AT_SINE2, 3: AT_SINE3, 4: AT_SINE4}


def tile_list_fragment_phase_fields_kernel(
    tc, tab_words, tab_scales, offs, tab2_words, tab2_scales, offs2, wq, bq, phi, gcos, gsin, mcos, m4_words, m4_scales, out
):
    nc = tc.nc
    with ExitStack() as ctx:
        keep = ctx.enter_context(tc.tile_pool(name="keep", bufs=1))
        arena = ctx.enter_context(tc.tile_pool(name="arena", bufs=1))
        ring = ctx.enter_context(tc.tile_pool(name="ring", bufs=2))
        psum = ctx.enter_context(tc.psum_pool(name="psum", bufs=1))

        def held(name, shape, dtype):
            return keep.tile(shape, dtype, name=name, tag=name, align_bytes=64)

        def placed(name, shape, dtype, at):
            return arena.tile(shape, dtype, name=name, align_bytes=64, offset=at)

        def turn(name, shape, dtype, bufs):
            return ring.tile(shape, dtype, name=name, align_bytes=64, bufs=bufs)

        def bank(index):
            return psum.tile([P, HALF], F32, name="bank%d" % index)

        def load_rows(raw, matrix, a):
            nc.sync.dma_start(raw[:], matrix[a * PASS : (a + 1) * PASS, :].rearrange("(p t) c -> p t c", t=SLOTS))
            return raw

        def load_words(sb, words):
            nc.sync.dma_start(sb[:], words.rearrange("p n t -> p (n t)").bitcast(I32))

        def quantise(words, plane, src):
            nc.vector.quantize_mx(out=words.bitcast(FP8X4), scales=plane, in_=src)

        def side_by_side(dst, run=RUN):
            return dst.rearrange("p (c i t) -> p c t i", i=run, t=SLOTS)

        def by_slot(src, run=RUN):
            return src.rearrange("p t (c i) -> p c t i", i=run)

        def spread(values, width, run=RUN):
            return values.unsqueeze(1).unsqueeze(3).to_broadcast([P, width // run, SLOTS, run])

        def by_line(flat):
            return flat.rearrange("p (c t i) -> p c t i", t=SLOTS, i=LINE)

        def by_region(flat):
            return flat.rearrange("p (t c i) -> p c t i", t=SLOTS, i=LINE)

        idx = held("idx", [P, S // 16], U16)
        idx2 = held("idx2", [P, S2 // 16], U16)
        tab_rows = placed("tab_rows", [P, T], U8, AT_ROWS)
        tab2_plane = held("tab2_plane", [P, T2], U8)
        v_plane = [held("v_plane%d" % a, [P, S], U8) for a in range(2)]
        nc.gpsimd.memset(tab2_plane[:].bitcast(I32), 0)
        nc.vector.memset(tab_rows[64:P, :].bitcast(I32), 0)
        nc.vector.memset(tab_rows[32:64, :].bitcast(I32), 0)
        for a in range(2):
            nc.gpsimd.memset(v_plane[a][:].bitcast(I32), 0)
        identity = held("identity", [P, P], F32)
        make_identity(nc, identity[:])

        nc.sync.dma_start(idx[:], offs)
        nc.scalar.dma_start(tab_rows[0:32, :].bitcast(I32), tab_scales.rearrange("a q t -> (a q) t").bitcast(I32))
        tab_sb = [placed("tab_sb0", [P, T], I32, AT_TAB)]
        load_words(tab_sb[0], tab_words[0])
        wq_raw = [load_rows(held("wq_raw0", [P, SLOTS, H], F32), wq, 0)]
        nc.sync.dma_start(idx2[:], offs2)
        bq_sb = held("bq_sb", [P, SLOTS], F32)
        nc.scalar.dma_start(bq_sb[:], bq.rearrange("(p t) -> p t", t=SLOTS))
        for r in range(4):
            nc.scalar.dma_start(tab2_plane[V2_FIRST_ROW + r : P : 32, :].bitcast(I32), tab2_scales[0, r:16:4, :].bitcast(I32))
        warm = held("warm", [P, 1], F32)
        nc.scalar.activation(warm[:], identity[:, 0:1], ACT.Sin)

        wq_words = []
        wq_plane = []
        v_words = {}
        h_banks = {}
        h_words = {0: held("h_words", [P, HALF], U32)}
        h_plane = {0: held("h_plane", [P, HALF], U8)}
        v2_words = {}

        def place_v_rows(a, queue):
            for r in range(4):
                queue.dma_start(v_plane[a][r:P:32, :].bitcast(I32), v_rows[16 * a + r : 16 * (a + 1) : 4, :].bitcast(I32))

        def prepare_wq(a, rounded):
            target = rounded[:].rearrange("p (t m j) -> p m t j", t=SLOTS, j=SLOTS)
            nc.scalar.copy(target, wq_raw[a][:].rearrange("p j (m t) -> p m t j", t=SLOTS))
            words = held("wq_words%d" % a, [P, H], U32)
            plane = placed("wq_plane%d" % a, [P, H], U8, AT_WQ_PLANES + H * a)
            quantise(words[:], plane[:], rounded[:])
            wq_words.append(words)
            wq_plane.append(plane)

        def gather_v(a, j0, width, words):
            offsets = idx[:, j0 // LIST_ROWS : (j0 + width) // LIST_ROWS]
            nc.vector.tensor_copy(words[:], tab_sb[a][:].bitcast(U32).indirect(offsets))
            for c0 in range(0, width, QUARTER):
                v_words[a, (j0 + c0) // QUARTER] = words[:, c0 : c0 + QUARTER]

        def h_pass(a, quarter, banks=(0, 1), first=0):
            for u in banks:
                if a == first:
                    h_banks[quarter, u] = bank(H_BANKS[quarter][u])
                if quarter == SCALAR_QUARTER:
                    parts = [(t, quarter * QUARTER, QUARTER) for t in (2 * u, 2 * u + 1)]
                else:
                    parts = [(t, quarter * QUARTER + u * CHUNK, CHUNK) for t in range(SLOTS)]
                for k, (t, j0, width) in enumerate(parts):
                    nc.tensor.matmul_mx(
                        out=h_banks[quarter, u][:, k * width : (k + 1) * width],
                        lhsT=wq_words[a][:, t * P : (t + 1) * P].bitcast(FP8X4),
                        lhsT_scale=wq_plane[a][:, t * P : (t + 1) * P],
                        rhs=v_words[a, quarter][:, j0 % QUARTER : j0 % QUARTER + width].bitcast(FP8X4),
                        rhs_scale=v_plane[a][:, j0 : j0 + width],
                        start=(a == first and k == 0),
                        stop=(a != first and k == len(parts) - 1),
                    )

        def h_weave(quarter, u, part):
            source = h_banks[quarter, u][:].rearrange("p (t j) -> p t j", t=SLOTS)
            nc.vector.tensor_tensor(side_by_side(part), by_slot(source), spread(bq_sb[:], CHUNK), ALU.add)

        def h_quantise(j0, width, woven):
            half, c0 = divmod(j0, HALF)
            quantise(h_words[half][:, c0 : c0 + width], h_plane[half][:, c0 : c0 + width], woven)

        def gather_v2(b):
            v2_words[b] = held("v2_words%d" % b, [P, PASS], U32)
            nc.vector.tensor_copy(
                v2_words[b][:].rearrange("p (t q) -> p q t", t=SLOTS),
                tab2_sb[:].bitcast(U32).indirect(idx2[:, b * PASS // LIST_ROWS : (b + 1) * PASS // LIST_ROWS]),
            )

        v_rows = held("v_rows", [P, S], U8)
        nc.vector.tensor_copy(v_rows[:], tab_rows[:].indirect(idx[:]))
        tab2_sb = placed("tab2_sb", [P, T2], I32, AT_TAB2)
        load_words(tab2_sb, tab2_words[0])
        wq_raw.append(load_rows(placed("wq_raw1", [P, SLOTS, H], F32, AT_WQ1), wq, 1))
        place_v_rows(0, nc.scalar)
        for half in range(2):
            gather_v(0, half * HALF, HALF, held("v_words0_%d" % half, [P, HALF], U32))
        tab_sb.append(placed("tab_sb1", [P, T], I32, AT_TAB))
        load_words(tab_sb[1], tab_words[1])
        place_v_rows(1, nc.sync)
        v2_plane = held("v2_plane", [P, S2], U8)
        nc.vector.tensor_copy(v2_plane[:].rearrange("p (b t q) -> p b q t", b=2, t=SLOTS), tab2_plane[:].indirect(idx2[:]))
        for b in range(2):
            gather_v2(b)
        prepare_wq(0, placed("wq_rounded0", [P, SLOTS * H], BF16, AT_ROUNDED0))
        gain_rows = wq_raw[0][:, 0, :]
        twice = gain_rows[TWICE_ROW : TWICE_ROW + 1, :]
        nc.scalar.dma_start(twice, gcos[0:PASS].rearrange("(b m) -> b m", b=1))
        nc.scalar.activation(twice, twice, ACT.Copy, scale=-2.0)
        phi_sb = placed("phi_sb", [P, 2, 2 * SLOTS], F32, AT_ROUNDED0 + OVER)
        nc.sync.dma_start(phi_sb[:, :, 0:SLOTS], phi.rearrange("(b p t) -> p b t", b=2, t=SLOTS))
        for vec, row in ((gsin, GSIN_ROW), (gcos, GCOS_ROW)):
            nc.scalar.dma_start(gain_rows[row : row + 2, :], vec.rearrange("(b m) -> b m", b=2))
        gain_bank = bank(GAIN_BANK)
        for t in range(SLOTS):
            nc.tensor.transpose(gain_bank[:, t * P : (t + 1) * P], gain_rows[:, t:PASS:SLOTS], identity[:])
        gains_psum = gain_bank[:].rearrange("p (t r) -> p t r", t=SLOTS)
        gains_sbuf = held("gains_sbuf", [P, GAIN_ROWS, GROUPS, SLOTS, LINE], F32)
        by_row = gains_psum[:, :, 0:GAIN_ROWS].rearrange("p t r -> p r t").unsqueeze(2).unsqueeze(4)
        nc.scalar.copy(gains_sbuf[:], by_row.to_broadcast([P, GAIN_ROWS, GROUPS, SLOTS, LINE]))
        half_phi = held("half_phi", [P, SLOTS], F32)
        nc.scalar.activation(half_phi[:], phi_sb[:, 0, 0:SLOTS], ACT.Copy, scale=0.5)
        mcos_raw = []
        for b, at in enumerate((AT_MCOS0, AT_MCOS1)):
            mcos_raw.append(load_rows(placed("mcos_raw%d" % b, [P, SLOTS, N], F32, at), mcos, b))
        prepare_wq(1, placed("wq_rounded1", [P, SLOTS * H], BF16, AT_ROUNDED1))
        m4_sb = placed("m4_sb", [P, 2 * 2 * N], U8, AT_ROUNDED1)
        nc.sync.dma_start(
            m4_sb[:].bitcast(I32).rearrange("p (b c) -> p b c", b=2), m4_words.bitcast(I32).rearrange("b p c -> p b c")
        )
        m4_plane = placed("m4_plane", [P, 2 * N], U8, AT_ROUNDED1 + 4 * N)
        nc.gpsimd.memset(m4_plane[:].bitcast(I32), 0)
        for q in range(QUADS):
            nc.sync.dma_start(
                m4_plane[32 * q : 32 * q + 4, :].bitcast(I32).rearrange("p (b c) -> p b c", b=2),
                m4_scales[:, 4 * q : 4 * q + 4, :].bitcast(I32).rearrange("b r c -> r b c"),
            )
        for quarter in range(3):
            h_pass(0, quarter)
        h_pass(0, 3, (0,))
        for quarter in range(2):
            gather_v(1, quarter * QUARTER, QUARTER, held("v_words1_%d" % quarter, [P, QUARTER], U32))
            h_pass(1, quarter)
        h_biased = placed("h_biased", [P, SLOTS, QUARTER], BF16, AT_BIASED)
        for t in range(SLOTS):
            source = h_banks[SCALAR_QUARTER, t // 2][:, (t % 2) * QUARTER : (t % 2 + 1) * QUARTER]
            nc.scalar.activation(h_biased[:, t, :], source, ACT.Identity, bias=bq_sb[:, t : t + 1])
        first_woven = [placed("h_woven0_%d" % u, [P, SLOTS * CHUNK], BF16, AT_FIRST + 2 * SLOTS * CHUNK * u) for u in range(2)]
        for u in range(2):
            h_weave(0, u, first_woven[u][:])
        for u in range(2):
            h_quantise(u * CHUNK, CHUNK, first_woven[u][:])

        units = [(0, QUARTER, 0), (QUARTER, QUARTER, 0), (0, HALF, 1)]
        units.extend([(HALF, HALF, 0), (HALF, QUARTER, 1), (HALF + QUARTER, QUARTER, 1)])
        first_sines = held("first_sines", [P, SLOTS * HALF], F32)
        sines = [first_sines[:, 0 : SLOTS * QUARTER], first_sines[:, SLOTS * QUARTER : SLOTS * HALF]]
        cosines = {}

        def columns(tile, c0, width):
            return tile[:, SLOTS * c0 : SLOTS * (c0 + width)]

        def phases(unit, size):
            j0, width, b = unit
            half, c0 = divmod(j0, HALF)
            halved, last = (half, b) == (0, 0), unit == units[-1]
            g = units.index(unit)
            if g in SINES_AT:
                sines.append(placed("sine%d" % g, [P, SLOTS * width], F32, SINES_AT[g])[:])
            elif not halved:
                sines.append(held("sine%d" % g, [P, SLOTS * width], F32)[:])
            sine = by_line(sines[g]) if g in Y_SHARES else by_region(sines[g])
            per_bank = HALF // width
            sums = []
            sizes = by_region(size[:])
            early = 1 if width == HALF else 0
            for t0 in range(0, SLOTS, per_bank):
                e_bank = bank(E_BANKS[g][t0 // per_bank])
                for t in range(t0, t0 + per_bank):
                    target = e_bank[:, (t - t0) * width : (t - t0 + 1) * width]
                    sums.append(target.rearrange("p (c i) -> p c i", i=LINE))
                    nc.tensor.matmul_mx(
                        out=target,
                        lhsT=v2_words[b][:, t * P : (t + 1) * P].bitcast(FP8X4),
                        lhsT_scale=v2_plane[V2_FIRST_ROW:P, b * PASS + t * P : b * PASS + (t + 1) * P],
                        rhs=h_words[half][:, c0 : c0 + width].bitcast(FP8X4),
                        rhs_scale=h_plane[half][:, c0 : c0 + width],
                        start=True,
                        stop=True,
                    )
                for t in range(t0, t0 + per_bank):
                    if halved:
                        nc.scalar.activation(by_line(size[:])[:, :, t, :], sums[t], ACT.Sin, bias=half_phi[:, t : t + 1], scale=0.5)
                    else:
                        nc.scalar.activation(sine[:, :, t, :], sums[t], ACT.Sin, bias=phi_sb[:, b, t : t + 1])
                    if t < early:
                        nc.scalar.activation(sizes[:, :, t, :], sums[t], ACT.Abs, bias=phi_sb[:, b, t : t + 1])
            if halved:
                for t in range(SLOTS):
                    nc.scalar.activation(sine[:, :, t, :], sums[t], ACT.Sin, bias=phi_sb[:, b, t : t + 1])
                return
            for t in range(early, SLOTS):
                nc.scalar.activation(sizes[:, :, t, :], sums[t], ACT.Abs, bias=phi_sb[:, b, t : t + 1])
            steps = LAST_STEPS if last else (width,)
            cosines[g] = held("cosine%d" % g, [P, SLOTS * width], F32)
            for k, step in enumerate(steps):
                k0 = sum(steps[:k])
                piece = columns(cosines[g], k0, step)
                source = sizes[:, k0 // LINE : (k0 + step) // LINE]
                for t0, t1 in ((0, SLOTS - 1), (SLOTS - 1, SLOTS)) if k == 0 else ((0, SLOTS),):
                    nc.scalar.activation(
                        by_line(piece)[:, :, t0:t1, :], source[:, :, t0:t1, :], ACT.Sin, bias=math.pi / 2, scale=-1.0
                    )

        def square(target, halves):
            source = halves[:].rearrange("p (c t i) -> p c i t", t=SLOTS, i=LINE)
            nc.gpsimd.tensor_tensor(target[:].rearrange("p (c i t) -> p c i t", t=SLOTS, i=LINE), source, source, ALU.mult)

        halves = [held("halves0", [P, SLOTS * QUARTER], F32), placed("halves1", [P, SLOTS * QUARTER], F32, AT_HALVES)]
        phases(units[0], halves[0])
        second_woven = placed("h_woven1", [P, SLOTS * QUARTER], BF16, AT_SECOND)
        nc.vector.tensor_copy(side_by_side(second_woven[:], 2 * RUN), by_slot(h_biased[:], 2 * RUN))
        gather_v(1, 2 * QUARTER, QUARTER, placed("v_words1_2", [P, QUARTER], U32, AT_FIRST))
        gather_v(1, 3 * QUARTER, QUARTER, placed("v_words1_3", [P, QUARTER], U32, AT_FIRST + 4 * QUARTER))
        h_quantise(QUARTER, QUARTER, second_woven[:])
        phases(units[1], halves[1])
        mcos_words = held("mcos_words", [P, 2 * N], U32)
        mcos_plane = {}

        def quantise_mcos(b, rounded):
            mcos_plane[b] = held("mcos_plane1", [P, N], U8) if b else placed("mcos_plane0", [P, N], U8, AT_HALVES)
            quantise(mcos_words[:, b * N : (b + 1) * N], mcos_plane[b][:], rounded[:])

        rounded = placed("mcos_rounded0", [P, SLOTS * N], BF16, AT_BIASED)
        nc.vector.tensor_copy(side_by_side(rounded[:]), by_slot(mcos_raw[0][:]))
        squares = [placed("squares0", [P, SLOTS * QUARTER], F32, AT_SQUARES), held("squares1", [P, SLOTS * QUARTER], F32)]
        for k in range(2):
            square(squares[k], halves[k])
        late_woven = placed("h_woven2", [P, SLOTS * HALF], BF16, AT_LATE_WOVEN)
        h_pass(1, 2)
        h_pass(1, 3, (0,))
        for a in range(2):
            h_pass(a, 3, (1,))
        for quarter in (2, 3):
            for u in range(2):
                h_weave(quarter, u, columns(late_woven, (quarter - 2) * QUARTER + u * CHUNK, CHUNK))
        phases(units[2], turn("size", [P, SLOTS * HALF], F32, bufs=2))

        first_y = held("first_y", [P, SLOTS * HALF], BF16)

        def gain(woven, values, row, width, share, regions=False):
            mine = width - share
            nc.vector.tensor_tensor(
                side_by_side(columns(woven, 0, mine), LINE),
                by_region(values) if regions else by_line(columns(values, 0, mine)),
                spread(gains_psum[:, :, row], mine, LINE),
                ALU.mult,
            )
            if share > 0:
                nc.gpsimd.tensor_tensor(
                    columns(woven, mine, share).rearrange("p (a c i t) -> p a c t i", c=GROUPS, i=LINE, t=SLOTS),
                    columns(values, mine, share).rearrange("p (a c t i) -> p a c t i", c=GROUPS, t=SLOTS, i=LINE),
                    gains_sbuf[:, row].unsqueeze(1).to_broadcast([P, share // (GROUPS * LINE), GROUPS, SLOTS, LINE]),
                    ALU.mult,
                )

        later_y = []

        def gain_y(g):
            j0, width, b = units[g]
            woven = columns(later_y[0], 0, width) if g > 1 else columns(first_y, j0, width)
            gain(woven, sines[g], GSIN_ROW + b, width, Y_SHARES.get(g, 0), g not in Y_SHARES)
            return woven

        def gain_x(g, woven):
            gain(woven, cosines[g], GCOS_ROW + units[g][2], units[g][1], X_SHARES.get(g, 0))

        first_x = placed("first_x", [P, SLOTS * HALF], BF16, AT_SINE3 - 2 * SLOTS * HALF)

        def gain_squares(k):
            nc.vector.scalar_tensor_tensor(
                columns(first_x, k * QUARTER, QUARTER).rearrange("p (c t) -> p c t", t=SLOTS),
                squares[k][:].rearrange("p (c t) -> p c t", t=SLOTS),
                -0.5,
                gains_psum[:, :, TWICE_ROW].unsqueeze(1).to_broadcast([P, QUARTER, SLOTS]),
                ALU.add,
                ALU.mult,
            )

        def round_mcos(b):
            rounded = placed("mcos_rounded%d" % b, [P, SLOTS * N], BF16, AT_LATE)
            source = mcos_raw[b][:].rearrange("p t c -> p c t")
            nc.gpsimd.tensor_scalar(rounded[:].rearrange("p (c t) -> p c t", t=SLOTS), source, 1.0, 0.0, ALU.mult, ALU.add)
            return rounded

        out_rows = out.rearrange("(n p) j -> p n j", p=P)
        out_banks = {}

        def codes(name, woven, width, at=None):
            shape = [P, width]
            words = held(name + "_words", shape, U32) if at is None else placed(name + "_words", shape, U32, at)
            plane = held(name + "_plane", shape, U8)
            quantise(words[:], plane[:], woven)
            return words, plane

        def mix(operand, sines_pass, j0, width, b):
            words, plane = operand
            half = j0 // HALF
            step = CHUNK if half else width
            for k0 in range(0, width, step):
                chunk = (j0 + k0) // CHUNK
                for n in range(N // P):
                    apart = chunk == LAST_CHUNK and n == N // P - 1
                    key, at = (chunk + apart, 0 if apart else n * CHUNK) if half else (n, 0)
                    tiles = 1 if apart else N // P - (chunk == LAST_CHUNK)
                    start = sines_pass and b == 0 and at == 0
                    stop = not sines_pass and b == 1 and (half == 0 or apart or n == tiles - 1)
                    if start:
                        out_banks[key] = bank(OUT_BANKS[half][key - half * HALF // CHUNK])
                    w0 = b * N + n * P
                    if sines_pass:
                        weights, scales = m4_sb[:, 2 * w0 : 2 * (w0 + P)].bitcast(FP4X4), m4_plane[:, w0 : w0 + P]
                    else:
                        weights, scales = mcos_words[:, w0 : w0 + P].bitcast(FP8X4), mcos_plane[b][:, n * P : (n + 1) * P]
                    nc.tensor.matmul_mx(
                        out=out_banks[key][:, at : at + step],
                        lhsT=weights,
                        lhsT_scale=scales,
                        rhs=words[:, k0 : k0 + step].bitcast(FP8X4),
                        rhs_scale=plane[:, k0 : k0 + step],
                        start=start,
                        stop=stop,
                    )
                    if stop and half:
                        result = placed("result%d" % key, [P, tiles, CHUNK], F32, AT_WQ1 + 4 * N * (key - HALF // CHUNK))
                        sums = out_banks[key][:, 0 : tiles * CHUNK].rearrange("p (n j) -> p n j", j=CHUNK)
                        if apart:
                            nc.vector.tensor_copy(result[:], sums)
                        else:
                            nc.scalar.copy(result[:], sums)
                        queue = nc.scalar if key == LAST_CHUNK else nc.sync
                        queue.dma_start(out_rows[:, n + 1 - tiles : n + 1, chunk * CHUNK : (chunk + 1) * CHUNK], result[:])

        gain_y(0)
        gain_squares(0)
        gain_y(1)
        quantise_mcos(0, rounded)
        h_words[1] = placed("h_words_late", [P, HALF], U32, AT_LATE_WORDS)
        h_plane[1] = placed("h_plane_late", [P, HALF], U8, AT_LATE_PLANE)
        h_quantise(HALF, HALF, late_woven[:])
        phases(units[3], turn("size", [P, SLOTS * HALF], F32, bufs=2))
        mix(codes("y01", first_y[:], HALF, AT_FIRST_WORDS), True, 0, HALF, 0)
        later_y.append(placed("later_y", [P, SLOTS * HALF], BF16, AT_LATE_WOVEN))
        gain_squares(1)
        y = gain_y(2)
        mix(codes("x01", first_x[:], HALF), False, 0, HALF, 0)
        phases(units[4], turn("size", [P, SLOTS * QUARTER], F32, bufs=2))
        mix(codes("y2", y, HALF), True, *units[2])
        rounded = round_mcos(1)
        x = placed("x2", [P, SLOTS * HALF], BF16, AT_SINE2)
        gain_x(2, x)
        y = gain_y(3)
        x_codes = codes("x2", x[:], HALF)
        quantise_mcos(1, rounded)
        mix(x_codes, False, *units[2])
        y_codes = codes("y3", y, HALF)
        for n in range(SCALAR_ROWS):
            rows = held("rows%d" % n, [P, HALF], F32)
            nc.scalar.copy(rows[:], out_banks[n][:])
            nc.sync.dma_start(out_rows[:, n, 0:HALF], rows[:])
        x = placed("x3", [P, SLOTS * HALF], BF16, AT_LATE)
        gain_x(3, x)
        for n in range(SCALAR_ROWS, N // P):
            rows = placed("rows%d" % n, [P, HALF], F32, AT_RESULTS + 4 * HALF * (n - SCALAR_ROWS))
            nc.vector.tensor_copy(rows[:], out_banks[n][:])
            nc.sync.dma_start(out_rows[:, n, 0:HALF], rows[:])
        phases(units[5], placed("last_size", [P, SLOTS * QUARTER], F32, AT_LAST_SIZE))
        mix(y_codes, True, *units[3])
        y = gain_y(4)
        mix(codes("x3", x[:], HALF), False, *units[3])
        mix(codes("y4", y, QUARTER), True, *units[4])
        x = placed("x4", [P, SLOTS * QUARTER], BF16, AT_X4)
        gain_x(4, x)
        y = gain_y(5)
        mix(codes("x4", x[:], QUARTER), False, *units[4])
        mix(codes("y5", y, QUARTER), True, *units[5])
        x = held("x5", [P, SLOTS * QUARTER], BF16)
        for k, step in enumerate(LAST_STEPS):
            c0 = sum(LAST_STEPS[:k])
            gain(columns(x, c0, step), columns(cosines[5], c0, step), GCOS_ROW + 1, step, 0)
        for c0 in (0, CHUNK):
            mix(codes("x5_%d" % c0, columns(x, c0, CHUNK), CHUNK), False, units[5][0] + c0, CHUNK, 1)
